import numpy as np
import ml_dtypes


def mxq(x, axis, fmt="e4m3"):
    dtype, down = {"e4m3": (ml_dtypes.float8_e4m3fn, 7), "e5m2": (ml_dtypes.float8_e5m2, 14)}[fmt]
    v = np.moveaxis(np.asarray(x, np.float32).astype(ml_dtypes.bfloat16).astype(np.float64), axis, -1)
    blocks = v.reshape(v.shape[:-1] + (-1, 32))
    amax = np.abs(blocks).max(-1, keepdims=True)
    byte = np.maximum(np.where(amax > 0, np.frexp(amax)[1] - 1 + 127, 0) - down, 1)
    scale = np.exp2(byte - 127.0)
    codes = (blocks / scale).astype(np.float32).astype(dtype).astype(np.float64)
    return np.moveaxis((codes * scale).reshape(v.shape), -1, axis)


WIDE = False


def mx_kscale(k):
    if not WIDE:
        return np.ones(k)
    levels = np.array([18, -18])
    if k % 512:
        return np.exp2(np.random.permutation(np.resize(levels, k // 32))).repeat(32)
    a = np.empty((k // 512, 16))
    for p in range(k // 512):
        a[p, :8] = np.random.permutation(np.resize(levels, 8))
        for g in range(8):
            far = levels[np.abs(levels - a[p, g]) >= 10]
            a[p, g + 8] = far[np.random.randint(len(far))]
    return np.exp2(a.ravel()).repeat(32)


def f64(x):
    return np.asarray(x).astype(np.float64)


def striped(idx):
    return np.tile(np.asarray(idx).reshape(-1, 16).T, (8, 1)).astype(np.uint16)


def unstriped(offs):
    return offs[:16].T.reshape(-1).astype(np.int64)

def planes(y):
    n, m = y.shape
    v = y.astype(np.float32).astype(ml_dtypes.bfloat16).astype(np.float64).reshape(n // 32, 32, m)
    top = np.abs(v).max(1)
    byte = np.clip(np.where(top > 0, np.frexp(top)[1] - 1 + 127 - 7, 1), 1, 254)
    codes = (v * np.exp2(127.0 - byte)[:, None, :]).reshape(n, m).astype(np.float32).astype(ml_dtypes.float8_e4m3fn).view(np.uint8)
    words = codes.reshape(n // 512, 128, 4, m).transpose(0, 1, 3, 2)
    return np.ascontiguousarray(words), np.ascontiguousarray(byte.astype(np.uint8).reshape(n // 512, 16, m))


def setup_inputs():
    n = np.random.standard_normal
    uni = np.random.uniform
    idx = np.random.permutation(2048)[:512]
    f_d = mx_kscale(512)
    f_e = mx_kscale(512)
    return {
        "xT": (n((512, 2048)) * f_d[:, None]).astype(np.float32),
        "W": (0.5 * n((512, 512)) / np.sqrt(512) / f_d[:, None] * f_e[None, :]).astype(np.float32),
        "dg": (n((512, 512))).astype(np.float32),
        "lb": np.tile(n(512), (128, 1)).astype(np.float32),
        "ce": np.tile(uni(0.75, 1.3, 512) / f_e, (128, 1)).astype(np.float32),
        "tx": np.tile(uni(0.75, 1.3, 2048), (128, 1)).astype(np.float32),
        "offs": striped(idx),
    }


def reference(xT, W, dg, lb, ce, tx, offs):
    idx = unstriped(offs)
    xT_i = f64(xT)[:, idx]
    tx_i = f64(tx)[:1][:, idx]
    tc = tx_i.T
    a = mxq(xT_i, 0, "e4m3").T @ mxq(f64(W), 0, "e4m3")
    z = tc * f64(ce)[:1] * a
    m = (z).max(-1, keepdims=True)
    q = np.exp(z - m)
    tot = (q).sum(-1, keepdims=True)
    p = q / tot
    h = f64(dg) + f64(lb)[:1]
    s = (p * h).sum(-1, keepdims=True)
    g = tc * f64(ce)[:1] * p * (h - s)
    dx = mxq(f64(W), 1, "e4m3") @ mxq(g, 1, "e5m2").T
    out_0 = np.zeros((512, 2048))
    out_0[:, idx] = dx
    return (out_0,) + planes(out_0)

@@ -1,0 +1,256 @@
+from contextlib import ExitStack
+
+import concourse.mybir as mybir
+from concourse.masks import make_identity
+
+F32 = mybir.dt.float32
+BF16 = mybir.dt.bfloat16
+I32 = mybir.dt.int32
+U32 = mybir.dt.uint32
+U16 = mybir.dt.uint16
+U8 = mybir.dt.uint8
+E4M3X4 = mybir.dt.float8_e4m3fn_x4
+E5M2X4 = mybir.dt.float8_e5m2_x4
+ALU = mybir.AluOpType
+ACT = mybir.ActivationFunctionType
+
+P = 128
+LANES = 4
+D = 512
+E = 512
+SLOTS = 512
+TOKENS = 2048
+HALF = SLOTS // 2
+SLOT_TILES = SLOTS // P
+EARLY = 2
+CHUNK = 512
+CHUNKS = TOKENS // CHUNK
+
+FLOPS = 2 * 2 * D * E * SLOTS
+BYTES = 4 * (D * TOKENS + D * E + SLOTS * E + 2 * E + TOKENS) + 2 * SLOTS * 8 + 4 * D * TOKENS + D * TOKENS + 16 * TOKENS
+
+
+def tile_attend_grouter_x_pl_kernel(tc, xT, W, dg, lb, ce, tx, offs, out_0, out_1, out_2):
+    nc = tc.nc
+    with ExitStack() as ctx:
+        keep = ctx.enter_context(tc.tile_pool(name="keep", bufs=1))
+        psum = ctx.enter_context(tc.psum_pool(name="psum", bufs=1))
+
+        def sb(name, shape, dtype):
+            return keep.tile(shape, dtype, name=name, align_bytes=64)
+
+        banks = [psum.tile([P, 512], F32, name="bank%d" % b) for b in range(8)]
+
+        offsets = sb("offsets", [P, SLOTS // 16], U16)
+        nc.sync.dma_start(offsets[:], offs)
+        half_offsets = [offsets[:, 0:16], offsets[:, 16:32]]
+
+        ce_row = sb("ce_row", [P, E], F32)
+        tx_window = sb("tx_window", [P, TOKENS], F32)
+        g_codes = sb("g_codes", [P, HALF + SLOTS], U32)
+        g_scales = sb("g_scales", [P, HALF + SLOTS], U8)
+        planes = [sb("plane%d" % t, [P, TOKENS], F32) for t in range(LANES)]
+        ident = sb("ident", [P, P], F32)
+        tok = sb("tok", [P, SLOT_TILES, 2], F32)
+        warm = sb("warm", [P, 1], F32)
+        make_identity(nc, ident[:])
+        nc.gpsimd.memset(tok[:], -1.0)
+        nc.scalar.activation(warm[:], ident[:, 0:1], ACT.Exp)
+        nc.vector.memset(ce_row[:], 0.0)
+        nc.vector.memset(tx_window[:].bitcast(I32), 0)
+
+        w_raw = sb("w_raw", [P, LANES, E], F32)
+        nc.sync.dma_start(w_raw[:], W.rearrange("(p j) e -> p j e", j=LANES))
+        nc.sync.dma_start(
+            ce_row[0:1, :].rearrange("o (t b r) -> o t b r", t=LANES, r=8),
+            ce[0:1, :].rearrange("o (b t r) -> o t b r", t=LANES, r=8))
+        nc.sync.dma_start(tx_window[0:1, :], tx[0:1, :])
+        x_rows = xT.rearrange("(p j) n -> j p n", j=LANES)
+        x_raw = [sb("x_raw%d" % j, [P, TOKENS], F32) for j in range(LANES)]
+        for j in range(LANES):
+            nc.sync.dma_start(x_raw[j][:], x_rows[j])
+        lb_rows = sb("lb_rows", [P, E], F32)
+        nc.sync.dma_start(lb_rows[:], lb)
+        dg_raw = [sb("dg_raw%d" % h, [P, 2, E], F32) for h in range(2)]
+        for h in range(2):
+            nc.sync.dma_start(dg_raw[h][:], dg[h * HALF:(h + 1) * HALF, :].rearrange("(j p) e -> p j e", p=P))
+
+        nc.vector.memset(g_codes[:, 0:HALF], 0)
+        nc.vector.memset(g_scales[:, 0:HALF], 0)
+        for t in range(LANES):
+            nc.vector.memset(planes[t][:].bitcast(I32), 0)
+
+        w_bf = sb("w_bf", [P, E, LANES], BF16)
+        nc.scalar.copy(
+            w_bf[:].rearrange("p (t b r) j -> p t b r j", t=LANES, r=8),
+            w_raw[:].rearrange("p j (b t r) -> p t b r j", t=LANES, r=8))
+        w1_codes = sb("w1_codes", [P, E], U32)
+        w1_scales = sb("w1_scales", [P, E], U8)
+        nc.vector.quantize_mx(out=w1_codes[:].bitcast(E4M3X4), scales=w1_scales[:],
+                              in_=w_bf[:].rearrange("p e j -> p (e j)"))
+        w_words = w_bf[:].rearrange("p e j -> p (e j)").bitcast(F32)
+        wt_bf = sb("wt_bf", [P, D, LANES], BF16)
+        for u in range(2):
+            for t in range(LANES):
+                nc.tensor.transpose(banks[6 + u][:, t * P:(t + 1) * P],
+                                    w_words[:, 2 * P * t + u:2 * P * (t + 1):2], ident[:])
+            nc.scalar.copy(
+                wt_bf[:, 2 * P * u:2 * P * (u + 1), :].rearrange("p (c m) t -> p c m t", c=2),
+                banks[6 + u][:].bitcast(BF16).rearrange("p (t m c) -> p c m t", t=LANES, c=2))
+        w2_codes = sb("w2_codes", [P, D], U32)
+        w2_scales = sb("w2_scales", [P, D], U8)
+        nc.vector.quantize_mx(out=w2_codes[:].bitcast(E4M3X4), scales=w2_scales[:],
+                              in_=wt_bf[:].rearrange("p d t -> p (d t)"))
+
+        for t in range(LANES):
+            nc.tensor.transpose(banks[2][:, t * P:(t + 1) * P], ce_row[:, t * P:(t + 1) * P], ident[:])
+        ce_col = sb("ce_col", [P, LANES], F32)
+        neg_ce = sb("neg_ce", [P, 1, LANES], F32)
+        nc.scalar.copy(ce_col[:], banks[2][:, 0:512:P])
+        nc.scalar.activation(neg_ce[:, 0, :], banks[2][:, 0:512:P], ACT.Copy, scale=-1.0)
+        tx_listed = sb("tx_listed", [P, SLOTS], F32)
+        nc.vector.tensor_copy(tx_listed[:], tx_window[:].indirect(offsets[:]))
+        for j in range(SLOT_TILES):
+            nc.tensor.transpose(banks[3][:, j * P:(j + 1) * P], tx_listed[:, j * P:(j + 1) * P], ident[:])
+        nc.scalar.activation(tok[:, :, 0], banks[3][:, 0:512:P], ACT.Copy, scale=-1.0)
+
+        x_bf = sb("x_bf", [P, SLOTS, LANES], BF16)
+        x_codes = sb("x_codes", [P, SLOTS], U32)
+        x_scales = sb("x_scales", [P, SLOTS], U8)
+        for j in range(LANES - 1):
+            nc.vector.tensor_copy(x_bf[:, :, j], x_raw[j][:].indirect(offsets[:]))
+        u_t = [sb("u_t%d" % h, [P, LANES, HALF], F32) for h in range(2)]
+        for h in range(2):
+            cols = slice(h * HALF, (h + 1) * HALF)
+            nc.vector.tensor_copy(x_bf[:, cols, LANES - 1], x_raw[LANES - 1][:].indirect(half_offsets[h]))
+            nc.vector.quantize_mx(out=x_codes[:, cols].bitcast(E4M3X4), scales=x_scales[:, cols],
+                                  in_=x_bf[:, cols, :].rearrange("p i j -> p (i j)"))
+            for t in range(LANES):
+                acc = banks[2 * h + t // 2][:, (t % 2) * HALF:(t % 2 + 1) * HALF]
+                nc.tensor.matmul_mx(out=acc, lhsT=w1_codes[:, t * P:(t + 1) * P].bitcast(E4M3X4),
+                                    lhsT_scale=w1_scales[:, t * P:(t + 1) * P],
+                                    rhs=x_codes[:, cols].bitcast(E4M3X4), rhs_scale=x_scales[:, cols],
+                                    start=True, stop=True)
+            for t in range(LANES):
+                acc = banks[2 * h + t // 2][:, (t % 2) * HALF:(t % 2 + 1) * HALF]
+                nc.scalar.activation(u_t[h][:, t, :], acc, ACT.Copy, scale=ce_col[:, t:t + 1])
+
+        hs = [sb("h%d" % j, [P, E], F32) for j in range(SLOT_TILES)]
+        for j in range(SLOT_TILES):
+            nc.vector.tensor_tensor(
+                hs[j][:].rearrange("p (t b r) -> p t b r", t=LANES, r=8),
+                dg_raw[j // 2][:, j % 2, :].rearrange("p (b t r) -> p t b r", t=LANES, r=8),
+                lb_rows[:].rearrange("p (b t r) -> p t b r", t=LANES, r=8), ALU.add)
+
+        dx = [sb("dx%d" % t, [P, SLOTS], F32) for t in range(LANES)]
+        g_bf = [sb("g_bf%d" % h, [P, HALF, LANES], BF16) for h in range(2)]
+
+        def second_product(t, bank, first):
+            cols = slice(first, first + SLOTS)
+            nc.tensor.matmul_mx(out=bank[:], lhsT=w2_codes[:, t * P:(t + 1) * P].bitcast(E4M3X4),
+                                lhsT_scale=w2_scales[:, t * P:(t + 1) * P],
+                                rhs=g_codes[:, cols].bitcast(E5M2X4), rhs_scale=g_scales[:, cols],
+                                start=True, stop=True)
+
+        q, neg_z, neg_m, tot, rec, fac, ph, acc_s, kk, t2 = [[] for n in range(10)]
+        for j in range(SLOT_TILES):
+            q.append(sb("q%d" % j, [P, E], F32))
+            neg_z.append(sb("neg_z%d" % j, [P, E], F32))
+            ph.append(sb("ph%d" % j, [P, E], F32))
+            t2.append(sb("t2%d" % j, [P, E], F32))
+            neg_m.append(sb("neg_m%d" % j, [P, 1], F32))
+            tot.append(sb("tot%d" % j, [P, 1], F32))
+            rec.append(sb("rec%d" % j, [P, 1], F32))
+            fac.append(sb("fac%d" % j, [P, 2], F32))
+            acc_s.append(sb("acc_s%d" % j, [P, 1], F32))
+            kk.append(sb("kk%d" % j, [P, 1], F32))
+
+        def scores(j):
+            bank = banks[4 + j % 2]
+            for t in range(LANES):
+                nc.tensor.transpose(bank[:, t * P:(t + 1) * P],
+                                    u_t[j // 2][:, t, (j % 2) * P:(j % 2 + 1) * P], ident[:])
+            nc.vector.tensor_scalar(neg_z[j][:], bank[:], tok[:, j, 0:1], None, ALU.mult, ALU.min,
+                                    accum_out=neg_m[j][:])
+            nc.scalar.activation(q[j][:], neg_z[j][:], ACT.Exp, bias=neg_m[j][:], scale=-1.0,
+                                 accum_out=tot[j][:])
+
+        def weights(j):
+            nc.vector.reciprocal(rec[j][:], tot[j][:])
+            nc.vector.tensor_scalar(fac[j][:], tok[:, j, :], rec[j][:], None, ALU.mult)
+            nc.vector.scalar_tensor_tensor(ph[j][:], q[j][:], fac[j][:, 0:1], hs[j][:], ALU.mult, ALU.mult,
+                                           accum_out=acc_s[j][:])
+            nc.scalar.activation(kk[j][:], acc_s[j][:], ACT.Copy, scale=fac[j][:, 1:2])
+            nc.scalar.activation(t2[j][:], q[j][:], ACT.Copy, scale=kk[j][:])
+
+        def turn(j):
+            bank = banks[j]
+            for t in range(LANES):
+                cols = slice(t * P, (t + 1) * P)
+                nc.tensor.matmul(bank[:, cols], ph[j][:, cols], ident[:], start=(t == 0), stop=False, is_transpose=True)
+            for t in range(LANES):
+                cols = slice(t * P, (t + 1) * P)
+                nc.tensor.matmul(bank[:, cols], t2[j][:, cols], ident[:], start=False, stop=(t == LANES - 1), is_transpose=True)
+            nc.vector.tensor_tensor(g_bf[j // 2][:, (j % 2) * P:(j % 2 + 1) * P, :],
+                                    bank[:].rearrange("p (t i) -> p i t", t=LANES),
+                                    neg_ce[:].to_broadcast([P, P, LANES]), ALU.mult)
+
+        def quantise_g(h):
+            cols = slice((h + 1) * HALF, (h + 2) * HALF)
+            nc.vector.quantize_mx(out=g_codes[:, cols].bitcast(E5M2X4), scales=g_scales[:, cols],
+                                  in_=g_bf[h][:].rearrange("p i t -> p (i t)"))
+
+        scores(0)
+        scores(1)
+        weights(0)
+        scores(2)
+        weights(1)
+        turn(0)
+        scores(3)
+        weights(2)
+        turn(1)
+        weights(3)
+        turn(2)
+        turn(3)
+        quantise_g(0)
+        for t in range(EARLY):
+            second_product(t, banks[2], 0)
+            nc.scalar.copy(dx[t][:, 0:HALF], banks[2][:, HALF:SLOTS])
+        quantise_g(1)
+        for t in range(EARLY):
+            nc.vector.tensor_copy(planes[t][:].indirect(half_offsets[0]), dx[t][:, 0:HALF])
+        for t in range(LANES):
+            second_product(t, banks[4 + t], HALF)
+            first = HALF if t < EARLY else 0
+            nc.scalar.copy(dx[t][:, first:SLOTS], banks[4 + t][:, first:SLOTS])
+
+        out_rows = out_0.rearrange("(p j) n -> j p n", j=LANES)
+        pairs = [sb("pairs%d" % c, [P, 2, CHUNK, 2], BF16) for c in range(CHUNKS)]
+        y_scales = sb("y_scales", [P, TOKENS], U8)
+        words_out = out_1[0].rearrange("p n l -> p (n l)").bitcast(I32)
+        for t in range(LANES):
+            if t < EARLY:
+                nc.vector.tensor_copy(planes[t][:].indirect(half_offsets[1]), dx[t][:, HALF:SLOTS])
+            else:
+                nc.vector.tensor_copy(planes[t][:].indirect(offsets[:]), dx[t][:])
+            nc.sync.dma_start(out_rows[t], planes[t][:])
+            for c in range(CHUNKS if t < 2 else CHUNKS - 1):
+                nc.scalar.copy(pairs[c][:, t // 2, :, t % 2], planes[t][:, c * CHUNK:(c + 1) * CHUNK])
+        for t in (2, 3):
+            nc.vector.tensor_copy(pairs[CHUNKS - 1][:, 1, :, t % 2], planes[t][:, TOKENS - CHUNK:TOKENS])
+        for c in (3, 0, 1, 2):
+            cols = slice(c * CHUNK, (c + 1) * CHUNK)
+            y_bf = sb("y_bf%d" % c, [P, CHUNK * LANES], BF16)
+            y_codes = sb("y_codes%d" % c, [P, CHUNK], U32)
+            merged = y_bf[:].bitcast(F32).rearrange("p (n u) -> p n u", u=2)
+            apart = pairs[c][:].rearrange("p u n b -> p (u n b)").bitcast(F32).rearrange("p (u n) -> p n u", u=2)
+            if c == 2:
+                nc.scalar.copy(merged, apart)
+            else:
+                nc.vector.tensor_copy(merged, apart)
+            nc.vector.quantize_mx(out=y_codes[:].bitcast(E4M3X4), scales=y_scales[:, cols], in_=y_bf[:])
+            nc.sync.dma_start(words_out[:, cols], y_codes[:].bitcast(I32))
+        for quad in range(4):
+            queue = nc.sync if quad % 2 == 0 else nc.scalar
+            queue.dma_start(out_2[0, 4 * quad:4 * quad + 4, :].bitcast(I32),
+                            y_scales[32 * quad:32 * quad + 4, :].bitcast(I32))

@@ -22,7 +22,7 @@ SLOTS = 512
 TOKENS = 2048
 HALF = SLOTS // 2
 SLOT_TILES = SLOTS // P
-EARLY = 2
+EARLY = 1
 CHUNK = 512
 CHUNKS = TOKENS // CHUNK
 
@@ -36,8 +36,8 @@ def tile_attend_grouter_x_pl_kernel(tc, xT, W, dg, lb, ce, tx, offs, out_0, out_
         keep = ctx.enter_context(tc.tile_pool(name="keep", bufs=1))
         psum = ctx.enter_context(tc.psum_pool(name="psum", bufs=1))
 
-        def sb(name, shape, dtype):
-            return keep.tile(shape, dtype, name=name, align_bytes=64)
+        def sb(name, shape, dtype, tag=""):
+            return keep.tile(shape, dtype, name=name, tag=tag or name, align_bytes=64)
 
         banks = [psum.tile([P, 512], F32, name="bank%d" % b) for b in range(8)]
 
@@ -49,7 +49,6 @@ def tile_attend_grouter_x_pl_kernel(tc, xT, W, dg, lb, ce, tx, offs, out_0, out_
         tx_window = sb("tx_window", [P, TOKENS], F32)
         g_codes = sb("g_codes", [P, HALF + SLOTS], U32)
         g_scales = sb("g_scales", [P, HALF + SLOTS], U8)
-        planes = [sb("plane%d" % t, [P, TOKENS], F32) for t in range(LANES)]
         ident = sb("ident", [P, P], F32)
         tok = sb("tok", [P, SLOT_TILES, 2], F32)
         warm = sb("warm", [P, 1], F32)
@@ -77,8 +76,6 @@ def tile_attend_grouter_x_pl_kernel(tc, xT, W, dg, lb, ce, tx, offs, out_0, out_
 
         nc.vector.memset(g_codes[:, 0:HALF], 0)
         nc.vector.memset(g_scales[:, 0:HALF], 0)
-        for t in range(LANES):
-            nc.vector.memset(planes[t][:].bitcast(I32), 0)
 
         w_bf = sb("w_bf", [P, E, LANES], BF16)
         nc.scalar.copy(
@@ -133,8 +130,16 @@ def tile_attend_grouter_x_pl_kernel(tc, xT, W, dg, lb, ce, tx, offs, out_0, out_
                                     start=True, stop=True)
             for t in range(LANES):
                 acc = banks[2 * h + t // 2][:, (t % 2) * HALF:(t % 2 + 1) * HALF]
-                nc.scalar.activation(u_t[h][:, t, :], acc, ACT.Copy, scale=ce_col[:, t:t + 1])
+                if h == 0 and t >= 2:
+                    nc.vector.tensor_scalar(u_t[h][:, t, :], acc, ce_col[:, t:t + 1], None, ALU.mult)
+                else:
+                    nc.scalar.activation(u_t[h][:, t, :], acc, ACT.Copy, scale=ce_col[:, t:t + 1])
 
+        planes = []
+        for t, tenant in enumerate(("x_bf", "x_codes", "w1_codes", "u_t0")):
+            planes.append(sb("plane%d" % t, [P, TOKENS], F32, tag=tenant))
+        for t in range(LANES - 1):
+            nc.gpsimd.memset(planes[t][:], 0.0)
         hs = [sb("h%d" % j, [P, E], F32) for j in range(SLOT_TILES)]
         for j in range(SLOT_TILES):
             nc.vector.tensor_tensor(
@@ -202,6 +207,7 @@ def tile_attend_grouter_x_pl_kernel(tc, xT, W, dg, lb, ce, tx, offs, out_0, out_
 
         scores(0)
         scores(1)
+        nc.gpsimd.memset(planes[LANES - 1][:], 0.0)
         weights(0)
         scores(2)
         weights(1)
@@ -209,20 +215,22 @@ def tile_attend_grouter_x_pl_kernel(tc, xT, W, dg, lb, ce, tx, offs, out_0, out_
         scores(3)
         weights(2)
         turn(1)
+        quantise_g(0)
         weights(3)
         turn(2)
         turn(3)
-        quantise_g(0)
         for t in range(EARLY):
-            second_product(t, banks[2], 0)
-            nc.scalar.copy(dx[t][:, 0:HALF], banks[2][:, HALF:SLOTS])
+            second_product(0, banks[2], 0)
+            dx_early = sb("dx_early", [P, HALF], F32)
+            nc.scalar.copy(dx_early[:], banks[2][:, HALF:SLOTS])
         quantise_g(1)
         for t in range(EARLY):
-            nc.vector.tensor_copy(planes[t][:].indirect(half_offsets[0]), dx[t][:, 0:HALF])
+            nc.vector.tensor_copy(planes[t][:].indirect(half_offsets[0]), dx_early[:])
         for t in range(LANES):
-            second_product(t, banks[4 + t], HALF)
+            bank = banks[4 + t]
+            second_product(t, bank, HALF)
             first = HALF if t < EARLY else 0
-            nc.scalar.copy(dx[t][:, first:SLOTS], banks[4 + t][:, first:SLOTS])
+            nc.scalar.copy(dx[t][:, first:SLOTS], bank[:, first:SLOTS])
 
         out_rows = out_0.rearrange("(p j) n -> j p n", j=LANES)
         pairs = [sb("pairs%d" % c, [P, 2, CHUNK, 2], BF16) for c in range(CHUNKS)]
@@ -238,18 +246,25 @@ def tile_attend_grouter_x_pl_kernel(tc, xT, W, dg, lb, ce, tx, offs, out_0, out_
                 nc.scalar.copy(pairs[c][:, t // 2, :, t % 2], planes[t][:, c * CHUNK:(c + 1) * CHUNK])
         for t in (2, 3):
             nc.vector.tensor_copy(pairs[CHUNKS - 1][:, 1, :, t % 2], planes[t][:, TOKENS - CHUNK:TOKENS])
-        for c in (3, 0, 1, 2):
+        y_bf = [sb("y_bf%d" % c, [P, CHUNK * LANES], BF16) for c in range(CHUNKS)]
+
+        def merge(c, engine_copy):
+            engine_copy(y_bf[c][:].bitcast(F32).rearrange("p (n u) -> p n u", u=2),
+                        pairs[c][:].rearrange("p u n b -> p (u n b)").bitcast(F32).rearrange("p (u n) -> p n u", u=2))
+
+        def quantise_y(c):
             cols = slice(c * CHUNK, (c + 1) * CHUNK)
-            y_bf = sb("y_bf%d" % c, [P, CHUNK * LANES], BF16)
             y_codes = sb("y_codes%d" % c, [P, CHUNK], U32)
-            merged = y_bf[:].bitcast(F32).rearrange("p (n u) -> p n u", u=2)
-            apart = pairs[c][:].rearrange("p u n b -> p (u n b)").bitcast(F32).rearrange("p (u n) -> p n u", u=2)
-            if c == 2:
-                nc.scalar.copy(merged, apart)
-            else:
-                nc.vector.tensor_copy(merged, apart)
-            nc.vector.quantize_mx(out=y_codes[:].bitcast(E4M3X4), scales=y_scales[:, cols], in_=y_bf[:])
+            nc.vector.quantize_mx(out=y_codes[:].bitcast(E4M3X4), scales=y_scales[:, cols], in_=y_bf[c][:])
             nc.sync.dma_start(words_out[:, cols], y_codes[:].bitcast(I32))
+
+        merge(3, nc.vector.tensor_copy)
+        merge(0, nc.vector.tensor_copy)
+        quantise_y(3)
+        merge(1, nc.vector.tensor_copy)
+        merge(2, nc.scalar.copy)
+        for c in range(CHUNKS - 1):
+            quantise_y(c)
         for quad in range(4):
             queue = nc.sync if quad % 2 == 0 else nc.scalar
             queue.dma_start(out_2[0, 4 * quad:4 * quad + 4, :].bitcast(I32),

@@ -76,6 +76,9 @@ def tile_attend_grouter_x_pl_kernel(tc, xT, W, dg, lb, ce, tx, offs, out_0, out_
 
         nc.vector.memset(g_codes[:, 0:HALF], 0)
         nc.vector.memset(g_scales[:, 0:HALF], 0)
+        planes = [sb("plane%d" % t, [P, TOKENS], F32) for t in range(LANES)]
+        for t in range(LANES):
+            nc.vector.memset(planes[t][:].bitcast(I32), 0)
 
         w_bf = sb("w_bf", [P, E, LANES], BF16)
         nc.scalar.copy(
@@ -83,8 +86,6 @@ def tile_attend_grouter_x_pl_kernel(tc, xT, W, dg, lb, ce, tx, offs, out_0, out_
             w_raw[:].rearrange("p j (b t r) -> p t b r j", t=LANES, r=8))
         w1_codes = sb("w1_codes", [P, E], U32)
         w1_scales = sb("w1_scales", [P, E], U8)
-        nc.vector.quantize_mx(out=w1_codes[:].bitcast(E4M3X4), scales=w1_scales[:],
-                              in_=w_bf[:].rearrange("p e j -> p (e j)"))
         w_words = w_bf[:].rearrange("p e j -> p (e j)").bitcast(F32)
         wt_bf = sb("wt_bf", [P, D, LANES], BF16)
         for u in range(2):
@@ -96,8 +97,6 @@ def tile_attend_grouter_x_pl_kernel(tc, xT, W, dg, lb, ce, tx, offs, out_0, out_
                 banks[6 + u][:].bitcast(BF16).rearrange("p (t m c) -> p c m t", t=LANES, c=2))
         w2_codes = sb("w2_codes", [P, D], U32)
         w2_scales = sb("w2_scales", [P, D], U8)
-        nc.vector.quantize_mx(out=w2_codes[:].bitcast(E4M3X4), scales=w2_scales[:],
-                              in_=wt_bf[:].rearrange("p d t -> p (d t)"))
 
         for t in range(LANES):
             nc.tensor.transpose(banks[2][:, t * P:(t + 1) * P], ce_row[:, t * P:(t + 1) * P], ident[:])
@@ -105,6 +104,10 @@ def tile_attend_grouter_x_pl_kernel(tc, xT, W, dg, lb, ce, tx, offs, out_0, out_
         neg_ce = sb("neg_ce", [P, 1, LANES], F32)
         nc.scalar.copy(ce_col[:], banks[2][:, 0:512:P])
         nc.scalar.activation(neg_ce[:, 0, :], banks[2][:, 0:512:P], ACT.Copy, scale=-1.0)
+        ce_rows = sb("ce_rows", [P, E], F32)
+        for t in range(LANES):
+            nc.tensor.transpose(banks[4][:, t * P:(t + 1) * P], ce_col[:, t:t + 1].to_broadcast([P, P]), ident[:])
+        nc.scalar.copy(ce_rows[:], banks[4][:])
         tx_listed = sb("tx_listed", [P, SLOTS], F32)
         nc.vector.tensor_copy(tx_listed[:], tx_window[:].indirect(offsets[:]))
         for j in range(SLOT_TILES):
@@ -114,32 +117,35 @@ def tile_attend_grouter_x_pl_kernel(tc, xT, W, dg, lb, ce, tx, offs, out_0, out_
         x_bf = sb("x_bf", [P, SLOTS, LANES], BF16)
         x_codes = sb("x_codes", [P, SLOTS], U32)
         x_scales = sb("x_scales", [P, SLOTS], U8)
-        for j in range(LANES - 1):
-            nc.vector.tensor_copy(x_bf[:, :, j], x_raw[j][:].indirect(offsets[:]))
-        u_t = [sb("u_t%d" % h, [P, LANES, HALF], F32) for h in range(2)]
+        x_pair = sb("x_pair", [P, 2, SLOTS], BF16)
+        nc.vector.tensor_copy(x_pair[:, 0, :], x_raw[0][:].indirect(offsets[:]))
+        nc.vector.quantize_mx(out=w1_codes[:].bitcast(E4M3X4), scales=w1_scales[:],
+                              in_=w_bf[:].rearrange("p e j -> p (e j)"))
+        nc.vector.tensor_copy(x_pair[:, 1, :], x_raw[1][:].indirect(offsets[:]))
+        nc.scalar.copy(x_bf[:, :, 0:2], x_pair[:].rearrange("p j i -> p i j"))
+        nc.vector.tensor_copy(x_bf[:, :, 2], x_raw[2][:].indirect(offsets[:]))
+        nc.vector.quantize_mx(out=w2_codes[:].bitcast(E4M3X4), scales=w2_scales[:],
+                              in_=wt_bf[:].rearrange("p d t -> p (d t)"))
+        u_t = sb("u_t", [P, LANES, HALF], F32)
         for h in range(2):
             cols = slice(h * HALF, (h + 1) * HALF)
             nc.vector.tensor_copy(x_bf[:, cols, LANES - 1], x_raw[LANES - 1][:].indirect(half_offsets[h]))
             nc.vector.quantize_mx(out=x_codes[:, cols].bitcast(E4M3X4), scales=x_scales[:, cols],
                                   in_=x_bf[:, cols, :].rearrange("p i j -> p (i j)"))
-            for t in range(LANES):
-                acc = banks[2 * h + t // 2][:, (t % 2) * HALF:(t % 2 + 1) * HALF]
-                nc.tensor.matmul_mx(out=acc, lhsT=w1_codes[:, t * P:(t + 1) * P].bitcast(E4M3X4),
-                                    lhsT_scale=w1_scales[:, t * P:(t + 1) * P],
-                                    rhs=x_codes[:, cols].bitcast(E4M3X4), rhs_scale=x_scales[:, cols],
-                                    start=True, stop=True)
-            for t in range(LANES):
-                acc = banks[2 * h + t // 2][:, (t % 2) * HALF:(t % 2 + 1) * HALF]
-                if h == 0 and t >= 2:
-                    nc.vector.tensor_scalar(u_t[h][:, t, :], acc, ce_col[:, t:t + 1], None, ALU.mult)
-                else:
-                    nc.scalar.activation(u_t[h][:, t, :], acc, ACT.Copy, scale=ce_col[:, t:t + 1])
+        for j in range(2):
+            cols = slice(j * P, (j + 1) * P)
+            nc.tensor.matmul_mx(out=banks[j][:], lhsT=x_codes[:, cols].bitcast(E4M3X4), lhsT_scale=x_scales[:, cols],
+                                rhs=w1_codes[:].bitcast(E4M3X4), rhs_scale=w1_scales[:], start=True, stop=True)
+        for t in range(LANES):
+            acc = banks[2 + t // 2][:, (t % 2) * HALF:(t % 2 + 1) * HALF]
+            nc.tensor.matmul_mx(out=acc, lhsT=w1_codes[:, t * P:(t + 1) * P].bitcast(E4M3X4),
+                                lhsT_scale=w1_scales[:, t * P:(t + 1) * P],
+                                rhs=x_codes[:, HALF:SLOTS].bitcast(E4M3X4), rhs_scale=x_scales[:, HALF:SLOTS],
+                                start=True, stop=True)
+        for t in range(LANES):
+            acc = banks[2 + t // 2][:, (t % 2) * HALF:(t % 2 + 1) * HALF]
+            nc.scalar.activation(u_t[:, t, :], acc, ACT.Copy, scale=ce_col[:, t:t + 1])
 
-        planes = []
-        for t, tenant in enumerate(("x_bf", "x_codes", "w1_codes", "u_t0")):
-            planes.append(sb("plane%d" % t, [P, TOKENS], F32, tag=tenant))
-        for t in range(LANES - 1):
-            nc.gpsimd.memset(planes[t][:], 0.0)
         hs = [sb("h%d" % j, [P, E], F32) for j in range(SLOT_TILES)]
         for j in range(SLOT_TILES):
             nc.vector.tensor_tensor(
@@ -171,12 +177,15 @@ def tile_attend_grouter_x_pl_kernel(tc, xT, W, dg, lb, ce, tx, offs, out_0, out_
             kk.append(sb("kk%d" % j, [P, 1], F32))
 
         def scores(j):
-            bank = banks[4 + j % 2]
-            for t in range(LANES):
-                nc.tensor.transpose(bank[:, t * P:(t + 1) * P],
-                                    u_t[j // 2][:, t, (j % 2) * P:(j % 2 + 1) * P], ident[:])
-            nc.vector.tensor_scalar(neg_z[j][:], bank[:], tok[:, j, 0:1], None, ALU.mult, ALU.min,
-                                    accum_out=neg_m[j][:])
+            if j < 2:
+                nc.vector.scalar_tensor_tensor(neg_z[j][:], banks[j][:], tok[:, j, 0:1], ce_rows[:], ALU.mult, ALU.mult)
+                nc.vector.tensor_reduce(neg_m[j][:], neg_z[j][:], mybir.AxisListType.X, ALU.min)
+            else:
+                bank = banks[2 + j]
+                for t in range(LANES):
+                    nc.tensor.transpose(bank[:, t * P:(t + 1) * P], u_t[:, t, (j % 2) * P:(j % 2 + 1) * P], ident[:])
+                nc.vector.tensor_scalar(neg_z[j][:], bank[:], tok[:, j, 0:1], None, ALU.mult, ALU.min,
+                                        accum_out=neg_m[j][:])
             nc.scalar.activation(q[j][:], neg_z[j][:], ACT.Exp, bias=neg_m[j][:], scale=-1.0,
                                  accum_out=tot[j][:])
 
@@ -207,7 +216,6 @@ def tile_attend_grouter_x_pl_kernel(tc, xT, W, dg, lb, ce, tx, offs, out_0, out_
 
         scores(0)
         scores(1)
-        nc.gpsimd.memset(planes[LANES - 1][:], 0.0)
         weights(0)
         scores(2)
         weights(1)

@@ -16,18 +16,24 @@ ACT = mybir.ActivationFunctionType
 
 P = 128
 LANES = 4
+RUN = 8
+BANK = 512
 D = 512
 E = 512
 SLOTS = 512
 TOKENS = 2048
 HALF = SLOTS // 2
 SLOT_TILES = SLOTS // P
-EARLY = 1
+LIST_ROWS = 16
 CHUNK = 512
 CHUNKS = TOKENS // CHUNK
+VECTOR_CHUNK = CHUNKS - 1
+SCALAR_CHUNK = CHUNKS - 2
+QUADRANTS = 4
 
 FLOPS = 2 * 2 * D * E * SLOTS
-BYTES = 4 * (D * TOKENS + D * E + SLOTS * E + 2 * E + TOKENS) + 2 * SLOTS * 8 + 4 * D * TOKENS + D * TOKENS + 16 * TOKENS
+BYTES = (4 * (D * TOKENS + D * E + SLOTS * E + 2 * E + TOKENS) + 2 * P * SLOTS // LIST_ROWS
+         + 4 * D * TOKENS + D * TOKENS + 16 * TOKENS)
 
 
 def tile_attend_grouter_x_pl_kernel(tc, xT, W, dg, lb, ce, tx, offs, out_0, out_1, out_2):
@@ -39,241 +45,247 @@ def tile_attend_grouter_x_pl_kernel(tc, xT, W, dg, lb, ce, tx, offs, out_0, out_
         def sb(name, shape, dtype, tag=""):
             return keep.tile(shape, dtype, name=name, tag=tag or name, align_bytes=64)
 
-        banks = [psum.tile([P, 512], F32, name="bank%d" % b) for b in range(8)]
+        def block(number):
+            return slice(number * P, (number + 1) * P)
 
-        offsets = sb("offsets", [P, SLOTS // 16], U16)
+        def dealt(ap):
+            return ap.rearrange("p (t b r) -> p t b r", t=LANES, r=RUN)
+
+        def natural(ap):
+            return ap.rearrange("p (b t r) -> p t b r", t=LANES, r=RUN)
+
+        banks = [psum.tile([P, BANK], F32, name="bank%d" % b) for b in range(8)]
+
+        offsets = sb("offsets", [P, SLOTS // LIST_ROWS], U16)
         nc.sync.dma_start(offsets[:], offs)
-        half_offsets = [offsets[:, 0:16], offsets[:, 16:32]]
+        half_columns = HALF // LIST_ROWS
+        half_offsets = [offsets[:, 0:half_columns], offsets[:, half_columns:2 * half_columns]]
 
-        ce_row = sb("ce_row", [P, E], F32)
-        tx_window = sb("tx_window", [P, TOKENS], F32)
-        g_codes = sb("g_codes", [P, HALF + SLOTS], U32)
-        g_scales = sb("g_scales", [P, HALF + SLOTS], U8)
         ident = sb("ident", [P, P], F32)
-        tok = sb("tok", [P, SLOT_TILES, 2], F32)
-        warm = sb("warm", [P, 1], F32)
         make_identity(nc, ident[:])
-        nc.gpsimd.memset(tok[:], -1.0)
-        nc.scalar.activation(warm[:], ident[:, 0:1], ACT.Exp)
-        nc.vector.memset(ce_row[:], 0.0)
-        nc.vector.memset(tx_window[:].bitcast(I32), 0)
+        token_factors = sb("token_factors", [P, SLOT_TILES, 2], F32)
+        ones = sb("ones", [P, SLOT_TILES], F32)
+        nc.scalar.activation(ones[:], ident[:, 0:SLOT_TILES], ACT.Exp, scale=0.0)
+        nc.scalar.activation(token_factors[:, :, 1], ones[:], ACT.Copy, scale=-1.0)
 
+        ce_lanes = sb("ce_lanes", [P, P], F32)
+        tx_window = sb("tx_window", [P, TOKENS], F32)
+        nc.vector.memset(ce_lanes[:], 0.0)
+        nc.vector.memset(tx_window[:].bitcast(I32), 0)
         w_raw = sb("w_raw", [P, LANES, E], F32)
         nc.sync.dma_start(w_raw[:], W.rearrange("(p j) e -> p j e", j=LANES))
-        nc.sync.dma_start(
-            ce_row[0:1, :].rearrange("o (t b r) -> o t b r", t=LANES, r=8),
-            ce[0:1, :].rearrange("o (b t r) -> o t b r", t=LANES, r=8))
+        nc.sync.dma_start(ce_lanes[0:LANES, :].rearrange("t (b r) -> t b r", r=RUN),
+                          ce[0, :].rearrange("(b t r) -> t b r", t=LANES, r=RUN))
         nc.sync.dma_start(tx_window[0:1, :], tx[0:1, :])
-        x_rows = xT.rearrange("(p j) n -> j p n", j=LANES)
+        x_rows = xT.rearrange("(p j) x -> j p x", j=LANES)
         x_raw = [sb("x_raw%d" % j, [P, TOKENS], F32) for j in range(LANES)]
         for j in range(LANES):
             nc.sync.dma_start(x_raw[j][:], x_rows[j])
         lb_rows = sb("lb_rows", [P, E], F32)
         nc.sync.dma_start(lb_rows[:], lb)
-        dg_raw = [sb("dg_raw%d" % h, [P, 2, E], F32) for h in range(2)]
-        for h in range(2):
-            nc.sync.dma_start(dg_raw[h][:], dg[h * HALF:(h + 1) * HALF, :].rearrange("(j p) e -> p j e", p=P))
+        dg_raw = [sb("dg_raw%d" % half, [P, 2, E], F32) for half in range(2)]
+        for half in range(2):
+            nc.sync.dma_start(dg_raw[half][:],
+                              dg[half * HALF:(half + 1) * HALF, :].rearrange("(n p) e -> p n e", p=P))
 
+        g_codes = sb("g_codes", [P, HALF + SLOTS], U32)
+        g_scales = sb("g_scales", [P, HALF + SLOTS], U8)
         nc.vector.memset(g_codes[:, 0:HALF], 0)
         nc.vector.memset(g_scales[:, 0:HALF], 0)
-        planes = [sb("plane%d" % t, [P, TOKENS], F32) for t in range(LANES)]
-        for t in range(LANES):
-            nc.vector.memset(planes[t][:].bitcast(I32), 0)
+        planes = [sb("plane%d" % j, [P, TOKENS], F32) for j in range(LANES)]
+        for j in range(2):
+            nc.vector.memset(planes[j][:].bitcast(I32), 0)
 
         w_bf = sb("w_bf", [P, E, LANES], BF16)
-        nc.scalar.copy(
-            w_bf[:].rearrange("p (t b r) j -> p t b r j", t=LANES, r=8),
-            w_raw[:].rearrange("p j (b t r) -> p t b r j", t=LANES, r=8))
-        w1_codes = sb("w1_codes", [P, E], U32)
-        w1_scales = sb("w1_scales", [P, E], U8)
-        w_words = w_bf[:].rearrange("p e j -> p (e j)").bitcast(F32)
-        wt_bf = sb("wt_bf", [P, D, LANES], BF16)
-        for u in range(2):
-            for t in range(LANES):
-                nc.tensor.transpose(banks[6 + u][:, t * P:(t + 1) * P],
-                                    w_words[:, 2 * P * t + u:2 * P * (t + 1):2], ident[:])
-            nc.scalar.copy(
-                wt_bf[:, 2 * P * u:2 * P * (u + 1), :].rearrange("p (c m) t -> p c m t", c=2),
-                banks[6 + u][:].bitcast(BF16).rearrange("p (t m c) -> p c m t", t=LANES, c=2))
-        w2_codes = sb("w2_codes", [P, D], U32)
-        w2_scales = sb("w2_scales", [P, D], U8)
+        nc.scalar.copy(w_bf[:].rearrange("p (t b r) j -> p t b r j", t=LANES, r=RUN),
+                       w_raw[:].rearrange("p j (b t r) -> p t b r j", t=LANES, r=RUN))
 
-        for t in range(LANES):
-            nc.tensor.transpose(banks[2][:, t * P:(t + 1) * P], ce_row[:, t * P:(t + 1) * P], ident[:])
+        nc.tensor.transpose(banks[2][:, 0:P], ce_lanes[:], ident[:])
         ce_col = sb("ce_col", [P, LANES], F32)
         neg_ce = sb("neg_ce", [P, 1, LANES], F32)
-        nc.scalar.copy(ce_col[:], banks[2][:, 0:512:P])
-        nc.scalar.activation(neg_ce[:, 0, :], banks[2][:, 0:512:P], ACT.Copy, scale=-1.0)
+        nc.scalar.copy(ce_col[:], banks[2][:, 0:LANES])
+        nc.scalar.activation(neg_ce[:, 0, :], banks[2][:, 0:LANES], ACT.Copy, scale=-1.0)
         ce_rows = sb("ce_rows", [P, E], F32)
         for t in range(LANES):
-            nc.tensor.transpose(banks[4][:, t * P:(t + 1) * P], ce_col[:, t:t + 1].to_broadcast([P, P]), ident[:])
+            nc.tensor.transpose(banks[4][:, block(t)], ce_col[:, t:t + 1].to_broadcast([P, P]), ident[:])
         nc.scalar.copy(ce_rows[:], banks[4][:])
         tx_listed = sb("tx_listed", [P, SLOTS], F32)
         nc.vector.tensor_copy(tx_listed[:], tx_window[:].indirect(offsets[:]))
-        for j in range(SLOT_TILES):
-            nc.tensor.transpose(banks[3][:, j * P:(j + 1) * P], tx_listed[:, j * P:(j + 1) * P], ident[:])
-        nc.scalar.activation(tok[:, :, 0], banks[3][:, 0:512:P], ACT.Copy, scale=-1.0)
+        for n in range(SLOT_TILES):
+            nc.tensor.transpose(banks[3][:, block(n)], tx_listed[:, block(n)], ident[:])
+        nc.scalar.activation(token_factors[:, :, 0], banks[3][:, 0:BANK:P], ACT.Copy, scale=-1.0)
 
         x_bf = sb("x_bf", [P, SLOTS, LANES], BF16)
+        x_pair = sb("x_pair", [P, 2, SLOTS], BF16)
+        for j in range(2):
+            nc.vector.tensor_copy(x_pair[:, j, :], x_raw[j][:].indirect(offsets[:]))
+        nc.scalar.copy(x_bf[:, :, 0:2], x_pair[:].rearrange("p j i -> p i j"))
+
+        w_words = w_bf[:].rearrange("p e j -> p (e j)").bitcast(F32)
+        wt_bf = sb("wt_bf", [P, D, LANES], BF16, tag="x_pair")
+        for u in range(2):
+            for t in range(LANES):
+                nc.tensor.transpose(banks[6 + u][:, block(t)], w_words[:, 2 * P * t + u:2 * P * (t + 1):2], ident[:])
+            nc.scalar.copy(wt_bf[:, 2 * P * u:2 * P * (u + 1), :].rearrange("p (k v) t -> p k v t", k=2),
+                           banks[6 + u][:].bitcast(BF16).rearrange("p (t v k) -> p k v t", t=LANES, k=2))
+
+        nc.vector.tensor_copy(x_bf[:, :, 2], x_raw[2][:].indirect(offsets[:]))
+        w_d_codes = sb("w_d_codes", [P, E], U32)
+        w_d_scales = sb("w_d_scales", [P, E], U8)
+        nc.vector.quantize_mx(out=w_d_codes[:].bitcast(E4M3X4), scales=w_d_scales[:],
+                              in_=w_bf[:].rearrange("p e j -> p (e j)"))
+
         x_codes = sb("x_codes", [P, SLOTS], U32)
         x_scales = sb("x_scales", [P, SLOTS], U8)
-        x_pair = sb("x_pair", [P, 2, SLOTS], BF16)
-        nc.vector.tensor_copy(x_pair[:, 0, :], x_raw[0][:].indirect(offsets[:]))
-        nc.vector.quantize_mx(out=w1_codes[:].bitcast(E4M3X4), scales=w1_scales[:],
-                              in_=w_bf[:].rearrange("p e j -> p (e j)"))
-        nc.vector.tensor_copy(x_pair[:, 1, :], x_raw[1][:].indirect(offsets[:]))
-        nc.scalar.copy(x_bf[:, :, 0:2], x_pair[:].rearrange("p j i -> p i j"))
-        nc.vector.tensor_copy(x_bf[:, :, 2], x_raw[2][:].indirect(offsets[:]))
-        nc.vector.quantize_mx(out=w2_codes[:].bitcast(E4M3X4), scales=w2_scales[:],
-                              in_=wt_bf[:].rearrange("p d t -> p (d t)"))
-        u_t = sb("u_t", [P, LANES, HALF], F32)
-        for h in range(2):
-            cols = slice(h * HALF, (h + 1) * HALF)
-            nc.vector.tensor_copy(x_bf[:, cols, LANES - 1], x_raw[LANES - 1][:].indirect(half_offsets[h]))
+        scaled_t = sb("scaled_t", [P, LANES, HALF], F32)
+        for half in range(2):
+            cols = slice(half * HALF, (half + 1) * HALF)
+            nc.vector.tensor_copy(x_bf[:, cols, LANES - 1], x_raw[LANES - 1][:].indirect(half_offsets[half]))
             nc.vector.quantize_mx(out=x_codes[:, cols].bitcast(E4M3X4), scales=x_scales[:, cols],
                                   in_=x_bf[:, cols, :].rearrange("p i j -> p (i j)"))
-        for j in range(2):
-            cols = slice(j * P, (j + 1) * P)
-            nc.tensor.matmul_mx(out=banks[j][:], lhsT=x_codes[:, cols].bitcast(E4M3X4), lhsT_scale=x_scales[:, cols],
-                                rhs=w1_codes[:].bitcast(E4M3X4), rhs_scale=w1_scales[:], start=True, stop=True)
+        for n in range(2):
+            nc.tensor.matmul_mx(out=banks[n][:], lhsT=x_codes[:, block(n)].bitcast(E4M3X4),
+                                lhsT_scale=x_scales[:, block(n)],
+                                rhs=w_d_codes[:].bitcast(E4M3X4), rhs_scale=w_d_scales[:], start=True, stop=True)
+        sums = [banks[2 + t // 2][:, (t % 2) * HALF:(t % 2 + 1) * HALF] for t in range(LANES)]
         for t in range(LANES):
-            acc = banks[2 + t // 2][:, (t % 2) * HALF:(t % 2 + 1) * HALF]
-            nc.tensor.matmul_mx(out=acc, lhsT=w1_codes[:, t * P:(t + 1) * P].bitcast(E4M3X4),
-                                lhsT_scale=w1_scales[:, t * P:(t + 1) * P],
+            nc.tensor.matmul_mx(out=sums[t], lhsT=w_d_codes[:, block(t)].bitcast(E4M3X4),
+                                lhsT_scale=w_d_scales[:, block(t)],
                                 rhs=x_codes[:, HALF:SLOTS].bitcast(E4M3X4), rhs_scale=x_scales[:, HALF:SLOTS],
                                 start=True, stop=True)
         for t in range(LANES):
-            acc = banks[2 + t // 2][:, (t % 2) * HALF:(t % 2 + 1) * HALF]
-            nc.scalar.activation(u_t[:, t, :], acc, ACT.Copy, scale=ce_col[:, t:t + 1])
+            nc.scalar.activation(scaled_t[:, t, :], sums[t], ACT.Copy, scale=ce_col[:, t:t + 1])
 
-        hs = [sb("h%d" % j, [P, E], F32) for j in range(SLOT_TILES)]
-        for j in range(SLOT_TILES):
-            nc.vector.tensor_tensor(
-                hs[j][:].rearrange("p (t b r) -> p t b r", t=LANES, r=8),
-                dg_raw[j // 2][:, j % 2, :].rearrange("p (b t r) -> p t b r", t=LANES, r=8),
-                lb_rows[:].rearrange("p (b t r) -> p t b r", t=LANES, r=8), ALU.add)
+        h_tiles = [sb("h%d" % n, [P, E], F32) for n in range(SLOT_TILES)]
+        for n in range(SLOT_TILES):
+            nc.vector.tensor_tensor(dealt(h_tiles[n][:]), natural(dg_raw[n // 2][:, n % 2, :]),
+                                    natural(lb_rows[:]), ALU.add)
 
-        dx = [sb("dx%d" % t, [P, SLOTS], F32) for t in range(LANES)]
-        g_bf = [sb("g_bf%d" % h, [P, HALF, LANES], BF16) for h in range(2)]
+        def per_tile(name, width):
+            return [sb("%s%d" % (name, n), [P, width], F32) for n in range(SLOT_TILES)]
 
-        def second_product(t, bank, first):
+        neg_z, q, term_h, term_s = [per_tile(name, E) for name in ("neg_z", "q", "term_h", "term_s")]
+        neg_m, tot, inv_tot, neg_tx_s, s_factor = [
+            per_tile(name, 1) for name in ("neg_m", "tot", "inv_tot", "neg_tx_s", "s_factor")]
+        factors = per_tile("factors", 2)
+        g_bf = [sb("g_bf%d" % half, [P, HALF, LANES], BF16) for half in range(2)]
+
+        def softmax(n):
+            neg_tx = token_factors[:, n, 0:1]
+            if n < 2:
+                nc.vector.scalar_tensor_tensor(neg_z[n][:], banks[n][:], neg_tx, ce_rows[:], ALU.mult, ALU.mult)
+                nc.vector.tensor_reduce(neg_m[n][:], neg_z[n][:], mybir.AxisListType.X, ALU.min)
+            else:
+                bank = banks[2 + n]
+                for t in range(LANES):
+                    nc.tensor.transpose(bank[:, block(t)], scaled_t[:, t, block(n % 2)], ident[:])
+                nc.vector.tensor_scalar(neg_z[n][:], bank[:], neg_tx, None, ALU.mult, ALU.min,
+                                        accum_out=neg_m[n][:])
+            nc.scalar.activation(q[n][:], neg_z[n][:], ACT.Exp, bias=neg_m[n][:], scale=-1.0, accum_out=tot[n][:])
+
+        def terms(n):
+            nc.vector.reciprocal(inv_tot[n][:], tot[n][:])
+            nc.vector.tensor_scalar(factors[n][:], token_factors[:, n, :], inv_tot[n][:], None, ALU.mult)
+            nc.vector.scalar_tensor_tensor(term_h[n][:], q[n][:], factors[n][:, 0:1], h_tiles[n][:],
+                                           ALU.mult, ALU.mult, accum_out=neg_tx_s[n][:])
+            nc.scalar.activation(s_factor[n][:], neg_tx_s[n][:], ACT.Copy, scale=factors[n][:, 1:2])
+            nc.scalar.activation(term_s[n][:], q[n][:], ACT.Copy, scale=s_factor[n][:])
+
+        def turn(n):
+            bank = banks[n]
+            for t in range(LANES):
+                nc.tensor.matmul(bank[:, block(t)], term_h[n][:, block(t)], ident[:],
+                                 start=(t == 0), stop=False, is_transpose=True)
+            for t in range(LANES):
+                nc.tensor.matmul(bank[:, block(t)], term_s[n][:, block(t)], ident[:],
+                                 start=False, stop=(t == LANES - 1), is_transpose=True)
+            nc.vector.tensor_tensor(g_bf[n // 2][:, block(n % 2), :], bank[:].rearrange("p (t i) -> p i t", t=LANES),
+                                    neg_ce[:].to_broadcast([P, P, LANES]), ALU.mult)
+
+        def quantise_g(half):
+            cols = slice((half + 1) * HALF, (half + 2) * HALF)
+            nc.vector.quantize_mx(out=g_codes[:, cols].bitcast(E5M2X4), scales=g_scales[:, cols],
+                                  in_=g_bf[half][:].rearrange("p i t -> p (i t)"))
+
+        softmax(0)
+        softmax(1)
+        terms(0)
+        softmax(2)
+        terms(1)
+        turn(0)
+        softmax(3)
+        w_e_codes = sb("w_e_codes", [P, D], U32, tag="scaled_t")
+        w_e_scales = sb("w_e_scales", [P, D], U8)
+        nc.vector.quantize_mx(out=w_e_codes[:].bitcast(E4M3X4), scales=w_e_scales[:],
+                              in_=wt_bf[:].rearrange("p d t -> p (d t)"))
+        terms(2)
+        turn(1)
+        quantise_g(0)
+        terms(3)
+        turn(2)
+        turn(3)
+
+        def dx_pass(j, bank, first):
             cols = slice(first, first + SLOTS)
-            nc.tensor.matmul_mx(out=bank[:], lhsT=w2_codes[:, t * P:(t + 1) * P].bitcast(E4M3X4),
-                                lhsT_scale=w2_scales[:, t * P:(t + 1) * P],
+            nc.tensor.matmul_mx(out=bank[:], lhsT=w_e_codes[:, block(j)].bitcast(E4M3X4),
+                                lhsT_scale=w_e_scales[:, block(j)],
                                 rhs=g_codes[:, cols].bitcast(E5M2X4), rhs_scale=g_scales[:, cols],
                                 start=True, stop=True)
 
-        q, neg_z, neg_m, tot, rec, fac, ph, acc_s, kk, t2 = [[] for n in range(10)]
-        for j in range(SLOT_TILES):
-            q.append(sb("q%d" % j, [P, E], F32))
-            neg_z.append(sb("neg_z%d" % j, [P, E], F32))
-            ph.append(sb("ph%d" % j, [P, E], F32))
-            t2.append(sb("t2%d" % j, [P, E], F32))
-            neg_m.append(sb("neg_m%d" % j, [P, 1], F32))
-            tot.append(sb("tot%d" % j, [P, 1], F32))
-            rec.append(sb("rec%d" % j, [P, 1], F32))
-            fac.append(sb("fac%d" % j, [P, 2], F32))
-            acc_s.append(sb("acc_s%d" % j, [P, 1], F32))
-            kk.append(sb("kk%d" % j, [P, 1], F32))
-
-        def scores(j):
-            if j < 2:
-                nc.vector.scalar_tensor_tensor(neg_z[j][:], banks[j][:], tok[:, j, 0:1], ce_rows[:], ALU.mult, ALU.mult)
-                nc.vector.tensor_reduce(neg_m[j][:], neg_z[j][:], mybir.AxisListType.X, ALU.min)
-            else:
-                bank = banks[2 + j]
-                for t in range(LANES):
-                    nc.tensor.transpose(bank[:, t * P:(t + 1) * P], u_t[:, t, (j % 2) * P:(j % 2 + 1) * P], ident[:])
-                nc.vector.tensor_scalar(neg_z[j][:], bank[:], tok[:, j, 0:1], None, ALU.mult, ALU.min,
-                                        accum_out=neg_m[j][:])
-            nc.scalar.activation(q[j][:], neg_z[j][:], ACT.Exp, bias=neg_m[j][:], scale=-1.0,
-                                 accum_out=tot[j][:])
-
-        def weights(j):
-            nc.vector.reciprocal(rec[j][:], tot[j][:])
-            nc.vector.tensor_scalar(fac[j][:], tok[:, j, :], rec[j][:], None, ALU.mult)
-            nc.vector.scalar_tensor_tensor(ph[j][:], q[j][:], fac[j][:, 0:1], hs[j][:], ALU.mult, ALU.mult,
-                                           accum_out=acc_s[j][:])
-            nc.scalar.activation(kk[j][:], acc_s[j][:], ACT.Copy, scale=fac[j][:, 1:2])
-            nc.scalar.activation(t2[j][:], q[j][:], ACT.Copy, scale=kk[j][:])
-
-        def turn(j):
-            bank = banks[j]
-            for t in range(LANES):
-                cols = slice(t * P, (t + 1) * P)
-                nc.tensor.matmul(bank[:, cols], ph[j][:, cols], ident[:], start=(t == 0), stop=False, is_transpose=True)
-            for t in range(LANES):
-                cols = slice(t * P, (t + 1) * P)
-                nc.tensor.matmul(bank[:, cols], t2[j][:, cols], ident[:], start=False, stop=(t == LANES - 1), is_transpose=True)
-            nc.vector.tensor_tensor(g_bf[j // 2][:, (j % 2) * P:(j % 2 + 1) * P, :],
-                                    bank[:].rearrange("p (t i) -> p i t", t=LANES),
-                                    neg_ce[:].to_broadcast([P, P, LANES]), ALU.mult)
-
-        def quantise_g(h):
-            cols = slice((h + 1) * HALF, (h + 2) * HALF)
-            nc.vector.quantize_mx(out=g_codes[:, cols].bitcast(E5M2X4), scales=g_scales[:, cols],
-                                  in_=g_bf[h][:].rearrange("p i t -> p (i t)"))
-
-        scores(0)
-        scores(1)
-        weights(0)
-        scores(2)
-        weights(1)
-        turn(0)
-        scores(3)
-        weights(2)
-        turn(1)
-        quantise_g(0)
-        weights(3)
-        turn(2)
-        turn(3)
-        for t in range(EARLY):
-            second_product(0, banks[2], 0)
-            dx_early = sb("dx_early", [P, HALF], F32)
-            nc.scalar.copy(dx_early[:], banks[2][:, HALF:SLOTS])
+        dx_pass(0, banks[7], 0)
+        dx_early = sb("dx_early", [P, HALF], F32)
+        nc.scalar.copy(dx_early[:], banks[7][:, HALF:SLOTS])
         quantise_g(1)
-        for t in range(EARLY):
-            nc.vector.tensor_copy(planes[t][:].indirect(half_offsets[0]), dx_early[:])
-        for t in range(LANES):
-            bank = banks[4 + t]
-            second_product(t, bank, HALF)
-            first = HALF if t < EARLY else 0
-            nc.scalar.copy(dx[t][:, first:SLOTS], bank[:, first:SLOTS])
+        nc.vector.tensor_copy(planes[0][:].indirect(half_offsets[0]), dx_early[:])
+        dx = [sb("dx%d" % j, [P, SLOTS], F32) for j in range(LANES)]
+        for j in range(LANES):
+            first = HALF if j == 0 else 0
+            dx_pass(j, banks[4 + j], HALF)
+            nc.scalar.copy(dx[j][:, first:SLOTS], banks[4 + j][:, first:SLOTS])
 
-        out_rows = out_0.rearrange("(p j) n -> j p n", j=LANES)
+        out_rows = out_0.rearrange("(p j) x -> j p x", j=LANES)
         pairs = [sb("pairs%d" % c, [P, 2, CHUNK, 2], BF16) for c in range(CHUNKS)]
-        y_scales = sb("y_scales", [P, TOKENS], U8)
-        words_out = out_1[0].rearrange("p n l -> p (n l)").bitcast(I32)
-        for t in range(LANES):
-            if t < EARLY:
-                nc.vector.tensor_copy(planes[t][:].indirect(half_offsets[1]), dx[t][:, HALF:SLOTS])
-            else:
-                nc.vector.tensor_copy(planes[t][:].indirect(offsets[:]), dx[t][:])
-            nc.sync.dma_start(out_rows[t], planes[t][:])
-            for c in range(CHUNKS if t < 2 else CHUNKS - 1):
-                nc.scalar.copy(pairs[c][:, t // 2, :, t % 2], planes[t][:, c * CHUNK:(c + 1) * CHUNK])
-        for t in (2, 3):
-            nc.vector.tensor_copy(pairs[CHUNKS - 1][:, 1, :, t % 2], planes[t][:, TOKENS - CHUNK:TOKENS])
-        y_bf = [sb("y_bf%d" % c, [P, CHUNK * LANES], BF16) for c in range(CHUNKS)]
 
-        def merge(c, engine_copy):
-            engine_copy(y_bf[c][:].bitcast(F32).rearrange("p (n u) -> p n u", u=2),
-                        pairs[c][:].rearrange("p u n b -> p (u n b)").bitcast(F32).rearrange("p (u n) -> p n u", u=2))
+        def chunk(c):
+            return slice(c * CHUNK, (c + 1) * CHUNK)
+
+        for j in range(LANES):
+            if j >= 2:
+                for c in range(CHUNKS):
+                    nc.vector.memset(planes[j][:, chunk(c)].bitcast(I32), 0)
+            if j == 0:
+                nc.vector.tensor_copy(planes[j][:].indirect(half_offsets[1]), dx[j][:, HALF:SLOTS])
+            else:
+                nc.vector.tensor_copy(planes[j][:].indirect(offsets[:]), dx[j][:])
+            nc.sync.dma_start(out_rows[j], planes[j][:])
+            for c in range(CHUNKS):
+                if j < 2 or c != VECTOR_CHUNK:
+                    nc.scalar.copy(pairs[c][:, j // 2, :, j % 2], planes[j][:, chunk(c)])
+        for j in (2, 3):
+            nc.vector.tensor_copy(pairs[VECTOR_CHUNK][:, 1, :, j % 2], planes[j][:, chunk(VECTOR_CHUNK)])
+
+        y_bf = [sb("y_bf%d" % c, [P, CHUNK * LANES], BF16) for c in range(CHUNKS)]
+        y_scales = sb("y_scales", [P, TOKENS], U8)
+        words_out = out_1[0].rearrange("p x j -> p (x j)").bitcast(I32)
+
+        def merge(c):
+            copy_words = nc.scalar.copy if c == SCALAR_CHUNK else nc.vector.tensor_copy
+            copy_words(y_bf[c][:].bitcast(F32).rearrange("p (x u) -> p x u", u=2),
+                       pairs[c][:].rearrange("p u x k -> p (u x k)").bitcast(F32).rearrange("p (u x) -> p x u", u=2))
 
         def quantise_y(c):
-            cols = slice(c * CHUNK, (c + 1) * CHUNK)
             y_codes = sb("y_codes%d" % c, [P, CHUNK], U32)
-            nc.vector.quantize_mx(out=y_codes[:].bitcast(E4M3X4), scales=y_scales[:, cols], in_=y_bf[c][:])
-            nc.sync.dma_start(words_out[:, cols], y_codes[:].bitcast(I32))
+            nc.vector.quantize_mx(out=y_codes[:].bitcast(E4M3X4), scales=y_scales[:, chunk(c)], in_=y_bf[c][:])
+            nc.sync.dma_start(words_out[:, chunk(c)], y_codes[:].bitcast(I32))
 
-        merge(3, nc.vector.tensor_copy)
-        merge(0, nc.vector.tensor_copy)
-        quantise_y(3)
-        merge(1, nc.vector.tensor_copy)
-        merge(2, nc.scalar.copy)
-        for c in range(CHUNKS - 1):
+        merge(VECTOR_CHUNK)
+        merge(0)
+        quantise_y(VECTOR_CHUNK)
+        merge(1)
+        merge(SCALAR_CHUNK)
+        for c in range(VECTOR_CHUNK):
             quantise_y(c)
-        for quad in range(4):
+        for quad in range(QUADRANTS):
             queue = nc.sync if quad % 2 == 0 else nc.scalar
             queue.dma_start(out_2[0, 4 * quad:4 * quad + 4, :].bitcast(I32),
                             y_scales[32 * quad:32 * quad + 4, :].bitcast(I32))

@@ -29,6 +29,7 @@ CHUNK = 512
 CHUNKS = TOKENS // CHUNK
 VECTOR_CHUNK = CHUNKS - 1
 SCALAR_CHUNK = CHUNKS - 2
+WINDOWS = 3
 QUADRANTS = 4
 
 FLOPS = 2 * 2 * D * E * SLOTS
@@ -92,9 +93,10 @@ def tile_attend_grouter_x_pl_kernel(tc, xT, W, dg, lb, ce, tx, offs, out_0, out_
         g_scales = sb("g_scales", [P, HALF + SLOTS], U8)
         nc.vector.memset(g_codes[:, 0:HALF], 0)
         nc.vector.memset(g_scales[:, 0:HALF], 0)
-        planes = [sb("plane%d" % j, [P, TOKENS], F32) for j in range(LANES)]
-        for j in range(2):
-            nc.vector.memset(planes[j][:].bitcast(I32), 0)
+        windows = [sb("window%d" % j, [P, TOKENS], F32) for j in range(WINDOWS)]
+        for window in windows:
+            nc.vector.memset(window[:].bitcast(I32), 0)
+        planes = [windows[j % WINDOWS] for j in range(LANES)]
 
         w_bf = sb("w_bf", [P, E, LANES], BF16)
         nc.scalar.copy(w_bf[:].rearrange("p (t b r) j -> p t b r j", t=LANES, r=RUN),
@@ -114,6 +116,8 @@ def tile_attend_grouter_x_pl_kernel(tc, xT, W, dg, lb, ce, tx, offs, out_0, out_
         for n in range(SLOT_TILES):
             nc.tensor.transpose(banks[3][:, block(n)], tx_listed[:, block(n)], ident[:])
         nc.scalar.activation(token_factors[:, :, 0], banks[3][:, 0:BANK:P], ACT.Copy, scale=-1.0)
+        token_inverses = sb("token_inverses", [P, SLOT_TILES, 2], F32)
+        nc.vector.reciprocal(token_inverses[:], token_factors[:])
 
         x_bf = sb("x_bf", [P, SLOTS, LANES], BF16)
         x_pair = sb("x_pair", [P, 2, SLOTS], BF16)
@@ -122,7 +126,7 @@ def tile_attend_grouter_x_pl_kernel(tc, xT, W, dg, lb, ce, tx, offs, out_0, out_
         nc.scalar.copy(x_bf[:, :, 0:2], x_pair[:].rearrange("p j i -> p i j"))
 
         w_words = w_bf[:].rearrange("p e j -> p (e j)").bitcast(F32)
-        wt_bf = sb("wt_bf", [P, D, LANES], BF16, tag="x_pair")
+        wt_bf = sb("wt_bf", [P, D, LANES], BF16)
         for u in range(2):
             for t in range(LANES):
                 nc.tensor.transpose(banks[6 + u][:, block(t)], w_words[:, 2 * P * t + u:2 * P * (t + 1):2], ident[:])
@@ -134,6 +138,10 @@ def tile_attend_grouter_x_pl_kernel(tc, xT, W, dg, lb, ce, tx, offs, out_0, out_
         w_d_scales = sb("w_d_scales", [P, E], U8)
         nc.vector.quantize_mx(out=w_d_codes[:].bitcast(E4M3X4), scales=w_d_scales[:],
                               in_=w_bf[:].rearrange("p e j -> p (e j)"))
+        w_e_codes = sb("w_e_codes", [P, D], U32)
+        w_e_scales = sb("w_e_scales", [P, D], U8)
+        nc.vector.quantize_mx(out=w_e_codes[:].bitcast(E4M3X4), scales=w_e_scales[:],
+                              in_=wt_bf[:].rearrange("p d t -> p (d t)"))
 
         x_codes = sb("x_codes", [P, SLOTS], U32)
         x_scales = sb("x_scales", [P, SLOTS], U8)
@@ -165,9 +173,10 @@ def tile_attend_grouter_x_pl_kernel(tc, xT, W, dg, lb, ce, tx, offs, out_0, out_
             return [sb("%s%d" % (name, n), [P, width], F32) for n in range(SLOT_TILES)]
 
         neg_z, q, term_h, term_s = [per_tile(name, E) for name in ("neg_z", "q", "term_h", "term_s")]
-        neg_m, tot, inv_tot, neg_tx_s, s_factor = [
-            per_tile(name, 1) for name in ("neg_m", "tot", "inv_tot", "neg_tx_s", "s_factor")]
+        neg_m, tot, neg_tx_s, s_factor = [
+            per_tile(name, 1) for name in ("neg_m", "tot", "neg_tx_s", "s_factor")]
         factors = per_tile("factors", 2)
+        divisors = per_tile("divisors", 2)
         g_bf = [sb("g_bf%d" % half, [P, HALF, LANES], BF16) for half in range(2)]
 
         def softmax(n):
@@ -182,10 +191,10 @@ def tile_attend_grouter_x_pl_kernel(tc, xT, W, dg, lb, ce, tx, offs, out_0, out_
                 nc.vector.tensor_scalar(neg_z[n][:], bank[:], neg_tx, None, ALU.mult, ALU.min,
                                         accum_out=neg_m[n][:])
             nc.scalar.activation(q[n][:], neg_z[n][:], ACT.Exp, bias=neg_m[n][:], scale=-1.0, accum_out=tot[n][:])
+            nc.scalar.activation(divisors[n][:], token_inverses[:, n, :], ACT.Copy, scale=tot[n][:])
 
         def terms(n):
-            nc.vector.reciprocal(inv_tot[n][:], tot[n][:])
-            nc.vector.tensor_scalar(factors[n][:], token_factors[:, n, :], inv_tot[n][:], None, ALU.mult)
+            nc.vector.reciprocal(factors[n][:], divisors[n][:])
             nc.vector.scalar_tensor_tensor(term_h[n][:], q[n][:], factors[n][:, 0:1], h_tiles[n][:],
                                            ALU.mult, ALU.mult, accum_out=neg_tx_s[n][:])
             nc.scalar.activation(s_factor[n][:], neg_tx_s[n][:], ACT.Copy, scale=factors[n][:, 1:2])
@@ -214,10 +223,6 @@ def tile_attend_grouter_x_pl_kernel(tc, xT, W, dg, lb, ce, tx, offs, out_0, out_
         terms(1)
         turn(0)
         softmax(3)
-        w_e_codes = sb("w_e_codes", [P, D], U32, tag="scaled_t")
-        w_e_scales = sb("w_e_scales", [P, D], U8)
-        nc.vector.quantize_mx(out=w_e_codes[:].bitcast(E4M3X4), scales=w_e_scales[:],
-                              in_=wt_bf[:].rearrange("p d t -> p (d t)"))
         terms(2)
         turn(1)
         quantise_g(0)
@@ -250,9 +255,6 @@ def tile_attend_grouter_x_pl_kernel(tc, xT, W, dg, lb, ce, tx, offs, out_0, out_
             return slice(c * CHUNK, (c + 1) * CHUNK)
 
         for j in range(LANES):
-            if j >= 2:
-                for c in range(CHUNKS):
-                    nc.vector.memset(planes[j][:, chunk(c)].bitcast(I32), 0)
             if j == 0:
                 nc.vector.tensor_copy(planes[j][:].indirect(half_offsets[1]), dx[j][:, HALF:SLOTS])
             else:

@@ -71,13 +71,13 @@ def tile_attend_grouter_x_pl_kernel(tc, xT, W, dg, lb, ce, tx, offs, out_0, out_
 
         ce_lanes = sb("ce_lanes", [P, P], F32)
         tx_window = sb("tx_window", [P, TOKENS], F32)
-        nc.vector.memset(ce_lanes[:], 0.0)
-        nc.vector.memset(tx_window[:].bitcast(I32), 0)
+        nc.vector.memset(ce_lanes[0:P - LANES, :], 0.0)
+        nc.vector.memset(tx_window[0:P - 1, :].bitcast(I32), 0)
+        nc.sync.dma_start(tx_window[P - 1:P, :], tx[0:1, :])
+        nc.sync.dma_start(ce_lanes[P - LANES:P, :].rearrange("t (b r) -> t b r", r=RUN),
+                          ce[0, :].rearrange("(b t r) -> t b r", t=LANES, r=RUN))
         w_raw = sb("w_raw", [P, LANES, E], F32)
         nc.sync.dma_start(w_raw[:], W.rearrange("(p j) e -> p j e", j=LANES))
-        nc.sync.dma_start(ce_lanes[0:LANES, :].rearrange("t (b r) -> t b r", r=RUN),
-                          ce[0, :].rearrange("(b t r) -> t b r", t=LANES, r=RUN))
-        nc.sync.dma_start(tx_window[0:1, :], tx[0:1, :])
         x_rows = xT.rearrange("(p j) x -> j p x", j=LANES)
         x_raw = [sb("x_raw%d" % j, [P, TOKENS], F32) for j in range(LANES)]
         for j in range(LANES):
@@ -91,11 +91,7 @@ def tile_attend_grouter_x_pl_kernel(tc, xT, W, dg, lb, ce, tx, offs, out_0, out_
 
         g_codes = sb("g_codes", [P, HALF + SLOTS], U32)
         g_scales = sb("g_scales", [P, HALF + SLOTS], U8)
-        nc.vector.memset(g_codes[:, 0:HALF], 0)
-        nc.vector.memset(g_scales[:, 0:HALF], 0)
         windows = [sb("window%d" % j, [P, TOKENS], F32) for j in range(WINDOWS)]
-        for window in windows:
-            nc.vector.memset(window[:].bitcast(I32), 0)
         planes = [windows[j % WINDOWS] for j in range(LANES)]
 
         w_bf = sb("w_bf", [P, E, LANES], BF16)
@@ -105,25 +101,23 @@ def tile_attend_grouter_x_pl_kernel(tc, xT, W, dg, lb, ce, tx, offs, out_0, out_
         nc.tensor.transpose(banks[2][:, 0:P], ce_lanes[:], ident[:])
         ce_col = sb("ce_col", [P, LANES], F32)
         neg_ce = sb("neg_ce", [P, 1, LANES], F32)
-        nc.scalar.copy(ce_col[:], banks[2][:, 0:LANES])
-        nc.scalar.activation(neg_ce[:, 0, :], banks[2][:, 0:LANES], ACT.Copy, scale=-1.0)
-        ce_rows = sb("ce_rows", [P, E], F32)
-        for t in range(LANES):
-            nc.tensor.transpose(banks[4][:, block(t)], ce_col[:, t:t + 1].to_broadcast([P, P]), ident[:])
-        nc.scalar.copy(ce_rows[:], banks[4][:])
+        nc.scalar.copy(ce_col[:], banks[2][:, P - LANES:P])
+        nc.scalar.activation(neg_ce[:, 0, :], banks[2][:, P - LANES:P], ACT.Copy, scale=-1.0)
         tx_listed = sb("tx_listed", [P, SLOTS], F32)
         nc.vector.tensor_copy(tx_listed[:], tx_window[:].indirect(offsets[:]))
+        nc.vector.memset(g_codes[:, 0:HALF], 0)
+        nc.vector.memset(g_scales[:, 0:HALF], 0)
+        for window in windows:
+            nc.vector.memset(window[:].bitcast(I32), 0)
         for n in range(SLOT_TILES):
             nc.tensor.transpose(banks[3][:, block(n)], tx_listed[:, block(n)], ident[:])
-        nc.scalar.activation(token_factors[:, :, 0], banks[3][:, 0:BANK:P], ACT.Copy, scale=-1.0)
+        nc.scalar.activation(token_factors[:, :, 0], banks[3][:, P - 1:BANK:P], ACT.Copy, scale=-1.0)
         token_inverses = sb("token_inverses", [P, SLOT_TILES, 2], F32)
         nc.vector.reciprocal(token_inverses[:], token_factors[:])
 
         x_bf = sb("x_bf", [P, SLOTS, LANES], BF16)
-        x_pair = sb("x_pair", [P, 2, SLOTS], BF16)
         for j in range(2):
-            nc.vector.tensor_copy(x_pair[:, j, :], x_raw[j][:].indirect(offsets[:]))
-        nc.scalar.copy(x_bf[:, :, 0:2], x_pair[:].rearrange("p j i -> p i j"))
+            nc.vector.tensor_copy(x_bf[:, :, j], x_raw[j][:].indirect(offsets[:]))
 
         w_words = w_bf[:].rearrange("p e j -> p (e j)").bitcast(F32)
         wt_bf = sb("wt_bf", [P, D, LANES], BF16)
@@ -145,34 +139,34 @@ def tile_attend_grouter_x_pl_kernel(tc, xT, W, dg, lb, ce, tx, offs, out_0, out_
 
         x_codes = sb("x_codes", [P, SLOTS], U32)
         x_scales = sb("x_scales", [P, SLOTS], U8)
-        scaled_t = sb("scaled_t", [P, LANES, HALF], F32)
+        scaled_t = [sb("scaled_t%d" % half, [P, LANES, HALF], F32) for half in range(2)]
         for half in range(2):
             cols = slice(half * HALF, (half + 1) * HALF)
             nc.vector.tensor_copy(x_bf[:, cols, LANES - 1], x_raw[LANES - 1][:].indirect(half_offsets[half]))
             nc.vector.quantize_mx(out=x_codes[:, cols].bitcast(E4M3X4), scales=x_scales[:, cols],
                                   in_=x_bf[:, cols, :].rearrange("p i j -> p (i j)"))
-        for n in range(2):
-            nc.tensor.matmul_mx(out=banks[n][:], lhsT=x_codes[:, block(n)].bitcast(E4M3X4),
-                                lhsT_scale=x_scales[:, block(n)],
-                                rhs=w_d_codes[:].bitcast(E4M3X4), rhs_scale=w_d_scales[:], start=True, stop=True)
-        sums = [banks[2 + t // 2][:, (t % 2) * HALF:(t % 2 + 1) * HALF] for t in range(LANES)]
-        for t in range(LANES):
-            nc.tensor.matmul_mx(out=sums[t], lhsT=w_d_codes[:, block(t)].bitcast(E4M3X4),
-                                lhsT_scale=w_d_scales[:, block(t)],
-                                rhs=x_codes[:, HALF:SLOTS].bitcast(E4M3X4), rhs_scale=x_scales[:, HALF:SLOTS],
-                                start=True, stop=True)
-        for t in range(LANES):
-            nc.scalar.activation(scaled_t[:, t, :], sums[t], ACT.Copy, scale=ce_col[:, t:t + 1])
+        for half in range(2):
+            cols = slice(half * HALF, (half + 1) * HALF)
+            sums = [banks[2 * half + t // 2][:, (t % 2) * HALF:(t % 2 + 1) * HALF] for t in range(LANES)]
+            for t in range(LANES):
+                nc.tensor.matmul_mx(out=sums[t], lhsT=w_d_codes[:, block(t)].bitcast(E4M3X4),
+                                    lhsT_scale=w_d_scales[:, block(t)],
+                                    rhs=x_codes[:, cols].bitcast(E4M3X4), rhs_scale=x_scales[:, cols],
+                                    start=True, stop=True)
+            for t in range(LANES):
+                nc.scalar.activation(scaled_t[half][:, t, :], sums[t], ACT.Copy, scale=ce_col[:, t:t + 1])
 
-        h_tiles = [sb("h%d" % n, [P, E], F32) for n in range(SLOT_TILES)]
+        h_all = sb("h_all", [P, SLOT_TILES, E], F32, tag="x_raw%d" % (LANES - 1))
+        h_tiles = [h_all[:, n, :] for n in range(SLOT_TILES)]
         for n in range(SLOT_TILES):
-            nc.vector.tensor_tensor(dealt(h_tiles[n][:]), natural(dg_raw[n // 2][:, n % 2, :]),
+            nc.vector.tensor_tensor(dealt(h_tiles[n]), natural(dg_raw[n // 2][:, n % 2, :]),
                                     natural(lb_rows[:]), ALU.add)
 
         def per_tile(name, width):
             return [sb("%s%d" % (name, n), [P, width], F32) for n in range(SLOT_TILES)]
 
-        neg_z, q, term_h, term_s = [per_tile(name, E) for name in ("neg_z", "q", "term_h", "term_s")]
+        q, term_h, term_s = [per_tile(name, E) for name in ("q", "term_h", "term_s")]
+        neg_z = [sb("neg_z%d" % n, [P, E], F32, tag="dg_raw1" if n == 0 else "") for n in range(SLOT_TILES)]
         neg_m, tot, neg_tx_s, s_factor = [
             per_tile(name, 1) for name in ("neg_m", "tot", "neg_tx_s", "s_factor")]
         factors = per_tile("factors", 2)
@@ -181,21 +175,17 @@ def tile_attend_grouter_x_pl_kernel(tc, xT, W, dg, lb, ce, tx, offs, out_0, out_
 
         def softmax(n):
             neg_tx = token_factors[:, n, 0:1]
-            if n < 2:
-                nc.vector.scalar_tensor_tensor(neg_z[n][:], banks[n][:], neg_tx, ce_rows[:], ALU.mult, ALU.mult)
-                nc.vector.tensor_reduce(neg_m[n][:], neg_z[n][:], mybir.AxisListType.X, ALU.min)
-            else:
-                bank = banks[2 + n]
-                for t in range(LANES):
-                    nc.tensor.transpose(bank[:, block(t)], scaled_t[:, t, block(n % 2)], ident[:])
-                nc.vector.tensor_scalar(neg_z[n][:], bank[:], neg_tx, None, ALU.mult, ALU.min,
-                                        accum_out=neg_m[n][:])
+            bank = banks[4 + n]
+            for t in range(LANES):
+                nc.tensor.transpose(bank[:, block(t)], scaled_t[n // 2][:, t, block(n % 2)], ident[:])
+            nc.vector.tensor_scalar(neg_z[n][:], bank[:], neg_tx, None, ALU.mult, ALU.min,
+                                    accum_out=neg_m[n][:])
             nc.scalar.activation(q[n][:], neg_z[n][:], ACT.Exp, bias=neg_m[n][:], scale=-1.0, accum_out=tot[n][:])
             nc.scalar.activation(divisors[n][:], token_inverses[:, n, :], ACT.Copy, scale=tot[n][:])
 
         def terms(n):
             nc.vector.reciprocal(factors[n][:], divisors[n][:])
-            nc.vector.scalar_tensor_tensor(term_h[n][:], q[n][:], factors[n][:, 0:1], h_tiles[n][:],
+            nc.vector.scalar_tensor_tensor(term_h[n][:], q[n][:], factors[n][:, 0:1], h_tiles[n],
                                            ALU.mult, ALU.mult, accum_out=neg_tx_s[n][:])
             nc.scalar.activation(s_factor[n][:], neg_tx_s[n][:], ACT.Copy, scale=factors[n][:, 1:2])
             nc.scalar.activation(term_s[n][:], q[n][:], ACT.Copy, scale=s_factor[n][:])

@@ -100,9 +100,9 @@ def tile_attend_grouter_x_pl_kernel(tc, xT, W, dg, lb, ce, tx, offs, out_0, out_
 
         nc.tensor.transpose(banks[2][:, 0:P], ce_lanes[:], ident[:])
         ce_col = sb("ce_col", [P, LANES], F32)
-        neg_ce = sb("neg_ce", [P, 1, LANES], F32)
+        neg_ce = sb("neg_ce", [P, 1, LANES, 1], F32)
         nc.scalar.copy(ce_col[:], banks[2][:, P - LANES:P])
-        nc.scalar.activation(neg_ce[:, 0, :], banks[2][:, P - LANES:P], ACT.Copy, scale=-1.0)
+        nc.scalar.activation(neg_ce[:, 0, :, 0], banks[2][:, P - LANES:P], ACT.Copy, scale=-1.0)
         tx_listed = sb("tx_listed", [P, SLOTS], F32)
         nc.vector.tensor_copy(tx_listed[:], tx_window[:].indirect(offsets[:]))
         nc.vector.memset(g_codes[:, 0:HALF], 0)
@@ -124,18 +124,14 @@ def tile_attend_grouter_x_pl_kernel(tc, xT, W, dg, lb, ce, tx, offs, out_0, out_
         for u in range(2):
             for t in range(LANES):
                 nc.tensor.transpose(banks[6 + u][:, block(t)], w_words[:, 2 * P * t + u:2 * P * (t + 1):2], ident[:])
-            nc.scalar.copy(wt_bf[:, 2 * P * u:2 * P * (u + 1), :].rearrange("p (k v) t -> p k v t", k=2),
-                           banks[6 + u][:].bitcast(BF16).rearrange("p (t v k) -> p k v t", t=LANES, k=2))
+            nc.scalar.copy(wt_bf[:, 2 * P * u:2 * P * (u + 1), :].rearrange("p (k v w) t -> p v t w k", k=2, w=2),
+                           banks[6 + u][:].bitcast(BF16).rearrange("p (t v w k) -> p v t w k", t=LANES, w=2, k=2))
 
         nc.vector.tensor_copy(x_bf[:, :, 2], x_raw[2][:].indirect(offsets[:]))
         w_d_codes = sb("w_d_codes", [P, E], U32)
         w_d_scales = sb("w_d_scales", [P, E], U8)
         nc.vector.quantize_mx(out=w_d_codes[:].bitcast(E4M3X4), scales=w_d_scales[:],
                               in_=w_bf[:].rearrange("p e j -> p (e j)"))
-        w_e_codes = sb("w_e_codes", [P, D], U32)
-        w_e_scales = sb("w_e_scales", [P, D], U8)
-        nc.vector.quantize_mx(out=w_e_codes[:].bitcast(E4M3X4), scales=w_e_scales[:],
-                              in_=wt_bf[:].rearrange("p d t -> p (d t)"))
 
         x_codes = sb("x_codes", [P, SLOTS], U32)
         x_scales = sb("x_scales", [P, SLOTS], U8)
@@ -156,7 +152,11 @@ def tile_attend_grouter_x_pl_kernel(tc, xT, W, dg, lb, ce, tx, offs, out_0, out_
             for t in range(LANES):
                 nc.scalar.activation(scaled_t[half][:, t, :], sums[t], ACT.Copy, scale=ce_col[:, t:t + 1])
 
-        h_all = sb("h_all", [P, SLOT_TILES, E], F32, tag="x_raw%d" % (LANES - 1))
+        w_e_codes = sb("w_e_codes", [P, D], U32, tag="x_raw%d" % (LANES - 1))
+        w_e_scales = sb("w_e_scales", [P, D], U8)
+        nc.vector.quantize_mx(out=w_e_codes[:].bitcast(E4M3X4), scales=w_e_scales[:],
+                              in_=wt_bf[:].rearrange("p d t -> p (d t)"))
+        h_all = sb("h_all", [P, SLOT_TILES, E], F32)
         h_tiles = [h_all[:, n, :] for n in range(SLOT_TILES)]
         for n in range(SLOT_TILES):
             nc.vector.tensor_tensor(dealt(h_tiles[n]), natural(dg_raw[n // 2][:, n % 2, :]),
@@ -198,8 +198,9 @@ def tile_attend_grouter_x_pl_kernel(tc, xT, W, dg, lb, ce, tx, offs, out_0, out_
             for t in range(LANES):
                 nc.tensor.matmul(bank[:, block(t)], term_s[n][:, block(t)], ident[:],
                                  start=False, stop=(t == LANES - 1), is_transpose=True)
-            nc.vector.tensor_tensor(g_bf[n // 2][:, block(n % 2), :], bank[:].rearrange("p (t i) -> p i t", t=LANES),
-                                    neg_ce[:].to_broadcast([P, P, LANES]), ALU.mult)
+            nc.vector.tensor_tensor(g_bf[n // 2][:, block(n % 2), :].rearrange("p (i w) t -> p i t w", w=2),
+                                    bank[:].rearrange("p (t i w) -> p i t w", t=LANES, w=2),
+                                    neg_ce[:].to_broadcast([P, P // 2, LANES, 2]), ALU.mult)
 
         def quantise_g(half):
             cols = slice((half + 1) * HALF, (half + 2) * HALF)

@@ -30,6 +30,7 @@ CHUNKS = TOKENS // CHUNK
 VECTOR_CHUNK = CHUNKS - 1
 SCALAR_CHUNK = CHUNKS - 2
 WINDOWS = 3
+PLANE_ORDER = (2, 0, 1, 3)
 QUADRANTS = 4
 
 FLOPS = 2 * 2 * D * E * SLOTS
@@ -92,7 +93,7 @@ def tile_attend_grouter_x_pl_kernel(tc, xT, W, dg, lb, ce, tx, offs, out_0, out_
         g_codes = sb("g_codes", [P, HALF + SLOTS], U32)
         g_scales = sb("g_scales", [P, HALF + SLOTS], U8)
         windows = [sb("window%d" % j, [P, TOKENS], F32) for j in range(WINDOWS)]
-        planes = [windows[j % WINDOWS] for j in range(LANES)]
+        planes = {j: windows[step % WINDOWS] for step, j in enumerate(PLANE_ORDER)}
 
         w_bf = sb("w_bf", [P, E, LANES], BF16)
         nc.scalar.copy(w_bf[:].rearrange("p (t b r) j -> p t b r j", t=LANES, r=RUN),
@@ -228,16 +229,17 @@ def tile_attend_grouter_x_pl_kernel(tc, xT, W, dg, lb, ce, tx, offs, out_0, out_
                                 rhs=g_codes[:, cols].bitcast(E5M2X4), rhs_scale=g_scales[:, cols],
                                 start=True, stop=True)
 
-        dx_pass(0, banks[7], 0)
+        early = PLANE_ORDER[0]
+        dx_pass(early, banks[7], 0)
         dx_early = sb("dx_early", [P, HALF], F32)
         nc.scalar.copy(dx_early[:], banks[7][:, HALF:SLOTS])
         quantise_g(1)
-        nc.vector.tensor_copy(planes[0][:].indirect(half_offsets[0]), dx_early[:])
+        nc.vector.tensor_copy(planes[early][:].indirect(half_offsets[0]), dx_early[:])
         dx = [sb("dx%d" % j, [P, SLOTS], F32) for j in range(LANES)]
-        for j in range(LANES):
-            first = HALF if j == 0 else 0
-            dx_pass(j, banks[4 + j], HALF)
-            nc.scalar.copy(dx[j][:, first:SLOTS], banks[4 + j][:, first:SLOTS])
+        for step, j in enumerate(PLANE_ORDER):
+            first = HALF if j == early else 0
+            dx_pass(j, banks[4 + step], HALF)
+            nc.scalar.copy(dx[j][:, first:SLOTS], banks[4 + step][:, first:SLOTS])
 
         out_rows = out_0.rearrange("(p j) x -> j p x", j=LANES)
         pairs = [sb("pairs%d" % c, [P, 2, CHUNK, 2], BF16) for c in range(CHUNKS)]
@@ -245,17 +247,16 @@ def tile_attend_grouter_x_pl_kernel(tc, xT, W, dg, lb, ce, tx, offs, out_0, out_
         def chunk(c):
             return slice(c * CHUNK, (c + 1) * CHUNK)
 
-        for j in range(LANES):
-            if j == 0:
+        for j in PLANE_ORDER:
+            if j == early:
                 nc.vector.tensor_copy(planes[j][:].indirect(half_offsets[1]), dx[j][:, HALF:SLOTS])
             else:
                 nc.vector.tensor_copy(planes[j][:].indirect(offsets[:]), dx[j][:])
             nc.sync.dma_start(out_rows[j], planes[j][:])
             for c in range(CHUNKS):
-                if j < 2 or c != VECTOR_CHUNK:
+                if j != PLANE_ORDER[-1] or c != VECTOR_CHUNK:
                     nc.scalar.copy(pairs[c][:, j // 2, :, j % 2], planes[j][:, chunk(c)])
-        for j in (2, 3):
-            nc.vector.tensor_copy(pairs[VECTOR_CHUNK][:, 1, :, j % 2], planes[j][:, chunk(VECTOR_CHUNK)])
+        nc.vector.tensor_copy(pairs[VECTOR_CHUNK][:, 1, :, 1], planes[LANES - 1][:, chunk(VECTOR_CHUNK)])
 
         y_bf = [sb("y_bf%d" % c, [P, CHUNK * LANES], BF16) for c in range(CHUNKS)]
         y_scales = sb("y_scales", [P, TOKENS], U8)

@@ -27,8 +27,7 @@ SLOT_TILES = SLOTS // P
 LIST_ROWS = 16
 CHUNK = 512
 CHUNKS = TOKENS // CHUNK
-VECTOR_CHUNK = CHUNKS - 1
-SCALAR_CHUNK = CHUNKS - 2
+VECTOR_CHUNKS = CHUNKS // 2
 WINDOWS = 3
 PLANE_ORDER = (2, 0, 1, 3)
 QUADRANTS = 4
@@ -92,8 +91,7 @@ def tile_attend_grouter_x_pl_kernel(tc, xT, W, dg, lb, ce, tx, offs, out_0, out_
 
         g_codes = sb("g_codes", [P, HALF + SLOTS], U32)
         g_scales = sb("g_scales", [P, HALF + SLOTS], U8)
-        windows = [sb("window%d" % j, [P, TOKENS], F32) for j in range(WINDOWS)]
-        planes = {j: windows[step % WINDOWS] for step, j in enumerate(PLANE_ORDER)}
+        windows = [sb("window%d" % j, [P, TOKENS], F32) for j in range(WINDOWS - 1)]
 
         w_bf = sb("w_bf", [P, E, LANES], BF16)
         nc.scalar.copy(w_bf[:].rearrange("p (t b r) j -> p t b r j", t=LANES, r=RUN),
@@ -117,11 +115,13 @@ def tile_attend_grouter_x_pl_kernel(tc, xT, W, dg, lb, ce, tx, offs, out_0, out_
         nc.vector.reciprocal(token_inverses[:], token_factors[:])
 
         x_bf = sb("x_bf", [P, SLOTS, LANES], BF16)
+        x_pair = sb("x_pair", [P, 2, SLOTS], BF16)
         for j in range(2):
-            nc.vector.tensor_copy(x_bf[:, :, j], x_raw[j][:].indirect(offsets[:]))
+            nc.vector.tensor_copy(x_pair[:, j, :], x_raw[j][:].indirect(offsets[:]))
+        nc.scalar.copy(x_bf[:, :, 0:2], x_pair[:].rearrange("p j i -> p i j"))
 
         w_words = w_bf[:].rearrange("p e j -> p (e j)").bitcast(F32)
-        wt_bf = sb("wt_bf", [P, D, LANES], BF16)
+        wt_bf = sb("wt_bf", [P, D, LANES], BF16, tag="x_pair")
         for u in range(2):
             for t in range(LANES):
                 nc.tensor.transpose(banks[6 + u][:, block(t)], w_words[:, 2 * P * t + u:2 * P * (t + 1):2], ident[:])
@@ -157,11 +157,17 @@ def tile_attend_grouter_x_pl_kernel(tc, xT, W, dg, lb, ce, tx, offs, out_0, out_
         w_e_scales = sb("w_e_scales", [P, D], U8)
         nc.vector.quantize_mx(out=w_e_codes[:].bitcast(E4M3X4), scales=w_e_scales[:],
                               in_=wt_bf[:].rearrange("p d t -> p (d t)"))
+
         h_all = sb("h_all", [P, SLOT_TILES, E], F32)
         h_tiles = [h_all[:, n, :] for n in range(SLOT_TILES)]
         for n in range(SLOT_TILES):
             nc.vector.tensor_tensor(dealt(h_tiles[n]), natural(dg_raw[n // 2][:, n % 2, :]),
                                     natural(lb_rows[:]), ALU.add)
+
+        windows.append(sb("window_last", [P, TOKENS], F32, tag="x_raw1"))
+        for c in range(CHUNKS):
+            nc.vector.memset(windows[-1][:, c * CHUNK:(c + 1) * CHUNK].bitcast(I32), 0)
+        planes = {j: windows[step % WINDOWS] for step, j in enumerate(PLANE_ORDER)}
 
         def per_tile(name, width):
             return [sb("%s%d" % (name, n), [P, width], F32) for n in range(SLOT_TILES)]
@@ -247,23 +253,23 @@ def tile_attend_grouter_x_pl_kernel(tc, xT, W, dg, lb, ce, tx, offs, out_0, out_
         def chunk(c):
             return slice(c * CHUNK, (c + 1) * CHUNK)
 
+        last = PLANE_ORDER[-1]
         for j in PLANE_ORDER:
             if j == early:
                 nc.vector.tensor_copy(planes[j][:].indirect(half_offsets[1]), dx[j][:, HALF:SLOTS])
             else:
                 nc.vector.tensor_copy(planes[j][:].indirect(offsets[:]), dx[j][:])
             nc.sync.dma_start(out_rows[j], planes[j][:])
-            for c in range(CHUNKS):
-                if j != PLANE_ORDER[-1] or c != VECTOR_CHUNK:
+            if j != last:
+                for c in range(CHUNKS):
                     nc.scalar.copy(pairs[c][:, j // 2, :, j % 2], planes[j][:, chunk(c)])
-        nc.vector.tensor_copy(pairs[VECTOR_CHUNK][:, 1, :, 1], planes[LANES - 1][:, chunk(VECTOR_CHUNK)])
 
         y_bf = [sb("y_bf%d" % c, [P, CHUNK * LANES], BF16) for c in range(CHUNKS)]
         y_scales = sb("y_scales", [P, TOKENS], U8)
         words_out = out_1[0].rearrange("p x j -> p (x j)").bitcast(I32)
 
         def merge(c):
-            copy_words = nc.scalar.copy if c == SCALAR_CHUNK else nc.vector.tensor_copy
+            copy_words = nc.scalar.copy if c >= VECTOR_CHUNKS else nc.vector.tensor_copy
             copy_words(y_bf[c][:].bitcast(F32).rearrange("p (x u) -> p x u", u=2),
                        pairs[c][:].rearrange("p u x k -> p (u x k)").bitcast(F32).rearrange("p (u x) -> p x u", u=2))
 
@@ -272,12 +278,14 @@ def tile_attend_grouter_x_pl_kernel(tc, xT, W, dg, lb, ce, tx, offs, out_0, out_
             nc.vector.quantize_mx(out=y_codes[:].bitcast(E4M3X4), scales=y_scales[:, chunk(c)], in_=y_bf[c][:])
             nc.sync.dma_start(words_out[:, chunk(c)], y_codes[:].bitcast(I32))
 
-        merge(VECTOR_CHUNK)
-        merge(0)
-        quantise_y(VECTOR_CHUNK)
-        merge(1)
-        merge(SCALAR_CHUNK)
-        for c in range(VECTOR_CHUNK):
+        for c in range(VECTOR_CHUNKS):
+            nc.vector.tensor_copy(pairs[c][:, last // 2, :, last % 2], planes[last][:, chunk(c)])
+        for c in range(VECTOR_CHUNKS):
+            merge(c)
+        for c in range(VECTOR_CHUNKS, CHUNKS):
+            nc.scalar.copy(pairs[c][:, last // 2, :, last % 2], planes[last][:, chunk(c)])
+            merge(c)
+        for c in range(CHUNKS):
             quantise_y(c)
         for quad in range(QUADRANTS):
             queue = nc.sync if quad % 2 == 0 else nc.scalar

@@ -261,8 +261,11 @@ def tile_attend_grouter_x_pl_kernel(tc, xT, W, dg, lb, ce, tx, offs, out_0, out_
                 nc.vector.tensor_copy(planes[j][:].indirect(offsets[:]), dx[j][:])
             nc.sync.dma_start(out_rows[j], planes[j][:])
             if j != last:
-                for c in range(CHUNKS):
+                for c in range(VECTOR_CHUNKS):
                     nc.scalar.copy(pairs[c][:, j // 2, :, j % 2], planes[j][:, chunk(c)])
+                for c in range(VECTOR_CHUNKS, CHUNKS):
+                    nc.gpsimd.tensor_scalar(pairs[c][:, j // 2, :, j % 2], planes[j][:, chunk(c)],
+                                            1.0, 0.0, ALU.mult, ALU.add)
 
         y_bf = [sb("y_bf%d" % c, [P, CHUNK * LANES], BF16) for c in range(CHUNKS)]
         y_scales = sb("y_scales", [P, TOKENS], U8)

@@ -30,6 +30,7 @@ CHUNKS = TOKENS // CHUNK
 VECTOR_CHUNKS = CHUNKS // 2
 WINDOWS = 3
 PLANE_ORDER = (2, 0, 1, 3)
+EARLY = 2
 QUADRANTS = 4
 
 FLOPS = 2 * 2 * D * E * SLOTS
@@ -72,7 +73,7 @@ def tile_attend_grouter_x_pl_kernel(tc, xT, W, dg, lb, ce, tx, offs, out_0, out_
         ce_lanes = sb("ce_lanes", [P, P], F32)
         tx_window = sb("tx_window", [P, TOKENS], F32)
         nc.vector.memset(ce_lanes[0:P - LANES, :], 0.0)
-        nc.vector.memset(tx_window[0:P - 1, :].bitcast(I32), 0)
+        nc.gpsimd.memset(tx_window[0:P - 1, :].bitcast(I32), 0)
         nc.sync.dma_start(tx_window[P - 1:P, :], tx[0:1, :])
         nc.sync.dma_start(ce_lanes[P - LANES:P, :].rearrange("t (b r) -> t b r", r=RUN),
                           ce[0, :].rearrange("(b t r) -> t b r", t=LANES, r=RUN))
@@ -91,7 +92,7 @@ def tile_attend_grouter_x_pl_kernel(tc, xT, W, dg, lb, ce, tx, offs, out_0, out_
 
         g_codes = sb("g_codes", [P, HALF + SLOTS], U32)
         g_scales = sb("g_scales", [P, HALF + SLOTS], U8)
-        windows = [sb("window%d" % j, [P, TOKENS], F32) for j in range(WINDOWS - 1)]
+        windows = [sb("window%d" % j, [P, TOKENS], F32) for j in range(WINDOWS)]
 
         w_bf = sb("w_bf", [P, E, LANES], BF16)
         nc.scalar.copy(w_bf[:].rearrange("p (t b r) j -> p t b r j", t=LANES, r=RUN),
@@ -107,7 +108,7 @@ def tile_attend_grouter_x_pl_kernel(tc, xT, W, dg, lb, ce, tx, offs, out_0, out_
         nc.vector.memset(g_codes[:, 0:HALF], 0)
         nc.vector.memset(g_scales[:, 0:HALF], 0)
         for window in windows:
-            nc.vector.memset(window[:].bitcast(I32), 0)
+            nc.gpsimd.memset(window[:].bitcast(I32), 0)
         for n in range(SLOT_TILES):
             nc.tensor.transpose(banks[3][:, block(n)], tx_listed[:, block(n)], ident[:])
         nc.scalar.activation(token_factors[:, :, 0], banks[3][:, P - 1:BANK:P], ACT.Copy, scale=-1.0)
@@ -115,13 +116,11 @@ def tile_attend_grouter_x_pl_kernel(tc, xT, W, dg, lb, ce, tx, offs, out_0, out_
         nc.vector.reciprocal(token_inverses[:], token_factors[:])
 
         x_bf = sb("x_bf", [P, SLOTS, LANES], BF16)
-        x_pair = sb("x_pair", [P, 2, SLOTS], BF16)
         for j in range(2):
-            nc.vector.tensor_copy(x_pair[:, j, :], x_raw[j][:].indirect(offsets[:]))
-        nc.scalar.copy(x_bf[:, :, 0:2], x_pair[:].rearrange("p j i -> p i j"))
+            nc.vector.tensor_copy(x_bf[:, :, j], x_raw[j][:].indirect(offsets[:]))
 
         w_words = w_bf[:].rearrange("p e j -> p (e j)").bitcast(F32)
-        wt_bf = sb("wt_bf", [P, D, LANES], BF16, tag="x_pair")
+        wt_bf = sb("wt_bf", [P, D, LANES], BF16)
         for u in range(2):
             for t in range(LANES):
                 nc.tensor.transpose(banks[6 + u][:, block(t)], w_words[:, 2 * P * t + u:2 * P * (t + 1):2], ident[:])
@@ -153,27 +152,24 @@ def tile_attend_grouter_x_pl_kernel(tc, xT, W, dg, lb, ce, tx, offs, out_0, out_
             for t in range(LANES):
                 nc.scalar.activation(scaled_t[half][:, t, :], sums[t], ACT.Copy, scale=ce_col[:, t:t + 1])
 
-        w_e_codes = sb("w_e_codes", [P, D], U32, tag="x_raw%d" % (LANES - 1))
+        w_e_codes = sb("w_e_codes", [P, D], U32)
         w_e_scales = sb("w_e_scales", [P, D], U8)
         nc.vector.quantize_mx(out=w_e_codes[:].bitcast(E4M3X4), scales=w_e_scales[:],
                               in_=wt_bf[:].rearrange("p d t -> p (d t)"))
 
-        h_all = sb("h_all", [P, SLOT_TILES, E], F32)
-        h_tiles = [h_all[:, n, :] for n in range(SLOT_TILES)]
+        h_tiles = [sb("h%d" % n, [P, E], F32, tag="dg_raw0" if n == 2 else "")[:] for n in range(SLOT_TILES)]
         for n in range(SLOT_TILES):
-            nc.vector.tensor_tensor(dealt(h_tiles[n]), natural(dg_raw[n // 2][:, n % 2, :]),
-                                    natural(lb_rows[:]), ALU.add)
+            engine = nc.vector if n < 2 else nc.gpsimd
+            engine.tensor_tensor(dealt(h_tiles[n]), natural(dg_raw[n // 2][:, n % 2, :]),
+                                 natural(lb_rows[:]), ALU.add)
 
-        windows.append(sb("window_last", [P, TOKENS], F32, tag="x_raw1"))
-        for c in range(CHUNKS):
-            nc.vector.memset(windows[-1][:, c * CHUNK:(c + 1) * CHUNK].bitcast(I32), 0)
         planes = {j: windows[step % WINDOWS] for step, j in enumerate(PLANE_ORDER)}
 
         def per_tile(name, width):
             return [sb("%s%d" % (name, n), [P, width], F32) for n in range(SLOT_TILES)]
 
         q, term_h, term_s = [per_tile(name, E) for name in ("q", "term_h", "term_s")]
-        neg_z = [sb("neg_z%d" % n, [P, E], F32, tag="dg_raw1" if n == 0 else "") for n in range(SLOT_TILES)]
+        neg_z = per_tile("neg_z", E)
         neg_m, tot, neg_tx_s, s_factor = [
             per_tile(name, 1) for name in ("neg_m", "tot", "neg_tx_s", "s_factor")]
         factors = per_tile("factors", 2)
@@ -235,15 +231,17 @@ def tile_attend_grouter_x_pl_kernel(tc, xT, W, dg, lb, ce, tx, offs, out_0, out_
                                 rhs=g_codes[:, cols].bitcast(E5M2X4), rhs_scale=g_scales[:, cols],
                                 start=True, stop=True)
 
-        early = PLANE_ORDER[0]
-        dx_pass(early, banks[7], 0)
-        dx_early = sb("dx_early", [P, HALF], F32)
-        nc.scalar.copy(dx_early[:], banks[7][:, HALF:SLOTS])
+        early = PLANE_ORDER[0:EARLY]
+        dx_early = [sb("dx_early%d" % k, [P, HALF], F32) for k in range(EARLY)]
+        for k, j in enumerate(early):
+            dx_pass(j, banks[6 + k], 0)
+            nc.scalar.copy(dx_early[k][:], banks[6 + k][:, HALF:SLOTS])
+        nc.vector.tensor_copy(planes[early[0]][:].indirect(half_offsets[0]), dx_early[0][:])
         quantise_g(1)
-        nc.vector.tensor_copy(planes[early][:].indirect(half_offsets[0]), dx_early[:])
+        nc.vector.tensor_copy(planes[early[1]][:].indirect(half_offsets[0]), dx_early[1][:])
         dx = [sb("dx%d" % j, [P, SLOTS], F32) for j in range(LANES)]
         for step, j in enumerate(PLANE_ORDER):
-            first = HALF if j == early else 0
+            first = HALF if j in early else 0
             dx_pass(j, banks[4 + step], HALF)
             nc.scalar.copy(dx[j][:, first:SLOTS], banks[4 + step][:, first:SLOTS])
 
@@ -255,7 +253,7 @@ def tile_attend_grouter_x_pl_kernel(tc, xT, W, dg, lb, ce, tx, offs, out_0, out_
 
         last = PLANE_ORDER[-1]
         for j in PLANE_ORDER:
-            if j == early:
+            if j in early:
                 nc.vector.tensor_copy(planes[j][:].indirect(half_offsets[1]), dx[j][:, HALF:SLOTS])
             else:
                 nc.vector.tensor_copy(planes[j][:].indirect(offsets[:]), dx[j][:])

@@ -58,6 +58,8 @@ def tile_attend_grouter_x_pl_kernel(tc, xT, W, dg, lb, ce, tx, offs, out_0, out_
 
         banks = [psum.tile([P, BANK], F32, name="bank%d" % b) for b in range(8)]
 
+        w_raw = sb("w_raw", [P, LANES, E], F32)
+        nc.sync.dma_start(w_raw[:], W.rearrange("(p j) e -> p j e", j=LANES))
         offsets = sb("offsets", [P, SLOTS // LIST_ROWS], U16)
         nc.sync.dma_start(offsets[:], offs)
         half_columns = HALF // LIST_ROWS
@@ -73,12 +75,10 @@ def tile_attend_grouter_x_pl_kernel(tc, xT, W, dg, lb, ce, tx, offs, out_0, out_
         ce_lanes = sb("ce_lanes", [P, P], F32)
         tx_window = sb("tx_window", [P, TOKENS], F32)
         nc.vector.memset(ce_lanes[0:P - LANES, :], 0.0)
-        nc.gpsimd.memset(tx_window[0:P - 1, :].bitcast(I32), 0)
+        nc.vector.memset(tx_window[0:P - 1, :].bitcast(I32), 0)
         nc.sync.dma_start(tx_window[P - 1:P, :], tx[0:1, :])
         nc.sync.dma_start(ce_lanes[P - LANES:P, :].rearrange("t (b r) -> t b r", r=RUN),
                           ce[0, :].rearrange("(b t r) -> t b r", t=LANES, r=RUN))
-        w_raw = sb("w_raw", [P, LANES, E], F32)
-        nc.sync.dma_start(w_raw[:], W.rearrange("(p j) e -> p j e", j=LANES))
         x_rows = xT.rearrange("(p j) x -> j p x", j=LANES)
         x_raw = [sb("x_raw%d" % j, [P, TOKENS], F32) for j in range(LANES)]
         for j in range(LANES):
@@ -108,7 +108,7 @@ def tile_attend_grouter_x_pl_kernel(tc, xT, W, dg, lb, ce, tx, offs, out_0, out_
         nc.vector.memset(g_codes[:, 0:HALF], 0)
         nc.vector.memset(g_scales[:, 0:HALF], 0)
         for window in windows:
-            nc.gpsimd.memset(window[:].bitcast(I32), 0)
+            nc.vector.memset(window[:].bitcast(I32), 0)
         for n in range(SLOT_TILES):
             nc.tensor.transpose(banks[3][:, block(n)], tx_listed[:, block(n)], ident[:])
         nc.scalar.activation(token_factors[:, :, 0], banks[3][:, P - 1:BANK:P], ACT.Copy, scale=-1.0)
@@ -157,10 +157,9 @@ def tile_attend_grouter_x_pl_kernel(tc, xT, W, dg, lb, ce, tx, offs, out_0, out_
         nc.vector.quantize_mx(out=w_e_codes[:].bitcast(E4M3X4), scales=w_e_scales[:],
                               in_=wt_bf[:].rearrange("p d t -> p (d t)"))
 
-        h_tiles = [sb("h%d" % n, [P, E], F32, tag="dg_raw0" if n == 2 else "")[:] for n in range(SLOT_TILES)]
+        h_tiles = [sb("h%d" % n, [P, E], F32)[:] for n in range(SLOT_TILES)]
         for n in range(SLOT_TILES):
-            engine = nc.vector if n < 2 else nc.gpsimd
-            engine.tensor_tensor(dealt(h_tiles[n]), natural(dg_raw[n // 2][:, n % 2, :]),
+            nc.vector.tensor_tensor(dealt(h_tiles[n]), natural(dg_raw[n // 2][:, n % 2, :]),
                                  natural(lb_rows[:]), ALU.add)
 
         planes = {j: windows[step % WINDOWS] for step, j in enumerate(PLANE_ORDER)}
@@ -169,7 +168,7 @@ def tile_attend_grouter_x_pl_kernel(tc, xT, W, dg, lb, ce, tx, offs, out_0, out_
             return [sb("%s%d" % (name, n), [P, width], F32) for n in range(SLOT_TILES)]
 
         q, term_h, term_s = [per_tile(name, E) for name in ("q", "term_h", "term_s")]
-        neg_z = per_tile("neg_z", E)
+        neg_z = [sb("neg_z%d" % n, [P, E], F32, tag="dg_raw1" if n == 0 else "") for n in range(SLOT_TILES)]
         neg_m, tot, neg_tx_s, s_factor = [
             per_tile(name, 1) for name in ("neg_m", "tot", "neg_tx_s", "s_factor")]
         factors = per_tile("factors", 2)

@@ -58,8 +58,6 @@ def tile_attend_grouter_x_pl_kernel(tc, xT, W, dg, lb, ce, tx, offs, out_0, out_
 
         banks = [psum.tile([P, BANK], F32, name="bank%d" % b) for b in range(8)]
 
-        w_raw = sb("w_raw", [P, LANES, E], F32)
-        nc.sync.dma_start(w_raw[:], W.rearrange("(p j) e -> p j e", j=LANES))
         offsets = sb("offsets", [P, SLOTS // LIST_ROWS], U16)
         nc.sync.dma_start(offsets[:], offs)
         half_columns = HALF // LIST_ROWS
@@ -74,11 +72,13 @@ def tile_attend_grouter_x_pl_kernel(tc, xT, W, dg, lb, ce, tx, offs, out_0, out_
 
         ce_lanes = sb("ce_lanes", [P, P], F32)
         tx_window = sb("tx_window", [P, TOKENS], F32)
-        nc.vector.memset(ce_lanes[0:P - LANES, :], 0.0)
+        nc.gpsimd.memset(ce_lanes[0:P - LANES, :], 0.0)
         nc.vector.memset(tx_window[0:P - 1, :].bitcast(I32), 0)
         nc.sync.dma_start(tx_window[P - 1:P, :], tx[0:1, :])
         nc.sync.dma_start(ce_lanes[P - LANES:P, :].rearrange("t (b r) -> t b r", r=RUN),
                           ce[0, :].rearrange("(b t r) -> t b r", t=LANES, r=RUN))
+        w_raw = sb("w_raw", [P, LANES, E], F32)
+        nc.sync.dma_start(w_raw[:], W.rearrange("(p j) e -> p j e", j=LANES))
         x_rows = xT.rearrange("(p j) x -> j p x", j=LANES)
         x_raw = [sb("x_raw%d" % j, [P, TOKENS], F32) for j in range(LANES)]
         for j in range(LANES):
@@ -105,10 +105,10 @@ def tile_attend_grouter_x_pl_kernel(tc, xT, W, dg, lb, ce, tx, offs, out_0, out_
         nc.scalar.activation(neg_ce[:, 0, :, 0], banks[2][:, P - LANES:P], ACT.Copy, scale=-1.0)
         tx_listed = sb("tx_listed", [P, SLOTS], F32)
         nc.vector.tensor_copy(tx_listed[:], tx_window[:].indirect(offsets[:]))
-        nc.vector.memset(g_codes[:, 0:HALF], 0)
-        nc.vector.memset(g_scales[:, 0:HALF], 0)
+        nc.gpsimd.memset(g_codes[:, 0:HALF], 0)
+        nc.gpsimd.memset(g_scales[:, 0:HALF].bitcast(U32), 0)
         for window in windows:
-            nc.vector.memset(window[:].bitcast(I32), 0)
+            nc.gpsimd.memset(window[:].bitcast(I32), 0)
         for n in range(SLOT_TILES):
             nc.tensor.transpose(banks[3][:, block(n)], tx_listed[:, block(n)], ident[:])
         nc.scalar.activation(token_factors[:, :, 0], banks[3][:, P - 1:BANK:P], ACT.Copy, scale=-1.0)
@@ -157,7 +157,8 @@ def tile_attend_grouter_x_pl_kernel(tc, xT, W, dg, lb, ce, tx, offs, out_0, out_
         nc.vector.quantize_mx(out=w_e_codes[:].bitcast(E4M3X4), scales=w_e_scales[:],
                               in_=wt_bf[:].rearrange("p d t -> p (d t)"))
 
-        h_tiles = [sb("h%d" % n, [P, E], F32)[:] for n in range(SLOT_TILES)]
+        h_all = sb("h_all", [P, SLOT_TILES, E], F32, tag="x_bf")
+        h_tiles = [h_all[:, n, :] for n in range(SLOT_TILES)]
         for n in range(SLOT_TILES):
             nc.vector.tensor_tensor(dealt(h_tiles[n]), natural(dg_raw[n // 2][:, n % 2, :]),
                                  natural(lb_rows[:]), ALU.add)

@@ -31,6 +31,7 @@ VECTOR_CHUNKS = CHUNKS // 2
 WINDOWS = 3
 PLANE_ORDER = (2, 0, 1, 3)
 EARLY = 2
+X_ORDER = (2, 0, 1, 3)
 QUADRANTS = 4
 
 FLOPS = 2 * 2 * D * E * SLOTS
@@ -81,7 +82,7 @@ def tile_attend_grouter_x_pl_kernel(tc, xT, W, dg, lb, ce, tx, offs, out_0, out_
         nc.sync.dma_start(w_raw[:], W.rearrange("(p j) e -> p j e", j=LANES))
         x_rows = xT.rearrange("(p j) x -> j p x", j=LANES)
         x_raw = [sb("x_raw%d" % j, [P, TOKENS], F32) for j in range(LANES)]
-        for j in range(LANES):
+        for j in X_ORDER:
             nc.sync.dma_start(x_raw[j][:], x_rows[j])
         lb_rows = sb("lb_rows", [P, E], F32)
         nc.sync.dma_start(lb_rows[:], lb)
@@ -116,8 +117,13 @@ def tile_attend_grouter_x_pl_kernel(tc, xT, W, dg, lb, ce, tx, offs, out_0, out_
         nc.vector.reciprocal(token_inverses[:], token_factors[:])
 
         x_bf = sb("x_bf", [P, SLOTS, LANES], BF16)
+        nc.vector.tensor_copy(x_bf[:, :, 2], x_raw[2][:].indirect(offsets[:]))
+        x_pair = sb("x_pair", [P, 2, SLOTS], BF16)
         for j in range(2):
-            nc.vector.tensor_copy(x_bf[:, :, j], x_raw[j][:].indirect(offsets[:]))
+            nc.vector.tensor_copy(x_pair[:, j, :], x_raw[j][:].indirect(offsets[:]))
+        for half in range(2):
+            cols = slice(half * HALF, (half + 1) * HALF)
+            nc.scalar.copy(x_bf[:, cols, 0:2], x_pair[:, :, cols].rearrange("p j i -> p i j"))
 
         w_words = w_bf[:].rearrange("p e j -> p (e j)").bitcast(F32)
         wt_bf = sb("wt_bf", [P, D, LANES], BF16)
@@ -127,8 +133,7 @@ def tile_attend_grouter_x_pl_kernel(tc, xT, W, dg, lb, ce, tx, offs, out_0, out_
             nc.scalar.copy(wt_bf[:, 2 * P * u:2 * P * (u + 1), :].rearrange("p (k v w) t -> p v t w k", k=2, w=2),
                            banks[6 + u][:].bitcast(BF16).rearrange("p (t v w k) -> p v t w k", t=LANES, w=2, k=2))
 
-        nc.vector.tensor_copy(x_bf[:, :, 2], x_raw[2][:].indirect(offsets[:]))
-        w_d_codes = sb("w_d_codes", [P, E], U32)
+        w_d_codes = sb("w_d_codes", [P, E], U32, tag="x_raw0")
         w_d_scales = sb("w_d_scales", [P, E], U8)
         nc.vector.quantize_mx(out=w_d_codes[:].bitcast(E4M3X4), scales=w_d_scales[:],
                               in_=w_bf[:].rearrange("p e j -> p (e j)"))
@@ -152,7 +157,7 @@ def tile_attend_grouter_x_pl_kernel(tc, xT, W, dg, lb, ce, tx, offs, out_0, out_
             for t in range(LANES):
                 nc.scalar.activation(scaled_t[half][:, t, :], sums[t], ACT.Copy, scale=ce_col[:, t:t + 1])
 
-        w_e_codes = sb("w_e_codes", [P, D], U32)
+        w_e_codes = sb("w_e_codes", [P, D], U32, tag="x_raw1")
         w_e_scales = sb("w_e_scales", [P, D], U8)
         nc.vector.quantize_mx(out=w_e_codes[:].bitcast(E4M3X4), scales=w_e_scales[:],
                               in_=wt_bf[:].rearrange("p d t -> p (d t)"))

@@ -30,7 +30,7 @@ CHUNKS = TOKENS // CHUNK
 VECTOR_CHUNKS = CHUNKS // 2
 WINDOWS = 3
 PLANE_ORDER = (2, 0, 1, 3)
-EARLY = 2
+EARLY = 1
 X_ORDER = (2, 0, 1, 3)
 QUADRANTS = 4
 
@@ -93,7 +93,7 @@ def tile_attend_grouter_x_pl_kernel(tc, xT, W, dg, lb, ce, tx, offs, out_0, out_
 
         g_codes = sb("g_codes", [P, HALF + SLOTS], U32)
         g_scales = sb("g_scales", [P, HALF + SLOTS], U8)
-        windows = [sb("window%d" % j, [P, TOKENS], F32) for j in range(WINDOWS)]
+        windows = [sb("window0", [P, TOKENS], F32)]
 
         w_bf = sb("w_bf", [P, E, LANES], BF16)
         nc.scalar.copy(w_bf[:].rearrange("p (t b r) j -> p t b r j", t=LANES, r=RUN),
@@ -108,8 +108,7 @@ def tile_attend_grouter_x_pl_kernel(tc, xT, W, dg, lb, ce, tx, offs, out_0, out_
         nc.vector.tensor_copy(tx_listed[:], tx_window[:].indirect(offsets[:]))
         nc.gpsimd.memset(g_codes[:, 0:HALF], 0)
         nc.gpsimd.memset(g_scales[:, 0:HALF].bitcast(U32), 0)
-        for window in windows:
-            nc.gpsimd.memset(window[:].bitcast(I32), 0)
+        nc.vector.memset(windows[0][:].bitcast(I32), 0)
         for n in range(SLOT_TILES):
             nc.tensor.transpose(banks[3][:, block(n)], tx_listed[:, block(n)], ident[:])
         nc.scalar.activation(token_factors[:, :, 0], banks[3][:, P - 1:BANK:P], ACT.Copy, scale=-1.0)
@@ -168,7 +167,6 @@ def tile_attend_grouter_x_pl_kernel(tc, xT, W, dg, lb, ce, tx, offs, out_0, out_
             nc.vector.tensor_tensor(dealt(h_tiles[n]), natural(dg_raw[n // 2][:, n % 2, :]),
                                  natural(lb_rows[:]), ALU.add)
 
-        planes = {j: windows[step % WINDOWS] for step, j in enumerate(PLANE_ORDER)}
 
         def per_tile(name, width):
             return [sb("%s%d" % (name, n), [P, width], F32) for n in range(SLOT_TILES)]
@@ -237,18 +235,22 @@ def tile_attend_grouter_x_pl_kernel(tc, xT, W, dg, lb, ce, tx, offs, out_0, out_
                                 start=True, stop=True)
 
         early = PLANE_ORDER[0:EARLY]
+        planes = {PLANE_ORDER[0]: windows[0], PLANE_ORDER[-1]: windows[0]}
         dx_early = [sb("dx_early%d" % k, [P, HALF], F32) for k in range(EARLY)]
         for k, j in enumerate(early):
-            dx_pass(j, banks[6 + k], 0)
-            nc.scalar.copy(dx_early[k][:], banks[6 + k][:, HALF:SLOTS])
-        nc.vector.tensor_copy(planes[early[0]][:].indirect(half_offsets[0]), dx_early[0][:])
+            dx_pass(j, banks[7], 0)
+            nc.scalar.copy(dx_early[k][:], banks[7][:, HALF:SLOTS])
         quantise_g(1)
-        nc.vector.tensor_copy(planes[early[1]][:].indirect(half_offsets[0]), dx_early[1][:])
+        nc.vector.tensor_copy(planes[early[0]][:].indirect(half_offsets[0]), dx_early[0][:])
         dx = [sb("dx%d" % j, [P, SLOTS], F32) for j in range(LANES)]
         for step, j in enumerate(PLANE_ORDER):
             first = HALF if j in early else 0
             dx_pass(j, banks[4 + step], HALF)
             nc.scalar.copy(dx[j][:, first:SLOTS], banks[4 + step][:, first:SLOTS])
+
+        for j, tag in zip(PLANE_ORDER[1:WINDOWS], ("g_bf1", "x_raw1")):
+            planes[j] = sb("window_of%d" % j, [P, TOKENS], F32, tag=tag)
+            nc.gpsimd.memset(planes[j][:].bitcast(I32), 0)
 
         out_rows = out_0.rearrange("(p j) x -> j p x", j=LANES)
         pairs = [sb("pairs%d" % c, [P, 2, CHUNK, 2], BF16) for c in range(CHUNKS)]

@@ -30,7 +30,7 @@ CHUNKS = TOKENS // CHUNK
 VECTOR_CHUNKS = CHUNKS // 2
 WINDOWS = 3
 PLANE_ORDER = (2, 0, 1, 3)
-EARLY = 1
+EARLY = 2
 X_ORDER = (2, 0, 1, 3)
 QUADRANTS = 4
 
@@ -93,7 +93,7 @@ def tile_attend_grouter_x_pl_kernel(tc, xT, W, dg, lb, ce, tx, offs, out_0, out_
 
         g_codes = sb("g_codes", [P, HALF + SLOTS], U32)
         g_scales = sb("g_scales", [P, HALF + SLOTS], U8)
-        windows = [sb("window0", [P, TOKENS], F32)]
+        windows = [sb("window%d" % k, [P, TOKENS], F32) for k in range(EARLY)]
 
         w_bf = sb("w_bf", [P, E, LANES], BF16)
         nc.scalar.copy(w_bf[:].rearrange("p (t b r) j -> p t b r j", t=LANES, r=RUN),
@@ -108,7 +108,8 @@ def tile_attend_grouter_x_pl_kernel(tc, xT, W, dg, lb, ce, tx, offs, out_0, out_
         nc.vector.tensor_copy(tx_listed[:], tx_window[:].indirect(offsets[:]))
         nc.gpsimd.memset(g_codes[:, 0:HALF], 0)
         nc.gpsimd.memset(g_scales[:, 0:HALF].bitcast(U32), 0)
-        nc.vector.memset(windows[0][:].bitcast(I32), 0)
+        for window in windows:
+            nc.vector.memset(window[:].bitcast(I32), 0)
         for n in range(SLOT_TILES):
             nc.tensor.transpose(banks[3][:, block(n)], tx_listed[:, block(n)], ident[:])
         nc.scalar.activation(token_factors[:, :, 0], banks[3][:, P - 1:BANK:P], ACT.Copy, scale=-1.0)
@@ -235,22 +236,23 @@ def tile_attend_grouter_x_pl_kernel(tc, xT, W, dg, lb, ce, tx, offs, out_0, out_
                                 start=True, stop=True)
 
         early = PLANE_ORDER[0:EARLY]
-        planes = {PLANE_ORDER[0]: windows[0], PLANE_ORDER[-1]: windows[0]}
-        dx_early = [sb("dx_early%d" % k, [P, HALF], F32) for k in range(EARLY)]
+        planes = {PLANE_ORDER[0]: windows[0], PLANE_ORDER[1]: windows[1], PLANE_ORDER[-1]: windows[0]}
+        dx_early = [sb("dx_early%d" % k, [P, HALF], F32, tag="neg_ce" if k == 1 else "") for k in range(EARLY)]
         for k, j in enumerate(early):
-            dx_pass(j, banks[7], 0)
-            nc.scalar.copy(dx_early[k][:], banks[7][:, HALF:SLOTS])
-        quantise_g(1)
+            dx_pass(j, banks[6 + k], 0)
+            nc.scalar.copy(dx_early[k][:], banks[6 + k][:, HALF:SLOTS])
         nc.vector.tensor_copy(planes[early[0]][:].indirect(half_offsets[0]), dx_early[0][:])
+        quantise_g(1)
+        nc.vector.tensor_copy(planes[early[1]][:].indirect(half_offsets[0]), dx_early[1][:])
         dx = [sb("dx%d" % j, [P, SLOTS], F32) for j in range(LANES)]
         for step, j in enumerate(PLANE_ORDER):
             first = HALF if j in early else 0
             dx_pass(j, banks[4 + step], HALF)
             nc.scalar.copy(dx[j][:, first:SLOTS], banks[4 + step][:, first:SLOTS])
 
-        for j, tag in zip(PLANE_ORDER[1:WINDOWS], ("g_bf1", "x_raw1")):
-            planes[j] = sb("window_of%d" % j, [P, TOKENS], F32, tag=tag)
-            nc.gpsimd.memset(planes[j][:].bitcast(I32), 0)
+        third = PLANE_ORDER[EARLY]
+        planes[third] = sb("window_late", [P, TOKENS], F32, tag="g_bf1")
+        nc.gpsimd.memset(planes[third][:].bitcast(I32), 0)
 
         out_rows = out_0.rearrange("(p j) x -> j p x", j=LANES)
         pairs = [sb("pairs%d" % c, [P, 2, CHUNK, 2], BF16) for c in range(CHUNKS)]

@@ -32,6 +32,8 @@ WINDOWS = 3
 PLANE_ORDER = (2, 0, 1, 3)
 EARLY = 2
 X_ORDER = (2, 0, 1, 3)
+DIRECT = 1
+VECTOR_H = 2
 QUADRANTS = 4
 
 FLOPS = 2 * 2 * D * E * SLOTS
@@ -73,19 +75,19 @@ def tile_attend_grouter_x_pl_kernel(tc, xT, W, dg, lb, ce, tx, offs, out_0, out_
 
         ce_lanes = sb("ce_lanes", [P, P], F32)
         tx_window = sb("tx_window", [P, TOKENS], F32)
-        nc.gpsimd.memset(ce_lanes[0:P - LANES, :], 0.0)
+        nc.gpsimd.memset(ce_lanes[0:P - 2 * LANES, :], 0.0)
         nc.vector.memset(tx_window[0:P - 1, :].bitcast(I32), 0)
         nc.sync.dma_start(tx_window[P - 1:P, :], tx[0:1, :])
         nc.sync.dma_start(ce_lanes[P - LANES:P, :].rearrange("t (b r) -> t b r", r=RUN),
                           ce[0, :].rearrange("(b t r) -> t b r", t=LANES, r=RUN))
+        nc.sync.dma_start(ce_lanes[P - 2 * LANES:P - LANES, :].rearrange("t (b r) -> t b r", r=RUN),
+                            lb[0, :].rearrange("(b t r) -> t b r", t=LANES, r=RUN))
         w_raw = sb("w_raw", [P, LANES, E], F32)
         nc.sync.dma_start(w_raw[:], W.rearrange("(p j) e -> p j e", j=LANES))
         x_rows = xT.rearrange("(p j) x -> j p x", j=LANES)
         x_raw = [sb("x_raw%d" % j, [P, TOKENS], F32) for j in range(LANES)]
         for j in X_ORDER:
             nc.sync.dma_start(x_raw[j][:], x_rows[j])
-        lb_rows = sb("lb_rows", [P, E], F32)
-        nc.sync.dma_start(lb_rows[:], lb)
         dg_raw = [sb("dg_raw%d" % half, [P, 2, E], F32) for half in range(2)]
         for half in range(2):
             nc.sync.dma_start(dg_raw[half][:],
@@ -103,13 +105,15 @@ def tile_attend_grouter_x_pl_kernel(tc, xT, W, dg, lb, ce, tx, offs, out_0, out_
         ce_col = sb("ce_col", [P, LANES], F32)
         neg_ce = sb("neg_ce", [P, 1, LANES, 1], F32)
         nc.scalar.copy(ce_col[:], banks[2][:, P - LANES:P])
+        lb_col = sb("lb_col", [P, LANES], F32)
+        nc.scalar.copy(lb_col[:], banks[2][:, P - 2 * LANES:P - LANES])
         nc.scalar.activation(neg_ce[:, 0, :, 0], banks[2][:, P - LANES:P], ACT.Copy, scale=-1.0)
         tx_listed = sb("tx_listed", [P, SLOTS], F32)
         nc.vector.tensor_copy(tx_listed[:], tx_window[:].indirect(offsets[:]))
         nc.gpsimd.memset(g_codes[:, 0:HALF], 0)
         nc.gpsimd.memset(g_scales[:, 0:HALF].bitcast(U32), 0)
-        for window in windows:
-            nc.vector.memset(window[:].bitcast(I32), 0)
+        nc.vector.memset(windows[0][:].bitcast(I32), 0)
+        nc.gpsimd.memset(windows[1][:].bitcast(I32), 0)
         for n in range(SLOT_TILES):
             nc.tensor.transpose(banks[3][:, block(n)], tx_listed[:, block(n)], ident[:])
         nc.scalar.activation(token_factors[:, :, 0], banks[3][:, P - 1:BANK:P], ACT.Copy, scale=-1.0)
@@ -146,16 +150,29 @@ def tile_attend_grouter_x_pl_kernel(tc, xT, W, dg, lb, ce, tx, offs, out_0, out_
             nc.vector.tensor_copy(x_bf[:, cols, LANES - 1], x_raw[LANES - 1][:].indirect(half_offsets[half]))
             nc.vector.quantize_mx(out=x_codes[:, cols].bitcast(E4M3X4), scales=x_scales[:, cols],
                                   in_=x_bf[:, cols, :].rearrange("p i j -> p (i j)"))
-        for half in range(2):
-            cols = slice(half * HALF, (half + 1) * HALF)
-            sums = [banks[2 * half + t // 2][:, (t % 2) * HALF:(t % 2 + 1) * HALF] for t in range(LANES)]
+        for n in range(DIRECT):
+            nc.tensor.matmul_mx(out=banks[4 + n][:], lhsT=x_codes[:, block(n)].bitcast(E4M3X4),
+                                lhsT_scale=x_scales[:, block(n)],
+                                rhs=w_d_codes[:].bitcast(E4M3X4), rhs_scale=w_d_scales[:], start=True, stop=True)
+
+        def scores(first, width, first_bank):
+            cols = slice(first, first + width)
+            per_bank = BANK // width
+            sums = [banks[first_bank + t // per_bank][:, (t % per_bank) * width:(t % per_bank + 1) * width]
+                    for t in range(LANES)]
             for t in range(LANES):
                 nc.tensor.matmul_mx(out=sums[t], lhsT=w_d_codes[:, block(t)].bitcast(E4M3X4),
                                     lhsT_scale=w_d_scales[:, block(t)],
                                     rhs=x_codes[:, cols].bitcast(E4M3X4), rhs_scale=x_scales[:, cols],
                                     start=True, stop=True)
             for t in range(LANES):
-                nc.scalar.activation(scaled_t[half][:, t, :], sums[t], ACT.Copy, scale=ce_col[:, t:t + 1])
+                nc.scalar.activation(scaled_t[first // HALF][:, t, first % HALF:first % HALF + width], sums[t],
+                                     ACT.Copy, scale=ce_col[:, t:t + 1])
+
+        for n in range(DIRECT, 2):
+            scores(n * P, P, n)
+        for n in range(2, SLOT_TILES):
+            scores(n * P, P, n)
 
         w_e_codes = sb("w_e_codes", [P, D], U32, tag="x_raw1")
         w_e_scales = sb("w_e_scales", [P, D], U8)
@@ -164,16 +181,29 @@ def tile_attend_grouter_x_pl_kernel(tc, xT, W, dg, lb, ce, tx, offs, out_0, out_
 
         h_all = sb("h_all", [P, SLOT_TILES, E], F32, tag="x_bf")
         h_tiles = [h_all[:, n, :] for n in range(SLOT_TILES)]
-        for n in range(SLOT_TILES):
-            nc.vector.tensor_tensor(dealt(h_tiles[n]), natural(dg_raw[n // 2][:, n % 2, :]),
-                                 natural(lb_rows[:]), ALU.add)
+        for t in range(LANES):
+            nc.tensor.transpose(banks[7][:, block(t)], lb_col[:, t:t + 1].to_broadcast([P, P]), ident[:])
+        lb_rows = sb("lb_rows", [P, E], F32)
+        nc.scalar.copy(lb_rows[:], banks[7][:])
+        for t in range(LANES):
+            nc.tensor.transpose(banks[0][:, block(t)], ce_col[:, t:t + 1].to_broadcast([P, P]), ident[:])
+        ce_rows = sb("ce_rows", [P, E], F32)
+        nc.scalar.copy(ce_rows[:], banks[0][:])
+
+        def add_h(n):
+            if n < VECTOR_H:
+                nc.vector.tensor_tensor(dealt(h_tiles[n]), natural(dg_raw[n // 2][:, n % 2, :]),
+                                        dealt(banks[7][:]), ALU.add)
+            else:
+                nc.gpsimd.tensor_tensor(dealt(h_tiles[n]), natural(dg_raw[n // 2][:, n % 2, :]),
+                                        dealt(lb_rows[:]), ALU.add)
 
 
         def per_tile(name, width):
             return [sb("%s%d" % (name, n), [P, width], F32) for n in range(SLOT_TILES)]
 
         q, term_h, term_s = [per_tile(name, E) for name in ("q", "term_h", "term_s")]
-        neg_z = [sb("neg_z%d" % n, [P, E], F32, tag="dg_raw1" if n == 0 else "") for n in range(SLOT_TILES)]
+        neg_z = per_tile("neg_z", E)
         neg_m, tot, neg_tx_s, s_factor = [
             per_tile(name, 1) for name in ("neg_m", "tot", "neg_tx_s", "s_factor")]
         factors = per_tile("factors", 2)
@@ -183,10 +213,16 @@ def tile_attend_grouter_x_pl_kernel(tc, xT, W, dg, lb, ce, tx, offs, out_0, out_
         def softmax(n):
             neg_tx = token_factors[:, n, 0:1]
             bank = banks[4 + n]
-            for t in range(LANES):
-                nc.tensor.transpose(bank[:, block(t)], scaled_t[n // 2][:, t, block(n % 2)], ident[:])
-            nc.vector.tensor_scalar(neg_z[n][:], bank[:], neg_tx, None, ALU.mult, ALU.min,
-                                    accum_out=neg_m[n][:])
+            if n < DIRECT:
+                nc.vector.scalar_tensor_tensor(neg_z[n][:], bank[:], neg_tx, ce_rows[:], ALU.mult, ALU.mult)
+                add_h(n)
+                nc.vector.tensor_reduce(neg_m[n][:], neg_z[n][:], mybir.AxisListType.X, ALU.min)
+            else:
+                add_h(n)
+                for t in range(LANES):
+                    nc.tensor.transpose(bank[:, block(t)], scaled_t[n // 2][:, t, block(n % 2)], ident[:])
+                nc.vector.tensor_scalar(neg_z[n][:], bank[:], neg_tx, None, ALU.mult, ALU.min,
+                                        accum_out=neg_m[n][:])
             nc.scalar.activation(q[n][:], neg_z[n][:], ACT.Exp, bias=neg_m[n][:], scale=-1.0, accum_out=tot[n][:])
             nc.scalar.activation(divisors[n][:], token_inverses[:, n, :], ACT.Copy, scale=tot[n][:])
 
@@ -237,7 +273,7 @@ def tile_attend_grouter_x_pl_kernel(tc, xT, W, dg, lb, ce, tx, offs, out_0, out_
 
         early = PLANE_ORDER[0:EARLY]
         planes = {PLANE_ORDER[0]: windows[0], PLANE_ORDER[1]: windows[1], PLANE_ORDER[-1]: windows[0]}
-        dx_early = [sb("dx_early%d" % k, [P, HALF], F32, tag="neg_ce" if k == 1 else "") for k in range(EARLY)]
+        dx_early = [sb("dx_early%d" % k, [P, HALF], F32, tag=("x_bf", "neg_ce")[k]) for k in range(EARLY)]
         for k, j in enumerate(early):
             dx_pass(j, banks[6 + k], 0)
             nc.scalar.copy(dx_early[k][:], banks[6 + k][:, HALF:SLOTS])
@@ -275,7 +311,7 @@ def tile_attend_grouter_x_pl_kernel(tc, xT, W, dg, lb, ce, tx, offs, out_0, out_
                                             1.0, 0.0, ALU.mult, ALU.add)
 
         y_bf = [sb("y_bf%d" % c, [P, CHUNK * LANES], BF16) for c in range(CHUNKS)]
-        y_scales = sb("y_scales", [P, TOKENS], U8)
+        y_scales = sb("y_scales", [P, 2 * CHUNK], U8)
         words_out = out_1[0].rearrange("p x j -> p (x j)").bitcast(I32)
 
         def merge(c):
@@ -285,7 +321,8 @@ def tile_attend_grouter_x_pl_kernel(tc, xT, W, dg, lb, ce, tx, offs, out_0, out_
 
         def quantise_y(c):
             y_codes = sb("y_codes%d" % c, [P, CHUNK], U32)
-            nc.vector.quantize_mx(out=y_codes[:].bitcast(E4M3X4), scales=y_scales[:, chunk(c)], in_=y_bf[c][:])
+            nc.vector.quantize_mx(out=y_codes[:].bitcast(E4M3X4), scales=y_scales[4 * (c // 2):P, chunk(c % 2)],
+                                  in_=y_bf[c][:])
             nc.sync.dma_start(words_out[:, chunk(c)], y_codes[:].bitcast(I32))
 
         for c in range(VECTOR_CHUNKS):
@@ -299,5 +336,5 @@ def tile_attend_grouter_x_pl_kernel(tc, xT, W, dg, lb, ce, tx, offs, out_0, out_
             quantise_y(c)
         for quad in range(QUADRANTS):
             queue = nc.sync if quad % 2 == 0 else nc.scalar
-            queue.dma_start(out_2[0, 4 * quad:4 * quad + 4, :].bitcast(I32),
-                            y_scales[32 * quad:32 * quad + 4, :].bitcast(I32))
+            queue.dma_start(out_2[0, 4 * quad:4 * quad + 4, :].bitcast(I32).rearrange("f (k x) -> k f x", k=2),
+                            y_scales[32 * quad:32 * quad + 8, :].bitcast(I32))

@@ -73,15 +73,13 @@ def tile_attend_grouter_x_pl_kernel(tc, xT, W, dg, lb, ce, tx, offs, out_0, out_
         nc.scalar.activation(ones[:], ident[:, 0:SLOT_TILES], ACT.Exp, scale=0.0)
         nc.scalar.activation(token_factors[:, :, 1], ones[:], ACT.Copy, scale=-1.0)
 
-        ce_lanes = sb("ce_lanes", [P, P], F32)
+        expert_rows = sb("expert_rows", [P, E], F32)
         tx_window = sb("tx_window", [P, TOKENS], F32)
-        nc.gpsimd.memset(ce_lanes[0:P - 2 * LANES, :], 0.0)
+        nc.vector.memset(expert_rows[0:P - 2, :], 0.0)
         nc.vector.memset(tx_window[0:P - 1, :].bitcast(I32), 0)
         nc.sync.dma_start(tx_window[P - 1:P, :], tx[0:1, :])
-        nc.sync.dma_start(ce_lanes[P - LANES:P, :].rearrange("t (b r) -> t b r", r=RUN),
-                          ce[0, :].rearrange("(b t r) -> t b r", t=LANES, r=RUN))
-        nc.sync.dma_start(ce_lanes[P - 2 * LANES:P - LANES, :].rearrange("t (b r) -> t b r", r=RUN),
-                            lb[0, :].rearrange("(b t r) -> t b r", t=LANES, r=RUN))
+        nc.sync.dma_start(expert_rows[P - 1:P, :], ce[0:1, :])
+        nc.sync.dma_start(expert_rows[P - 2:P - 1, :], lb[0:1, :])
         w_raw = sb("w_raw", [P, LANES, E], F32)
         nc.sync.dma_start(w_raw[:], W.rearrange("(p j) e -> p j e", j=LANES))
         x_rows = xT.rearrange("(p j) x -> j p x", j=LANES)
@@ -101,13 +99,16 @@ def tile_attend_grouter_x_pl_kernel(tc, xT, W, dg, lb, ce, tx, offs, out_0, out_
         nc.scalar.copy(w_bf[:].rearrange("p (t b r) j -> p t b r j", t=LANES, r=RUN),
                        w_raw[:].rearrange("p j (b t r) -> p t b r j", t=LANES, r=RUN))
 
-        nc.tensor.transpose(banks[2][:, 0:P], ce_lanes[:], ident[:])
+        expert_dealt = sb("expert_dealt", [P, E], F32)
+        nc.vector.tensor_copy(dealt(expert_dealt[:]), natural(expert_rows[:]))
+        for t in range(LANES):
+            nc.tensor.transpose(banks[2][:, block(t)], expert_dealt[:, block(t)], ident[:])
         ce_col = sb("ce_col", [P, LANES], F32)
         neg_ce = sb("neg_ce", [P, 1, LANES, 1], F32)
-        nc.scalar.copy(ce_col[:], banks[2][:, P - LANES:P])
+        nc.scalar.copy(ce_col[:], banks[2][:, P - 1:BANK:P])
         lb_col = sb("lb_col", [P, LANES], F32)
-        nc.scalar.copy(lb_col[:], banks[2][:, P - 2 * LANES:P - LANES])
-        nc.scalar.activation(neg_ce[:, 0, :, 0], banks[2][:, P - LANES:P], ACT.Copy, scale=-1.0)
+        nc.scalar.copy(lb_col[:], banks[2][:, P - 2:BANK:P])
+        nc.scalar.activation(neg_ce[:, 0, :, 0], banks[2][:, P - 1:BANK:P], ACT.Copy, scale=-1.0)
         tx_listed = sb("tx_listed", [P, SLOTS], F32)
         nc.vector.tensor_copy(tx_listed[:], tx_window[:].indirect(offsets[:]))
         nc.gpsimd.memset(g_codes[:, 0:HALF], 0)
@@ -133,9 +134,9 @@ def tile_attend_grouter_x_pl_kernel(tc, xT, W, dg, lb, ce, tx, offs, out_0, out_
         wt_bf = sb("wt_bf", [P, D, LANES], BF16)
         for u in range(2):
             for t in range(LANES):
-                nc.tensor.transpose(banks[6 + u][:, block(t)], w_words[:, 2 * P * t + u:2 * P * (t + 1):2], ident[:])
+                nc.tensor.transpose(banks[5 + u][:, block(t)], w_words[:, 2 * P * t + u:2 * P * (t + 1):2], ident[:])
             nc.scalar.copy(wt_bf[:, 2 * P * u:2 * P * (u + 1), :].rearrange("p (k v w) t -> p v t w k", k=2, w=2),
-                           banks[6 + u][:].bitcast(BF16).rearrange("p (t v w k) -> p v t w k", t=LANES, w=2, k=2))
+                           banks[5 + u][:].bitcast(BF16).rearrange("p (t v w k) -> p v t w k", t=LANES, w=2, k=2))
 
         w_d_codes = sb("w_d_codes", [P, E], U32, tag="x_raw0")
         w_d_scales = sb("w_d_scales", [P, E], U8)

@@ -96,8 +96,10 @@ def tile_attend_grouter_x_pl_kernel(tc, xT, W, dg, lb, ce, tx, offs, out_0, out_
         windows = [sb("window%d" % k, [P, TOKENS], F32) for k in range(EARLY)]
 
         w_bf = sb("w_bf", [P, E, LANES], BF16)
-        nc.scalar.copy(w_bf[:].rearrange("p (t b r) j -> p t b r j", t=LANES, r=RUN),
-                       w_raw[:].rearrange("p j (b t r) -> p t b r j", t=LANES, r=RUN))
+        w_dealt = w_bf[:].rearrange("p (t b r) j -> p t b r j", t=LANES, r=RUN)
+        w_natural = w_raw[:].rearrange("p j (b t r) -> p t b r j", t=LANES, r=RUN)
+        nc.vector.tensor_copy(w_dealt[:, 0:2], w_natural[:, 0:2])
+        nc.scalar.copy(w_dealt[:, 2:LANES], w_natural[:, 2:LANES])
 
         expert_dealt = sb("expert_dealt", [P, E], F32)
         nc.vector.tensor_copy(dealt(expert_dealt[:]), natural(expert_rows[:]))
@@ -124,10 +126,10 @@ def tile_attend_grouter_x_pl_kernel(tc, xT, W, dg, lb, ce, tx, offs, out_0, out_
         x_bf = sb("x_bf", [P, SLOTS, LANES], BF16)
         nc.vector.tensor_copy(x_bf[:, :, 2], x_raw[2][:].indirect(offsets[:]))
         x_pair = sb("x_pair", [P, 2, SLOTS], BF16)
-        for j in range(2):
-            nc.vector.tensor_copy(x_pair[:, j, :], x_raw[j][:].indirect(offsets[:]))
+        nc.vector.tensor_copy(x_pair[:, 0, :], x_raw[0][:].indirect(offsets[:]))
         for half in range(2):
             cols = slice(half * HALF, (half + 1) * HALF)
+            nc.vector.tensor_copy(x_pair[:, 1, cols], x_raw[1][:].indirect(half_offsets[half]))
             nc.scalar.copy(x_bf[:, cols, 0:2], x_pair[:, :, cols].rearrange("p j i -> p i j"))
 
         w_words = w_bf[:].rearrange("p e j -> p (e j)").bitcast(F32)

@@ -68,18 +68,17 @@ def tile_attend_grouter_x_pl_kernel(tc, xT, W, dg, lb, ce, tx, offs, out_0, out_
 
         ident = sb("ident", [P, P], F32)
         make_identity(nc, ident[:])
-        token_factors = sb("token_factors", [P, SLOT_TILES, 2], F32)
-        ones = sb("ones", [P, SLOT_TILES], F32)
-        nc.scalar.activation(ones[:], ident[:, 0:SLOT_TILES], ACT.Exp, scale=0.0)
-        nc.scalar.activation(token_factors[:, :, 1], ones[:], ACT.Copy, scale=-1.0)
+        neg_tx_col = sb("neg_tx_col", [P, SLOT_TILES], F32)
+        ones = sb("ones", [P, 1], F32)
+        nc.scalar.activation(ones[:], ident[:, 0:1], ACT.Exp, scale=0.0)
 
         expert_rows = sb("expert_rows", [P, E], F32)
         tx_window = sb("tx_window", [P, TOKENS], F32)
         nc.vector.memset(expert_rows[0:P - 2, :], 0.0)
         nc.vector.memset(tx_window[0:P - 1, :].bitcast(I32), 0)
-        nc.sync.dma_start(tx_window[P - 1:P, :], tx[0:1, :])
         nc.sync.dma_start(expert_rows[P - 1:P, :], ce[0:1, :])
         nc.sync.dma_start(expert_rows[P - 2:P - 1, :], lb[0:1, :])
+        nc.sync.dma_start(tx_window[P - 1:P, :], tx[0:1, :])
         w_raw = sb("w_raw", [P, LANES, E], F32)
         nc.sync.dma_start(w_raw[:], W.rearrange("(p j) e -> p j e", j=LANES))
         x_rows = xT.rearrange("(p j) x -> j p x", j=LANES)
@@ -93,7 +92,7 @@ def tile_attend_grouter_x_pl_kernel(tc, xT, W, dg, lb, ce, tx, offs, out_0, out_
 
         g_codes = sb("g_codes", [P, HALF + SLOTS], U32)
         g_scales = sb("g_scales", [P, HALF + SLOTS], U8)
-        windows = [sb("window%d" % k, [P, TOKENS], F32) for k in range(EARLY)]
+        windows = [sb("window%d" % k, [P, TOKENS], F32, tag=("tx_window", "")[k]) for k in range(EARLY)]
 
         w_bf = sb("w_bf", [P, E, LANES], BF16)
         w_dealt = w_bf[:].rearrange("p (t b r) j -> p t b r j", t=LANES, r=RUN)
@@ -106,11 +105,9 @@ def tile_attend_grouter_x_pl_kernel(tc, xT, W, dg, lb, ce, tx, offs, out_0, out_
         for t in range(LANES):
             nc.tensor.transpose(banks[2][:, block(t)], expert_dealt[:, block(t)], ident[:])
         ce_col = sb("ce_col", [P, LANES], F32)
-        neg_ce = sb("neg_ce", [P, 1, LANES, 1], F32)
         nc.scalar.copy(ce_col[:], banks[2][:, P - 1:BANK:P])
         lb_col = sb("lb_col", [P, LANES], F32)
         nc.scalar.copy(lb_col[:], banks[2][:, P - 2:BANK:P])
-        nc.scalar.activation(neg_ce[:, 0, :, 0], banks[2][:, P - 1:BANK:P], ACT.Copy, scale=-1.0)
         tx_listed = sb("tx_listed", [P, SLOTS], F32)
         nc.vector.tensor_copy(tx_listed[:], tx_window[:].indirect(offsets[:]))
         nc.gpsimd.memset(g_codes[:, 0:HALF], 0)
@@ -119,9 +116,14 @@ def tile_attend_grouter_x_pl_kernel(tc, xT, W, dg, lb, ce, tx, offs, out_0, out_
         nc.gpsimd.memset(windows[1][:].bitcast(I32), 0)
         for n in range(SLOT_TILES):
             nc.tensor.transpose(banks[3][:, block(n)], tx_listed[:, block(n)], ident[:])
-        nc.scalar.activation(token_factors[:, :, 0], banks[3][:, P - 1:BANK:P], ACT.Copy, scale=-1.0)
-        token_inverses = sb("token_inverses", [P, SLOT_TILES, 2], F32)
-        nc.vector.reciprocal(token_inverses[:], token_factors[:])
+        nc.scalar.activation(neg_tx_col[:], banks[3][:, P - 1:BANK:P], ACT.Copy, scale=-1.0)
+        for n in range(SLOT_TILES):
+            nc.tensor.transpose(banks[1][:, block(n)], neg_tx_col[:, n:n + 1].to_broadcast([P, P]), ident[:])
+        neg_tx_rows = sb("neg_tx_rows", [P, SLOTS], F32)
+        nc.scalar.activation(neg_tx_rows[:], banks[1][:], ACT.Copy, scale=ones[:])
+        scale_t = sb("scale_t", [P, LANES, SLOTS], F32)
+        for t in range(LANES):
+            nc.gpsimd.tensor_scalar(scale_t[:, t, :], neg_tx_rows[:], ce_col[:, t:t + 1], -1.0, ALU.mult, ALU.mult)
 
         x_bf = sb("x_bf", [P, SLOTS, LANES], BF16)
         nc.vector.tensor_copy(x_bf[:, :, 2], x_raw[2][:].indirect(offsets[:]))
@@ -207,14 +209,12 @@ def tile_attend_grouter_x_pl_kernel(tc, xT, W, dg, lb, ce, tx, offs, out_0, out_
 
         q, term_h, term_s = [per_tile(name, E) for name in ("q", "term_h", "term_s")]
         neg_z = per_tile("neg_z", E)
-        neg_m, tot, neg_tx_s, s_factor = [
-            per_tile(name, 1) for name in ("neg_m", "tot", "neg_tx_s", "s_factor")]
-        factors = per_tile("factors", 2)
-        divisors = per_tile("divisors", 2)
+        neg_m, tot, inv_tot, neg_inv_tot, s_sum, s_factor = [
+            per_tile(name, 1) for name in ("neg_m", "tot", "inv_tot", "neg_inv_tot", "s_sum", "s_factor")]
         g_bf = [sb("g_bf%d" % half, [P, HALF, LANES], BF16) for half in range(2)]
 
         def softmax(n):
-            neg_tx = token_factors[:, n, 0:1]
+            neg_tx = neg_tx_col[:, n:n + 1]
             bank = banks[4 + n]
             if n < DIRECT:
                 nc.vector.scalar_tensor_tensor(neg_z[n][:], bank[:], neg_tx, ce_rows[:], ALU.mult, ALU.mult)
@@ -227,13 +227,13 @@ def tile_attend_grouter_x_pl_kernel(tc, xT, W, dg, lb, ce, tx, offs, out_0, out_
                 nc.vector.tensor_scalar(neg_z[n][:], bank[:], neg_tx, None, ALU.mult, ALU.min,
                                         accum_out=neg_m[n][:])
             nc.scalar.activation(q[n][:], neg_z[n][:], ACT.Exp, bias=neg_m[n][:], scale=-1.0, accum_out=tot[n][:])
-            nc.scalar.activation(divisors[n][:], token_inverses[:, n, :], ACT.Copy, scale=tot[n][:])
 
         def terms(n):
-            nc.vector.reciprocal(factors[n][:], divisors[n][:])
-            nc.vector.scalar_tensor_tensor(term_h[n][:], q[n][:], factors[n][:, 0:1], h_tiles[n],
-                                           ALU.mult, ALU.mult, accum_out=neg_tx_s[n][:])
-            nc.scalar.activation(s_factor[n][:], neg_tx_s[n][:], ACT.Copy, scale=factors[n][:, 1:2])
+            nc.vector.reciprocal(inv_tot[n][:], tot[n][:])
+            nc.vector.scalar_tensor_tensor(term_h[n][:], q[n][:], inv_tot[n][:], h_tiles[n],
+                                           ALU.mult, ALU.mult, accum_out=s_sum[n][:])
+            nc.vector.tensor_scalar(neg_inv_tot[n][:], inv_tot[n][:], -1.0, None, ALU.mult)
+            nc.scalar.activation(s_factor[n][:], s_sum[n][:], ACT.Copy, scale=neg_inv_tot[n][:])
             nc.scalar.activation(term_s[n][:], q[n][:], ACT.Copy, scale=s_factor[n][:])
 
         def turn(n):
@@ -246,7 +246,7 @@ def tile_attend_grouter_x_pl_kernel(tc, xT, W, dg, lb, ce, tx, offs, out_0, out_
                                  start=False, stop=(t == LANES - 1), is_transpose=True)
             nc.vector.tensor_tensor(g_bf[n // 2][:, block(n % 2), :].rearrange("p (i w) t -> p i t w", w=2),
                                     bank[:].rearrange("p (t i w) -> p i t w", t=LANES, w=2),
-                                    neg_ce[:].to_broadcast([P, P // 2, LANES, 2]), ALU.mult)
+                                    scale_t[:, :, block(n)].rearrange("p t (i w) -> p i t w", w=2), ALU.mult)
 
         def quantise_g(half):
             cols = slice((half + 1) * HALF, (half + 2) * HALF)
@@ -276,7 +276,7 @@ def tile_attend_grouter_x_pl_kernel(tc, xT, W, dg, lb, ce, tx, offs, out_0, out_
 
         early = PLANE_ORDER[0:EARLY]
         planes = {PLANE_ORDER[0]: windows[0], PLANE_ORDER[1]: windows[1], PLANE_ORDER[-1]: windows[0]}
-        dx_early = [sb("dx_early%d" % k, [P, HALF], F32, tag=("x_bf", "neg_ce")[k]) for k in range(EARLY)]
+        dx_early = [sb("dx_early%d" % k, [P, HALF], F32, tag=("x_bf", "scale_t")[k]) for k in range(EARLY)]
         for k, j in enumerate(early):
             dx_pass(j, banks[6 + k], 0)
             nc.scalar.copy(dx_early[k][:], banks[6 + k][:, HALF:SLOTS])
@@ -317,15 +317,23 @@ def tile_attend_grouter_x_pl_kernel(tc, xT, W, dg, lb, ce, tx, offs, out_0, out_
         y_scales = sb("y_scales", [P, 2 * CHUNK], U8)
         words_out = out_1[0].rearrange("p x j -> p (x j)").bitcast(I32)
 
+        def pieces(c):
+            width = CHUNK // 2 if c == CHUNKS - 1 else CHUNK
+            return [slice(first, first + width) for first in range(0, CHUNK, width)]
+
         def merge(c):
             copy_words = nc.scalar.copy if c >= VECTOR_CHUNKS else nc.vector.tensor_copy
-            copy_words(y_bf[c][:].bitcast(F32).rearrange("p (x u) -> p x u", u=2),
-                       pairs[c][:].rearrange("p u x k -> p (u x k)").bitcast(F32).rearrange("p (u x) -> p x u", u=2))
+            for piece in pieces(c):
+                copy_words(y_bf[c][:].bitcast(F32).rearrange("p (x u) -> p x u", u=2)[:, piece, :],
+                           pairs[c][:].rearrange("p u x k -> p (u x k)").bitcast(F32)
+                           .rearrange("p (u x) -> p x u", u=2)[:, piece, :])
 
         def quantise_y(c):
             y_codes = sb("y_codes%d" % c, [P, CHUNK], U32)
-            nc.vector.quantize_mx(out=y_codes[:].bitcast(E4M3X4), scales=y_scales[4 * (c // 2):P, chunk(c % 2)],
-                                  in_=y_bf[c][:])
+            scales = y_scales[4 * (c // 2):P, chunk(c % 2)]
+            for piece in pieces(c):
+                nc.vector.quantize_mx(out=y_codes[:, piece].bitcast(E4M3X4), scales=scales[:, piece],
+                                      in_=y_bf[c][:, LANES * piece.start:LANES * piece.stop])
             nc.sync.dma_start(words_out[:, chunk(c)], y_codes[:].bitcast(I32))
 
         for c in range(VECTOR_CHUNKS):

@@ -92,7 +92,6 @@ def tile_attend_grouter_x_pl_kernel(tc, xT, W, dg, lb, ce, tx, offs, out_0, out_
 
         g_codes = sb("g_codes", [P, HALF + SLOTS], U32)
         g_scales = sb("g_scales", [P, HALF + SLOTS], U8)
-        windows = [sb("window%d" % k, [P, TOKENS], F32, tag=("tx_window", "")[k]) for k in range(EARLY)]
 
         w_bf = sb("w_bf", [P, E, LANES], BF16)
         w_dealt = w_bf[:].rearrange("p (t b r) j -> p t b r j", t=LANES, r=RUN)
@@ -112,8 +111,6 @@ def tile_attend_grouter_x_pl_kernel(tc, xT, W, dg, lb, ce, tx, offs, out_0, out_
         nc.vector.tensor_copy(tx_listed[:], tx_window[:].indirect(offsets[:]))
         nc.gpsimd.memset(g_codes[:, 0:HALF], 0)
         nc.gpsimd.memset(g_scales[:, 0:HALF].bitcast(U32), 0)
-        nc.vector.memset(windows[0][:].bitcast(I32), 0)
-        nc.gpsimd.memset(windows[1][:].bitcast(I32), 0)
         for n in range(SLOT_TILES):
             nc.tensor.transpose(banks[3][:, block(n)], tx_listed[:, block(n)], ident[:])
         nc.scalar.activation(neg_tx_col[:], banks[3][:, P - 1:BANK:P], ACT.Copy, scale=-1.0)
@@ -260,6 +257,9 @@ def tile_attend_grouter_x_pl_kernel(tc, xT, W, dg, lb, ce, tx, offs, out_0, out_
         terms(1)
         turn(0)
         softmax(3)
+        windows = [sb("window%d" % k, [P, TOKENS], F32, tag="dg_raw%d" % (1 - k)) for k in range(EARLY)]
+        for k in range(EARLY):
+            nc.gpsimd.memset(windows[k][:].bitcast(I32), 0)
         terms(2)
         turn(1)
         quantise_g(0)

@@ -150,18 +150,15 @@ def tile_attend_grouter_x_pl_kernel(tc, xT, W, dg, lb, ce, tx, offs, out_0, out_
         for half in range(2):
             cols = slice(half * HALF, (half + 1) * HALF)
             nc.vector.tensor_copy(x_bf[:, cols, LANES - 1], x_raw[LANES - 1][:].indirect(half_offsets[half]))
-            nc.vector.quantize_mx(out=x_codes[:, cols].bitcast(E4M3X4), scales=x_scales[:, cols],
-                                  in_=x_bf[:, cols, :].rearrange("p i j -> p (i j)"))
-        for n in range(DIRECT):
-            nc.tensor.matmul_mx(out=banks[4 + n][:], lhsT=x_codes[:, block(n)].bitcast(E4M3X4),
-                                lhsT_scale=x_scales[:, block(n)],
-                                rhs=w_d_codes[:].bitcast(E4M3X4), rhs_scale=w_d_scales[:], start=True, stop=True)
+            for part in ([block(0), block(1)], [cols])[half]:
+                nc.vector.quantize_mx(out=x_codes[:, part].bitcast(E4M3X4), scales=x_scales[:, part],
+                                      in_=x_bf[:, part, :].rearrange("p i j -> p (i j)"))
+        expert_halves = [slice(0, E // 2), slice(E // 2, E)]
+        direct_sums = [banks[0][:, expert_halves[0]], banks[4][:, expert_halves[1]]]
 
         def scores(first, width, first_bank):
             cols = slice(first, first + width)
-            per_bank = BANK // width
-            sums = [banks[first_bank + t // per_bank][:, (t % per_bank) * width:(t % per_bank + 1) * width]
-                    for t in range(LANES)]
+            sums = [banks[6 if first_bank == 1 and t >= 2 else first_bank][:, block(t)] for t in range(LANES)]
             for t in range(LANES):
                 nc.tensor.matmul_mx(out=sums[t], lhsT=w_d_codes[:, block(t)].bitcast(E4M3X4),
                                     lhsT_scale=w_d_scales[:, block(t)],
@@ -171,9 +168,16 @@ def tile_attend_grouter_x_pl_kernel(tc, xT, W, dg, lb, ce, tx, offs, out_0, out_
                 nc.scalar.activation(scaled_t[first // HALF][:, t, first % HALF:first % HALF + width], sums[t],
                                      ACT.Copy, scale=ce_col[:, t:t + 1])
 
-        for n in range(DIRECT, 2):
-            scores(n * P, P, n)
-        for n in range(2, SLOT_TILES):
+        for t in range(LANES):
+            nc.tensor.transpose(banks[0][:, block(t)], ce_col[:, t:t + 1].to_broadcast([P, P]), ident[:])
+        ce_rows = sb("ce_rows", [P, E], F32)
+        nc.scalar.copy(ce_rows[:], banks[0][:])
+        for k in range(2):
+            nc.tensor.matmul_mx(out=direct_sums[k], lhsT=x_codes[:, block(0)].bitcast(E4M3X4),
+                                lhsT_scale=x_scales[:, block(0)],
+                                rhs=w_d_codes[:, expert_halves[k]].bitcast(E4M3X4),
+                                rhs_scale=w_d_scales[:, expert_halves[k]], start=True, stop=True)
+        for n in range(DIRECT, SLOT_TILES):
             scores(n * P, P, n)
 
         w_e_codes = sb("w_e_codes", [P, D], U32, tag="x_raw1")
@@ -181,16 +185,12 @@ def tile_attend_grouter_x_pl_kernel(tc, xT, W, dg, lb, ce, tx, offs, out_0, out_
         nc.vector.quantize_mx(out=w_e_codes[:].bitcast(E4M3X4), scales=w_e_scales[:],
                               in_=wt_bf[:].rearrange("p d t -> p (d t)"))
 
-        h_all = sb("h_all", [P, SLOT_TILES, E], F32, tag="x_bf")
-        h_tiles = [h_all[:, n, :] for n in range(SLOT_TILES)]
+        h_late = sb("h_late", [P, 2, E], F32, tag="x_bf")
+        h_tiles = [sb("h0", [P, E], F32)[:], sb("h1", [P, E], F32, tag="ce_rows")[:], h_late[:, 0, :], h_late[:, 1, :]]
         for t in range(LANES):
             nc.tensor.transpose(banks[7][:, block(t)], lb_col[:, t:t + 1].to_broadcast([P, P]), ident[:])
         lb_rows = sb("lb_rows", [P, E], F32)
         nc.scalar.copy(lb_rows[:], banks[7][:])
-        for t in range(LANES):
-            nc.tensor.transpose(banks[0][:, block(t)], ce_col[:, t:t + 1].to_broadcast([P, P]), ident[:])
-        ce_rows = sb("ce_rows", [P, E], F32)
-        nc.scalar.copy(ce_rows[:], banks[0][:])
 
         def add_h(n):
             if n < VECTOR_H:
@@ -214,8 +214,9 @@ def tile_attend_grouter_x_pl_kernel(tc, xT, W, dg, lb, ce, tx, offs, out_0, out_
             neg_tx = neg_tx_col[:, n:n + 1]
             bank = banks[4 + n]
             if n < DIRECT:
-                nc.vector.scalar_tensor_tensor(neg_z[n][:], bank[:], neg_tx, ce_rows[:], ALU.mult, ALU.mult)
-                add_h(n)
+                for k in range(2):
+                    nc.vector.scalar_tensor_tensor(neg_z[n][:, expert_halves[k]], direct_sums[k], neg_tx,
+                                                   ce_rows[:, expert_halves[k]], ALU.mult, ALU.mult)
                 nc.vector.tensor_reduce(neg_m[n][:], neg_z[n][:], mybir.AxisListType.X, ALU.min)
             else:
                 add_h(n)
@@ -231,7 +232,8 @@ def tile_attend_grouter_x_pl_kernel(tc, xT, W, dg, lb, ce, tx, offs, out_0, out_
                                            ALU.mult, ALU.mult, accum_out=s_sum[n][:])
             nc.vector.tensor_scalar(neg_inv_tot[n][:], inv_tot[n][:], -1.0, None, ALU.mult)
             nc.scalar.activation(s_factor[n][:], s_sum[n][:], ACT.Copy, scale=neg_inv_tot[n][:])
-            nc.scalar.activation(term_s[n][:], q[n][:], ACT.Copy, scale=s_factor[n][:])
+            for cols in expert_halves:
+                nc.scalar.activation(term_s[n][:, cols], q[n][:, cols], ACT.Copy, scale=s_factor[n][:])
 
         def turn(n):
             bank = banks[n]
@@ -245,11 +247,13 @@ def tile_attend_grouter_x_pl_kernel(tc, xT, W, dg, lb, ce, tx, offs, out_0, out_
                                     bank[:].rearrange("p (t i w) -> p i t w", t=LANES, w=2),
                                     scale_t[:, :, block(n)].rearrange("p t (i w) -> p i t w", w=2), ALU.mult)
 
-        def quantise_g(half):
-            cols = slice((half + 1) * HALF, (half + 2) * HALF)
+        def quantise_g(first, width):
+            cols = slice(HALF + first, HALF + first + width)
             nc.vector.quantize_mx(out=g_codes[:, cols].bitcast(E5M2X4), scales=g_scales[:, cols],
-                                  in_=g_bf[half][:].rearrange("p i t -> p (i t)"))
+                                  in_=g_bf[first // HALF][:, first % HALF:first % HALF + width, :]
+                                  .rearrange("p i t -> p (i t)"))
 
+        add_h(0)
         softmax(0)
         softmax(1)
         terms(0)
@@ -262,10 +266,11 @@ def tile_attend_grouter_x_pl_kernel(tc, xT, W, dg, lb, ce, tx, offs, out_0, out_
             nc.gpsimd.memset(windows[k][:].bitcast(I32), 0)
         terms(2)
         turn(1)
-        quantise_g(0)
+        quantise_g(0, HALF)
         terms(3)
         turn(2)
         turn(3)
+        quantise_g(2 * P, P)
 
         def dx_pass(j, bank, first):
             cols = slice(first, first + SLOTS)
@@ -281,7 +286,7 @@ def tile_attend_grouter_x_pl_kernel(tc, xT, W, dg, lb, ce, tx, offs, out_0, out_
             dx_pass(j, banks[6 + k], 0)
             nc.scalar.copy(dx_early[k][:], banks[6 + k][:, HALF:SLOTS])
         nc.vector.tensor_copy(planes[early[0]][:].indirect(half_offsets[0]), dx_early[0][:])
-        quantise_g(1)
+        quantise_g(3 * P, P)
         nc.vector.tensor_copy(planes[early[1]][:].indirect(half_offsets[0]), dx_early[1][:])
         dx = [sb("dx%d" % j, [P, SLOTS], F32) for j in range(LANES)]
         for step, j in enumerate(PLANE_ORDER):

@@ -27,10 +27,9 @@ SLOT_TILES = SLOTS // P
 LIST_ROWS = 16
 CHUNK = 512
 CHUNKS = TOKENS // CHUNK
-VECTOR_CHUNKS = CHUNKS // 2
-WINDOWS = 3
-PLANE_ORDER = (2, 0, 1, 3)
-EARLY = 2
+ROUNDER = {(0, 0): "gpsimd", (0, 1): "gpsimd", (0, 2): "gpsimd", (0, 3): "scalar",
+           (1, 0): "vector", (1, 1): "vector", (1, 2): "vector", (1, 3): "scalar"}
+VECTOR_MERGES = 2
 X_ORDER = (2, 0, 1, 3)
 DIRECT = 1
 VECTOR_H = 2
@@ -90,9 +89,6 @@ def tile_attend_grouter_x_pl_kernel(tc, xT, W, dg, lb, ce, tx, offs, out_0, out_
             nc.sync.dma_start(dg_raw[half][:],
                               dg[half * HALF:(half + 1) * HALF, :].rearrange("(n p) e -> p n e", p=P))
 
-        g_codes = sb("g_codes", [P, HALF + SLOTS], U32)
-        g_scales = sb("g_scales", [P, HALF + SLOTS], U8)
-
         w_bf = sb("w_bf", [P, E, LANES], BF16)
         w_dealt = w_bf[:].rearrange("p (t b r) j -> p t b r j", t=LANES, r=RUN)
         w_natural = w_raw[:].rearrange("p j (b t r) -> p t b r j", t=LANES, r=RUN)
@@ -109,8 +105,8 @@ def tile_attend_grouter_x_pl_kernel(tc, xT, W, dg, lb, ce, tx, offs, out_0, out_
         nc.scalar.copy(lb_col[:], banks[2][:, P - 2:BANK:P])
         tx_listed = sb("tx_listed", [P, SLOTS], F32)
         nc.vector.tensor_copy(tx_listed[:], tx_window[:].indirect(offsets[:]))
-        nc.gpsimd.memset(g_codes[:, 0:HALF], 0)
-        nc.gpsimd.memset(g_scales[:, 0:HALF].bitcast(U32), 0)
+        windows = {2: sb("window2", [P, TOKENS], F32, tag="tx_window")}
+        nc.vector.memset(windows[2][:].bitcast(I32), 0)
         for n in range(SLOT_TILES):
             nc.tensor.transpose(banks[3][:, block(n)], tx_listed[:, block(n)], ident[:])
         nc.scalar.activation(neg_tx_col[:], banks[3][:, P - 1:BANK:P], ACT.Copy, scale=-1.0)
@@ -247,8 +243,11 @@ def tile_attend_grouter_x_pl_kernel(tc, xT, W, dg, lb, ce, tx, offs, out_0, out_
                                     bank[:].rearrange("p (t i w) -> p i t w", t=LANES, w=2),
                                     scale_t[:, :, block(n)].rearrange("p t (i w) -> p i t w", w=2), ALU.mult)
 
+        g_codes = sb("g_codes", [P, SLOTS], U32)
+        g_scales = sb("g_scales", [P, SLOTS], U8)
+
         def quantise_g(first, width):
-            cols = slice(HALF + first, HALF + first + width)
+            cols = slice(first, first + width)
             nc.vector.quantize_mx(out=g_codes[:, cols].bitcast(E5M2X4), scales=g_scales[:, cols],
                                   in_=g_bf[first // HALF][:, first % HALF:first % HALF + width, :]
                                   .rearrange("p i t -> p (i t)"))
@@ -261,9 +260,9 @@ def tile_attend_grouter_x_pl_kernel(tc, xT, W, dg, lb, ce, tx, offs, out_0, out_
         terms(1)
         turn(0)
         softmax(3)
-        windows = [sb("window%d" % k, [P, TOKENS], F32, tag="dg_raw%d" % (1 - k)) for k in range(EARLY)]
-        for k in range(EARLY):
-            nc.gpsimd.memset(windows[k][:].bitcast(I32), 0)
+        for j in range(2):
+            windows[j] = sb("window%d" % j, [P, TOKENS], F32, tag="dg_raw%d" % (1 - j))
+            nc.gpsimd.memset(windows[j][:].bitcast(I32), 0)
         terms(2)
         turn(1)
         quantise_g(0, HALF)
@@ -272,83 +271,93 @@ def tile_attend_grouter_x_pl_kernel(tc, xT, W, dg, lb, ce, tx, offs, out_0, out_
         turn(3)
         quantise_g(2 * P, P)
 
-        def dx_pass(j, bank, first):
-            cols = slice(first, first + SLOTS)
-            nc.tensor.matmul_mx(out=bank[:], lhsT=w_e_codes[:, block(j)].bitcast(E4M3X4),
+        halves = [slice(0, HALF), slice(HALF, SLOTS)]
+
+        def dx_pass(j, bank, cols):
+            nc.tensor.matmul_mx(out=bank[:, cols], lhsT=w_e_codes[:, block(j)].bitcast(E4M3X4),
                                 lhsT_scale=w_e_scales[:, block(j)],
                                 rhs=g_codes[:, cols].bitcast(E5M2X4), rhs_scale=g_scales[:, cols],
                                 start=True, stop=True)
 
-        early = PLANE_ORDER[0:EARLY]
-        planes = {PLANE_ORDER[0]: windows[0], PLANE_ORDER[1]: windows[1], PLANE_ORDER[-1]: windows[0]}
-        dx_early = [sb("dx_early%d" % k, [P, HALF], F32, tag=("x_bf", "scale_t")[k]) for k in range(EARLY)]
-        for k, j in enumerate(early):
-            dx_pass(j, banks[6 + k], 0)
-            nc.scalar.copy(dx_early[k][:], banks[6 + k][:, HALF:SLOTS])
-        nc.vector.tensor_copy(planes[early[0]][:].indirect(half_offsets[0]), dx_early[0][:])
-        quantise_g(3 * P, P)
-        nc.vector.tensor_copy(planes[early[1]][:].indirect(half_offsets[0]), dx_early[1][:])
-        dx = [sb("dx%d" % j, [P, SLOTS], F32) for j in range(LANES)]
-        for step, j in enumerate(PLANE_ORDER):
-            first = HALF if j in early else 0
-            dx_pass(j, banks[4 + step], HALF)
-            nc.scalar.copy(dx[j][:, first:SLOTS], banks[4 + step][:, first:SLOTS])
+        def scatter(j, half, values):
+            window = windows[j][:].indirect(half_offsets[half])
+            if j % 2:
+                nc.scalar.activation(window, values, ACT.Copy)
+            else:
+                nc.vector.tensor_copy(window, values)
 
-        third = PLANE_ORDER[EARLY]
-        planes[third] = sb("window_late", [P, TOKENS], F32, tag="g_bf1")
-        nc.gpsimd.memset(planes[third][:].bitcast(I32), 0)
+        dx_first = {}
+        for j, tag in ((1, "q3"), (0, "scale_t")):
+            dx_first[j] = sb("dx_first%d" % j, [P, HALF], F32, tag=tag)
+            dx_pass(j, banks[6 + j], halves[0])
+            nc.vector.tensor_copy(dx_first[j][:], banks[6 + j][:, halves[0]])
+        scatter(1, 0, dx_first[1][:])
+        quantise_g(3 * P, P)
+        scatter(0, 0, dx_first[0][:])
+        windows[3] = sb("window3", [P, TOKENS], F32, tag="g_bf1")
+        nc.gpsimd.memset(windows[3][:].bitcast(I32), 0)
 
         out_rows = out_0.rearrange("(p j) x -> j p x", j=LANES)
-        pairs = [sb("pairs%d" % c, [P, 2, CHUNK, 2], BF16) for c in range(CHUNKS)]
+        for j, bank in ((1, banks[4]), (0, banks[0]), (3, banks[2]), (2, banks[1])):
+            cols = halves[1] if j in dx_first else slice(0, SLOTS)
+            dx = sb("dx%d" % j, [P, SLOTS], F32, tag="dx_scalar" if j % 2 else "")
+            dx_pass(j, bank, cols)
+            copy_out = nc.scalar.copy if j % 2 else nc.vector.tensor_copy
+            copy_out(dx[:, cols], bank[:, cols])
+            if j == 2:
+                nc.vector.tensor_copy(windows[j][:].indirect(offsets[:]), dx[:])
+            else:
+                for half in range(cols.start // HALF, 2):
+                    scatter(j, half, dx[:, halves[half]])
+            nc.sync.dma_start(out_rows[j], windows[j][:])
+
+        pairs = [sb("pairs%d" % c, [P, 2, CHUNK, 2], BF16, tag="dx_scalar" if c == CHUNKS - 1 else "")
+                 for c in range(CHUNKS)]
 
         def chunk(c):
             return slice(c * CHUNK, (c + 1) * CHUNK)
 
-        last = PLANE_ORDER[-1]
-        for j in PLANE_ORDER:
-            if j in early:
-                nc.vector.tensor_copy(planes[j][:].indirect(half_offsets[1]), dx[j][:, HALF:SLOTS])
+        def round_plane(j, c):
+            rounded, values = pairs[c][:, j // 2, :, j % 2], windows[j][:, chunk(c)]
+            engine = ROUNDER[j // 2, c]
+            if engine == "gpsimd":
+                nc.gpsimd.tensor_scalar(rounded, values, 1.0, 0.0, ALU.mult, ALU.add)
+            elif engine == "scalar":
+                nc.scalar.copy(rounded, values)
             else:
-                nc.vector.tensor_copy(planes[j][:].indirect(offsets[:]), dx[j][:])
-            nc.sync.dma_start(out_rows[j], planes[j][:])
-            if j != last:
-                for c in range(VECTOR_CHUNKS):
-                    nc.scalar.copy(pairs[c][:, j // 2, :, j % 2], planes[j][:, chunk(c)])
-                for c in range(VECTOR_CHUNKS, CHUNKS):
-                    nc.gpsimd.tensor_scalar(pairs[c][:, j // 2, :, j % 2], planes[j][:, chunk(c)],
-                                            1.0, 0.0, ALU.mult, ALU.add)
+                nc.vector.tensor_copy(rounded, values)
 
         y_bf = [sb("y_bf%d" % c, [P, CHUNK * LANES], BF16) for c in range(CHUNKS)]
+        y_codes = sb("y_codes", [P, TOKENS], U32)
         y_scales = sb("y_scales", [P, 2 * CHUNK], U8)
         words_out = out_1[0].rearrange("p x j -> p (x j)").bitcast(I32)
 
         def pieces(c):
-            width = CHUNK // 2 if c == CHUNKS - 1 else CHUNK
+            width = CHUNK // 2 if c == 2 else CHUNK
             return [slice(first, first + width) for first in range(0, CHUNK, width)]
 
         def merge(c):
-            copy_words = nc.scalar.copy if c >= VECTOR_CHUNKS else nc.vector.tensor_copy
+            copy_words = nc.scalar.copy if c >= VECTOR_MERGES else nc.vector.tensor_copy
             for piece in pieces(c):
                 copy_words(y_bf[c][:].bitcast(F32).rearrange("p (x u) -> p x u", u=2)[:, piece, :],
                            pairs[c][:].rearrange("p u x k -> p (u x k)").bitcast(F32)
                            .rearrange("p (u x) -> p x u", u=2)[:, piece, :])
 
         def quantise_y(c):
-            y_codes = sb("y_codes%d" % c, [P, CHUNK], U32)
             scales = y_scales[4 * (c // 2):P, chunk(c % 2)]
             for piece in pieces(c):
-                nc.vector.quantize_mx(out=y_codes[:, piece].bitcast(E4M3X4), scales=scales[:, piece],
+                nc.vector.quantize_mx(out=y_codes[:, chunk(c)][:, piece].bitcast(E4M3X4), scales=scales[:, piece],
                                       in_=y_bf[c][:, LANES * piece.start:LANES * piece.stop])
-            nc.sync.dma_start(words_out[:, chunk(c)], y_codes[:].bitcast(I32))
+            if c > 0:
+                cols = slice(0, 2 * CHUNK) if c == 1 else chunk(c)
+                nc.sync.dma_start(words_out[:, cols], y_codes[:, cols].bitcast(I32))
 
-        for c in range(VECTOR_CHUNKS):
-            nc.vector.tensor_copy(pairs[c][:, last // 2, :, last % 2], planes[last][:, chunk(c)])
-        for c in range(VECTOR_CHUNKS):
+        for j in (1, 0, 3, 2):
+            for c in range(CHUNKS):
+                round_plane(j, c)
+        for c in (0, 1, 3, 2):
             merge(c)
-        for c in range(VECTOR_CHUNKS, CHUNKS):
-            nc.scalar.copy(pairs[c][:, last // 2, :, last % 2], planes[last][:, chunk(c)])
-            merge(c)
-        for c in range(CHUNKS):
+        for c in (0, 1, 3, 2):
             quantise_y(c)
         for quad in range(QUADRANTS):
             queue = nc.sync if quad % 2 == 0 else nc.scalar

@@ -28,8 +28,9 @@ LIST_ROWS = 16
 CHUNK = 512
 CHUNKS = TOKENS // CHUNK
 ROUNDER = {(0, 0): "gpsimd", (0, 1): "gpsimd", (0, 2): "gpsimd", (0, 3): "scalar",
-           (1, 0): "vector", (1, 1): "vector", (1, 2): "vector", (1, 3): "scalar"}
-VECTOR_MERGES = 2
+           (1, 0): "vector", (1, 1): "scalar", (1, 2): "scalar", (1, 3): "scalar"}
+SCALAR_PLANE = 1
+VECTOR_MERGES = 3
 X_ORDER = (2, 0, 1, 3)
 DIRECT = 1
 VECTOR_H = 2
@@ -105,8 +106,6 @@ def tile_attend_grouter_x_pl_kernel(tc, xT, W, dg, lb, ce, tx, offs, out_0, out_
         nc.scalar.copy(lb_col[:], banks[2][:, P - 2:BANK:P])
         tx_listed = sb("tx_listed", [P, SLOTS], F32)
         nc.vector.tensor_copy(tx_listed[:], tx_window[:].indirect(offsets[:]))
-        windows = {2: sb("window2", [P, TOKENS], F32, tag="tx_window")}
-        nc.vector.memset(windows[2][:].bitcast(I32), 0)
         for n in range(SLOT_TILES):
             nc.tensor.transpose(banks[3][:, block(n)], tx_listed[:, block(n)], ident[:])
         nc.scalar.activation(neg_tx_col[:], banks[3][:, P - 1:BANK:P], ACT.Copy, scale=-1.0)
@@ -252,6 +251,12 @@ def tile_attend_grouter_x_pl_kernel(tc, xT, W, dg, lb, ce, tx, offs, out_0, out_
                                   in_=g_bf[first // HALF][:, first % HALF:first % HALF + width, :]
                                   .rearrange("p i t -> p (i t)"))
 
+        windows = {}
+
+        def clear_window(j, tag):
+            windows[j] = sb("window%d" % j, [P, TOKENS], F32, tag=tag)
+            nc.gpsimd.memset(windows[j][:].bitcast(I32), 0)
+
         add_h(0)
         softmax(0)
         softmax(1)
@@ -260,9 +265,8 @@ def tile_attend_grouter_x_pl_kernel(tc, xT, W, dg, lb, ce, tx, offs, out_0, out_
         terms(1)
         turn(0)
         softmax(3)
-        for j in range(2):
-            windows[j] = sb("window%d" % j, [P, TOKENS], F32, tag="dg_raw%d" % (1 - j))
-            nc.gpsimd.memset(windows[j][:].bitcast(I32), 0)
+        clear_window(0, "dg_raw1")
+        clear_window(1, "dg_raw0")
         terms(2)
         turn(1)
         quantise_g(0, HALF)
@@ -281,37 +285,41 @@ def tile_attend_grouter_x_pl_kernel(tc, xT, W, dg, lb, ce, tx, offs, out_0, out_
 
         def scatter(j, half, values):
             window = windows[j][:].indirect(half_offsets[half])
-            if j % 2:
+            if j == SCALAR_PLANE:
                 nc.scalar.activation(window, values, ACT.Copy)
             else:
                 nc.vector.tensor_copy(window, values)
 
-        dx_first = {}
-        for j, tag in ((1, "q3"), (0, "scale_t")):
-            dx_first[j] = sb("dx_first%d" % j, [P, HALF], F32, tag=tag)
-            dx_pass(j, banks[6 + j], halves[0])
-            nc.vector.tensor_copy(dx_first[j][:], banks[6 + j][:, halves[0]])
+        dx_first = [sb("dx_first%d" % j, [P, HALF], F32, tag=tag) for j, tag in enumerate(("scale_t", "q3"))]
+        dx_pass(1, banks[7], halves[0])
+        nc.scalar.copy(dx_first[1][:], banks[7][:, halves[0]])
         scatter(1, 0, dx_first[1][:])
+        dx_pass(0, banks[6], halves[0])
+        nc.vector.tensor_copy(dx_first[0][:], banks[6][:, halves[0]])
         quantise_g(3 * P, P)
         scatter(0, 0, dx_first[0][:])
-        windows[3] = sb("window3", [P, TOKENS], F32, tag="g_bf1")
-        nc.gpsimd.memset(windows[3][:].bitcast(I32), 0)
+        clear_window(2, "g_bf1")
 
+        dx_second = [sb("dx_second%d" % j, [P, HALF], F32) for j in range(2)]
+        dx_whole = {j: sb("dx_whole%d" % j, [P, SLOTS], F32) for j in (2, 3)}
         out_rows = out_0.rearrange("(p j) x -> j p x", j=LANES)
-        for j, bank in ((1, banks[4]), (0, banks[0]), (3, banks[2]), (2, banks[1])):
-            cols = halves[1] if j in dx_first else slice(0, SLOTS)
-            dx = sb("dx%d" % j, [P, SLOTS], F32, tag="dx_scalar" if j % 2 else "")
-            dx_pass(j, bank, cols)
-            copy_out = nc.scalar.copy if j % 2 else nc.vector.tensor_copy
-            copy_out(dx[:, cols], bank[:, cols])
-            if j == 2:
-                nc.vector.tensor_copy(windows[j][:].indirect(offsets[:]), dx[:])
-            else:
-                for half in range(cols.start // HALF, 2):
-                    scatter(j, half, dx[:, halves[half]])
+        dx_pass(0, banks[4], halves[1])
+        nc.scalar.copy(dx_second[0][:], banks[4][:, halves[1]])
+        dx_pass(2, banks[0], slice(0, SLOTS))
+        nc.scalar.copy(dx_whole[2][:], banks[0][:])
+        dx_pass(1, banks[1], halves[1])
+        nc.scalar.copy(dx_second[1][:], banks[1][:, halves[1]])
+        for j in (0, 1):
+            scatter(j, 1, dx_second[j][:])
+            nc.sync.dma_start(out_rows[j], windows[j][:])
+        dx_pass(3, banks[2], slice(0, SLOTS))
+        nc.scalar.copy(dx_whole[3][:], banks[2][:])
+        clear_window(3, "g_scales")
+        for j in (2, 3):
+            nc.vector.tensor_copy(windows[j][:].indirect(offsets[:]), dx_whole[j][:])
             nc.sync.dma_start(out_rows[j], windows[j][:])
 
-        pairs = [sb("pairs%d" % c, [P, 2, CHUNK, 2], BF16, tag="dx_scalar" if c == CHUNKS - 1 else "")
+        pairs = [sb("pairs%d" % c, [P, 2, CHUNK, 2], BF16, tag="dx_second1" if c == CHUNKS - 1 else "")
                  for c in range(CHUNKS)]
 
         def chunk(c):
@@ -333,7 +341,7 @@ def tile_attend_grouter_x_pl_kernel(tc, xT, W, dg, lb, ce, tx, offs, out_0, out_
         words_out = out_1[0].rearrange("p x j -> p (x j)").bitcast(I32)
 
         def pieces(c):
-            width = CHUNK // 2 if c == 2 else CHUNK
+            width = CHUNK // 2 if c == CHUNKS - 1 else CHUNK
             return [slice(first, first + width) for first in range(0, CHUNK, width)]
 
         def merge(c):
@@ -352,12 +360,12 @@ def tile_attend_grouter_x_pl_kernel(tc, xT, W, dg, lb, ce, tx, offs, out_0, out_
                 cols = slice(0, 2 * CHUNK) if c == 1 else chunk(c)
                 nc.sync.dma_start(words_out[:, cols], y_codes[:, cols].bitcast(I32))
 
-        for j in (1, 0, 3, 2):
+        for j in range(LANES):
             for c in range(CHUNKS):
                 round_plane(j, c)
-        for c in (0, 1, 3, 2):
+        for c in range(CHUNKS):
             merge(c)
-        for c in (0, 1, 3, 2):
+        for c in range(CHUNKS):
             quantise_y(c)
         for quad in range(QUADRANTS):
             queue = nc.sync if quad % 2 == 0 else nc.scalar

@@ -27,8 +27,6 @@ SLOT_TILES = SLOTS // P
 LIST_ROWS = 16
 CHUNK = 512
 CHUNKS = TOKENS // CHUNK
-ROUNDER = {(0, 0): "gpsimd", (0, 1): "gpsimd", (0, 2): "gpsimd", (0, 3): "scalar",
-           (1, 0): "vector", (1, 1): "scalar", (1, 2): "scalar", (1, 3): "scalar"}
 SCALAR_PLANE = 1
 VECTOR_MERGES = 3
 X_ORDER = (2, 0, 1, 3)
@@ -106,6 +104,11 @@ def tile_attend_grouter_x_pl_kernel(tc, xT, W, dg, lb, ce, tx, offs, out_0, out_
         nc.scalar.copy(lb_col[:], banks[2][:, P - 2:BANK:P])
         tx_listed = sb("tx_listed", [P, SLOTS], F32)
         nc.vector.tensor_copy(tx_listed[:], tx_window[:].indirect(offsets[:]))
+        windows = {}
+
+        def clear_window(j, tag):
+            windows[j] = sb("window%d" % j, [P, TOKENS], F32, tag=tag)
+            nc.gpsimd.memset(windows[j][:].bitcast(I32), 0)
         for n in range(SLOT_TILES):
             nc.tensor.transpose(banks[3][:, block(n)], tx_listed[:, block(n)], ident[:])
         nc.scalar.activation(neg_tx_col[:], banks[3][:, P - 1:BANK:P], ACT.Copy, scale=-1.0)
@@ -251,12 +254,6 @@ def tile_attend_grouter_x_pl_kernel(tc, xT, W, dg, lb, ce, tx, offs, out_0, out_
                                   in_=g_bf[first // HALF][:, first % HALF:first % HALF + width, :]
                                   .rearrange("p i t -> p (i t)"))
 
-        windows = {}
-
-        def clear_window(j, tag):
-            windows[j] = sb("window%d" % j, [P, TOKENS], F32, tag=tag)
-            nc.gpsimd.memset(windows[j][:].bitcast(I32), 0)
-
         add_h(0)
         softmax(0)
         softmax(1)
@@ -319,21 +316,24 @@ def tile_attend_grouter_x_pl_kernel(tc, xT, W, dg, lb, ce, tx, offs, out_0, out_
             nc.vector.tensor_copy(windows[j][:].indirect(offsets[:]), dx_whole[j][:])
             nc.sync.dma_start(out_rows[j], windows[j][:])
 
-        pairs = [sb("pairs%d" % c, [P, 2, CHUNK, 2], BF16, tag="dx_second1" if c == CHUNKS - 1 else "")
-                 for c in range(CHUNKS)]
+        front = (CHUNKS - 1) * CHUNK
+        pairs_front = sb("pairs_front", [P, 2, front, 2], BF16)
+        pairs_last = sb("pairs_last", [P, 2, CHUNK, 2], BF16, tag="dx_second1")
 
         def chunk(c):
             return slice(c * CHUNK, (c + 1) * CHUNK)
 
-        def round_plane(j, c):
-            rounded, values = pairs[c][:, j // 2, :, j % 2], windows[j][:, chunk(c)]
-            engine = ROUNDER[j // 2, c]
-            if engine == "gpsimd":
-                nc.gpsimd.tensor_scalar(rounded, values, 1.0, 0.0, ALU.mult, ALU.add)
-            elif engine == "scalar":
-                nc.scalar.copy(rounded, values)
+        def pairs(c):
+            return pairs_last[:] if c == CHUNKS - 1 else pairs_front[:, :, chunk(c), :]
+
+        def round_plane(j):
+            u, k = divmod(j, 2)
+            if u == 0:
+                nc.gpsimd.tensor_scalar(pairs_front[:, u, :, k], windows[j][:, 0:front], 1.0, 0.0, ALU.mult, ALU.add)
             else:
-                nc.vector.tensor_copy(rounded, values)
+                nc.vector.tensor_copy(pairs(0)[:, u, :, k], windows[j][:, chunk(0)])
+            for c in range(1 if u else CHUNKS - 1, CHUNKS):
+                nc.scalar.copy(pairs(c)[:, u, :, k], windows[j][:, chunk(c)])
 
         y_bf = [sb("y_bf%d" % c, [P, CHUNK * LANES], BF16) for c in range(CHUNKS)]
         y_codes = sb("y_codes", [P, TOKENS], U32)
@@ -348,8 +348,8 @@ def tile_attend_grouter_x_pl_kernel(tc, xT, W, dg, lb, ce, tx, offs, out_0, out_
             copy_words = nc.scalar.copy if c >= VECTOR_MERGES else nc.vector.tensor_copy
             for piece in pieces(c):
                 copy_words(y_bf[c][:].bitcast(F32).rearrange("p (x u) -> p x u", u=2)[:, piece, :],
-                           pairs[c][:].rearrange("p u x k -> p (u x k)").bitcast(F32)
-                           .rearrange("p (u x) -> p x u", u=2)[:, piece, :])
+                           pairs(c).rearrange("p u x k -> p u (x k)").bitcast(F32)
+                           .rearrange("p u x -> p x u")[:, piece, :])
 
         def quantise_y(c):
             scales = y_scales[4 * (c // 2):P, chunk(c % 2)]
@@ -361,8 +361,7 @@ def tile_attend_grouter_x_pl_kernel(tc, xT, W, dg, lb, ce, tx, offs, out_0, out_
                 nc.sync.dma_start(words_out[:, cols], y_codes[:, cols].bitcast(I32))
 
         for j in range(LANES):
-            for c in range(CHUNKS):
-                round_plane(j, c)
+            round_plane(j)
         for c in range(CHUNKS):
             merge(c)
         for c in range(CHUNKS):

@@ -298,26 +298,27 @@ def tile_attend_grouter_x_pl_kernel(tc, xT, W, dg, lb, ce, tx, offs, out_0, out_
         clear_window(2, "g_bf1")
 
         dx_second = [sb("dx_second%d" % j, [P, HALF], F32) for j in range(2)]
-        dx_whole = {j: sb("dx_whole%d" % j, [P, SLOTS], F32) for j in (2, 3)}
+        front = (CHUNKS - 1) * CHUNK
+        pairs_front = sb("pairs_front", [P, 2, front, 2], BF16)
+        dx_whole = {2: sb("dx_whole2", [P, SLOTS], F32)[:],
+                    3: pairs_front[:, 1, 0:CHUNK, :].rearrange("p x k -> p (x k)").bitcast(F32)}
         out_rows = out_0.rearrange("(p j) x -> j p x", j=LANES)
         dx_pass(0, banks[4], halves[1])
         nc.scalar.copy(dx_second[0][:], banks[4][:, halves[1]])
         dx_pass(2, banks[0], slice(0, SLOTS))
-        nc.scalar.copy(dx_whole[2][:], banks[0][:])
+        nc.scalar.copy(dx_whole[2], banks[0][:])
         dx_pass(1, banks[1], halves[1])
         nc.scalar.copy(dx_second[1][:], banks[1][:, halves[1]])
         for j in (0, 1):
             scatter(j, 1, dx_second[j][:])
             nc.sync.dma_start(out_rows[j], windows[j][:])
         dx_pass(3, banks[2], slice(0, SLOTS))
-        nc.scalar.copy(dx_whole[3][:], banks[2][:])
+        nc.scalar.copy(dx_whole[3], banks[2][:])
         clear_window(3, "g_scales")
         for j in (2, 3):
-            nc.vector.tensor_copy(windows[j][:].indirect(offsets[:]), dx_whole[j][:])
+            nc.vector.tensor_copy(windows[j][:].indirect(offsets[:]), dx_whole[j])
             nc.sync.dma_start(out_rows[j], windows[j][:])
 
-        front = (CHUNKS - 1) * CHUNK
-        pairs_front = sb("pairs_front", [P, 2, front, 2], BF16)
         pairs_last = sb("pairs_last", [P, 2, CHUNK, 2], BF16, tag="dx_second1")
 
         def chunk(c):

@@ -28,6 +28,8 @@ LIST_ROWS = 16
 CHUNK = 512
 CHUNKS = TOKENS // CHUNK
 SCALAR_PLANE = 1
+GPSIMD_COLUMNS = 1792
+VECTOR_COLUMNS = 256
 VECTOR_MERGES = 3
 X_ORDER = (2, 0, 1, 3)
 DIRECT = 1
@@ -109,6 +111,8 @@ def tile_attend_grouter_x_pl_kernel(tc, xT, W, dg, lb, ce, tx, offs, out_0, out_
         def clear_window(j, tag):
             windows[j] = sb("window%d" % j, [P, TOKENS], F32, tag=tag)
             nc.gpsimd.memset(windows[j][:].bitcast(I32), 0)
+
+        clear_window(1, "expert_rows")
         for n in range(SLOT_TILES):
             nc.tensor.transpose(banks[3][:, block(n)], tx_listed[:, block(n)], ident[:])
         nc.scalar.activation(neg_tx_col[:], banks[3][:, P - 1:BANK:P], ACT.Copy, scale=-1.0)
@@ -137,7 +141,7 @@ def tile_attend_grouter_x_pl_kernel(tc, xT, W, dg, lb, ce, tx, offs, out_0, out_
             nc.scalar.copy(wt_bf[:, 2 * P * u:2 * P * (u + 1), :].rearrange("p (k v w) t -> p v t w k", k=2, w=2),
                            banks[5 + u][:].bitcast(BF16).rearrange("p (t v w k) -> p v t w k", t=LANES, w=2, k=2))
 
-        w_d_codes = sb("w_d_codes", [P, E], U32, tag="x_raw0")
+        w_d_codes = sb("w_d_codes", [P, E], U32)
         w_d_scales = sb("w_d_scales", [P, E], U8)
         nc.vector.quantize_mx(out=w_d_codes[:].bitcast(E4M3X4), scales=w_d_scales[:],
                               in_=w_bf[:].rearrange("p e j -> p (e j)"))
@@ -178,10 +182,11 @@ def tile_attend_grouter_x_pl_kernel(tc, xT, W, dg, lb, ce, tx, offs, out_0, out_
         for n in range(DIRECT, SLOT_TILES):
             scores(n * P, P, n)
 
-        w_e_codes = sb("w_e_codes", [P, D], U32, tag="x_raw1")
+        w_e_codes = sb("w_e_codes", [P, D], U32)
         w_e_scales = sb("w_e_scales", [P, D], U8)
         nc.vector.quantize_mx(out=w_e_codes[:].bitcast(E4M3X4), scales=w_e_scales[:],
                               in_=wt_bf[:].rearrange("p d t -> p (d t)"))
+        clear_window(0, "wt_bf")
 
         h_late = sb("h_late", [P, 2, E], F32, tag="x_bf")
         h_tiles = [sb("h0", [P, E], F32)[:], sb("h1", [P, E], F32, tag="ce_rows")[:], h_late[:, 0, :], h_late[:, 1, :]]
@@ -262,8 +267,7 @@ def tile_attend_grouter_x_pl_kernel(tc, xT, W, dg, lb, ce, tx, offs, out_0, out_
         terms(1)
         turn(0)
         softmax(3)
-        clear_window(0, "dg_raw1")
-        clear_window(1, "dg_raw0")
+        clear_window(2, "dg_raw1")
         terms(2)
         turn(1)
         quantise_g(0, HALF)
@@ -295,13 +299,12 @@ def tile_attend_grouter_x_pl_kernel(tc, xT, W, dg, lb, ce, tx, offs, out_0, out_
         nc.vector.tensor_copy(dx_first[0][:], banks[6][:, halves[0]])
         quantise_g(3 * P, P)
         scatter(0, 0, dx_first[0][:])
-        clear_window(2, "g_bf1")
 
         dx_second = [sb("dx_second%d" % j, [P, HALF], F32) for j in range(2)]
-        front = (CHUNKS - 1) * CHUNK
-        pairs_front = sb("pairs_front", [P, 2, front, 2], BF16)
+        spare = SLOTS - VECTOR_COLUMNS
+        pairs = sb("pairs", [P, 2, TOKENS + spare, 2], BF16)
         dx_whole = {2: sb("dx_whole2", [P, SLOTS], F32)[:],
-                    3: pairs_front[:, 1, 0:CHUNK, :].rearrange("p x k -> p (x k)").bitcast(F32)}
+                    3: pairs[:].rearrange("p u x k -> p (u x k)").bitcast(F32)[:, TOKENS:TOKENS + SLOTS]}
         out_rows = out_0.rearrange("(p j) x -> j p x", j=LANES)
         dx_pass(0, banks[4], halves[1])
         nc.scalar.copy(dx_second[0][:], banks[4][:, halves[1]])
@@ -319,22 +322,22 @@ def tile_attend_grouter_x_pl_kernel(tc, xT, W, dg, lb, ce, tx, offs, out_0, out_
             nc.vector.tensor_copy(windows[j][:].indirect(offsets[:]), dx_whole[j])
             nc.sync.dma_start(out_rows[j], windows[j][:])
 
-        pairs_last = sb("pairs_last", [P, 2, CHUNK, 2], BF16, tag="dx_second1")
-
         def chunk(c):
             return slice(c * CHUNK, (c + 1) * CHUNK)
-
-        def pairs(c):
-            return pairs_last[:] if c == CHUNKS - 1 else pairs_front[:, :, chunk(c), :]
 
         def round_plane(j):
             u, k = divmod(j, 2)
             if u == 0:
-                nc.gpsimd.tensor_scalar(pairs_front[:, u, :, k], windows[j][:, 0:front], 1.0, 0.0, ALU.mult, ALU.add)
+                front, back = slice(0, GPSIMD_COLUMNS), slice(GPSIMD_COLUMNS, TOKENS)
+                nc.gpsimd.tensor_scalar(pairs[:, u, front, k], windows[j][:, front], 1.0, 0.0, ALU.mult, ALU.add)
+                nc.scalar.copy(pairs[:, u, back, k], windows[j][:, back])
             else:
-                nc.vector.tensor_copy(pairs(0)[:, u, :, k], windows[j][:, chunk(0)])
-            for c in range(1 if u else CHUNKS - 1, CHUNKS):
-                nc.scalar.copy(pairs(c)[:, u, :, k], windows[j][:, chunk(c)])
+                nc.vector.tensor_copy(pairs[:, u, 0:VECTOR_COLUMNS, k], windows[j][:, 0:VECTOR_COLUMNS])
+                ends = range(CHUNK, TOKENS + 1, CHUNK) if j == LANES - 1 else [TOKENS]
+                first = VECTOR_COLUMNS
+                for end in ends:
+                    nc.scalar.copy(pairs[:, u, first:end, k], windows[j][:, first:end])
+                    first = end
 
         y_bf = [sb("y_bf%d" % c, [P, CHUNK * LANES], BF16) for c in range(CHUNKS)]
         y_codes = sb("y_codes", [P, TOKENS], U32)
@@ -349,7 +352,7 @@ def tile_attend_grouter_x_pl_kernel(tc, xT, W, dg, lb, ce, tx, offs, out_0, out_
             copy_words = nc.scalar.copy if c >= VECTOR_MERGES else nc.vector.tensor_copy
             for piece in pieces(c):
                 copy_words(y_bf[c][:].bitcast(F32).rearrange("p (x u) -> p x u", u=2)[:, piece, :],
-                           pairs(c).rearrange("p u x k -> p u (x k)").bitcast(F32)
+                           pairs[:, :, chunk(c), :].rearrange("p u x k -> p u (x k)").bitcast(F32)
                            .rearrange("p u x -> p x u")[:, piece, :])
 
         def quantise_y(c):

@@ -28,13 +28,14 @@ LIST_ROWS = 16
 CHUNK = 512
 CHUNKS = TOKENS // CHUNK
 SCALAR_PLANE = 1
-GPSIMD_COLUMNS = 1792
-VECTOR_COLUMNS = 256
+GPSIMD_COLUMNS = 1408
+VECTOR_COLUMNS = 512
 VECTOR_MERGES = 3
 X_ORDER = (2, 0, 1, 3)
 DIRECT = 1
 VECTOR_H = 2
 QUADRANTS = 4
+SCALE_ROWS = 4
 
 FLOPS = 2 * 2 * D * E * SLOTS
 BYTES = (4 * (D * TOKENS + D * E + SLOTS * E + 2 * E + TOKENS) + 2 * P * SLOTS // LIST_ROWS
@@ -158,16 +159,15 @@ def tile_attend_grouter_x_pl_kernel(tc, xT, W, dg, lb, ce, tx, offs, out_0, out_
         expert_halves = [slice(0, E // 2), slice(E // 2, E)]
         direct_sums = [banks[0][:, expert_halves[0]], banks[4][:, expert_halves[1]]]
 
-        def scores(first, width, first_bank):
-            cols = slice(first, first + width)
-            sums = [banks[6 if first_bank == 1 and t >= 2 else first_bank][:, block(t)] for t in range(LANES)]
+        def scores(n):
+            sums = [banks[6 if n == DIRECT and t >= 2 else n][:, block(t)] for t in range(LANES)]
             for t in range(LANES):
                 nc.tensor.matmul_mx(out=sums[t], lhsT=w_d_codes[:, block(t)].bitcast(E4M3X4),
                                     lhsT_scale=w_d_scales[:, block(t)],
-                                    rhs=x_codes[:, cols].bitcast(E4M3X4), rhs_scale=x_scales[:, cols],
+                                    rhs=x_codes[:, block(n)].bitcast(E4M3X4), rhs_scale=x_scales[:, block(n)],
                                     start=True, stop=True)
             for t in range(LANES):
-                nc.scalar.activation(scaled_t[first // HALF][:, t, first % HALF:first % HALF + width], sums[t],
+                nc.scalar.activation(scaled_t[n // 2][:, t, block(n % 2)], sums[t],
                                      ACT.Copy, scale=ce_col[:, t:t + 1])
 
         for t in range(LANES):
@@ -180,7 +180,7 @@ def tile_attend_grouter_x_pl_kernel(tc, xT, W, dg, lb, ce, tx, offs, out_0, out_
                                 rhs=w_d_codes[:, expert_halves[k]].bitcast(E4M3X4),
                                 rhs_scale=w_d_scales[:, expert_halves[k]], start=True, stop=True)
         for n in range(DIRECT, SLOT_TILES):
-            scores(n * P, P, n)
+            scores(n)
 
         w_e_codes = sb("w_e_codes", [P, D], U32)
         w_e_scales = sb("w_e_scales", [P, D], U8)
@@ -202,7 +202,6 @@ def tile_attend_grouter_x_pl_kernel(tc, xT, W, dg, lb, ce, tx, offs, out_0, out_
             else:
                 nc.gpsimd.tensor_tensor(dealt(h_tiles[n]), natural(dg_raw[n // 2][:, n % 2, :]),
                                         dealt(lb_rows[:]), ALU.add)
-
 
         def per_tile(name, width):
             return [sb("%s%d" % (name, n), [P, width], F32) for n in range(SLOT_TILES)]
@@ -291,36 +290,32 @@ def tile_attend_grouter_x_pl_kernel(tc, xT, W, dg, lb, ce, tx, offs, out_0, out_
             else:
                 nc.vector.tensor_copy(window, values)
 
-        dx_first = [sb("dx_first%d" % j, [P, HALF], F32, tag=tag) for j, tag in enumerate(("scale_t", "q3"))]
-        dx_pass(1, banks[7], halves[0])
-        nc.scalar.copy(dx_first[1][:], banks[7][:, halves[0]])
-        scatter(1, 0, dx_first[1][:])
-        dx_pass(0, banks[6], halves[0])
-        nc.vector.tensor_copy(dx_first[0][:], banks[6][:, halves[0]])
+        dx_first = [sb("dx_first%d" % j, [P, HALF], F32, tag=tag) for j, tag in enumerate(("x_bf", "q3", "scale_t"))]
+        for j in range(2):
+            dx_pass(j, banks[6 + j], halves[0])
+            nc.scalar.copy(dx_first[j][:], banks[6 + j][:, halves[0]])
+            scatter(j, 0, dx_first[j][:])
+        dx_pass(2, banks[5], halves[0])
+        nc.vector.tensor_copy(dx_first[2][:], banks[5][:, halves[0]])
         quantise_g(3 * P, P)
-        scatter(0, 0, dx_first[0][:])
+        scatter(2, 0, dx_first[2][:])
+        clear_window(3, "g_bf1")
 
-        dx_second = [sb("dx_second%d" % j, [P, HALF], F32) for j in range(2)]
+        dx_second = [sb("dx_second%d" % j, [P, HALF], F32) for j in range(3)]
         spare = SLOTS - VECTOR_COLUMNS
         pairs = sb("pairs", [P, 2, TOKENS + spare, 2], BF16)
-        dx_whole = {2: sb("dx_whole2", [P, SLOTS], F32)[:],
-                    3: pairs[:].rearrange("p u x k -> p (u x k)").bitcast(F32)[:, TOKENS:TOKENS + SLOTS]}
+        dx_last = pairs[:].rearrange("p u x k -> p (u x k)").bitcast(F32)[:, TOKENS:TOKENS + SLOTS]
         out_rows = out_0.rearrange("(p j) x -> j p x", j=LANES)
-        dx_pass(0, banks[4], halves[1])
-        nc.scalar.copy(dx_second[0][:], banks[4][:, halves[1]])
-        dx_pass(2, banks[0], slice(0, SLOTS))
-        nc.scalar.copy(dx_whole[2], banks[0][:])
-        dx_pass(1, banks[1], halves[1])
-        nc.scalar.copy(dx_second[1][:], banks[1][:, halves[1]])
-        for j in (0, 1):
+        for j, bank in ((0, banks[4]), (2, banks[0]), (1, banks[1])):
+            dx_pass(j, bank, halves[1])
+            nc.scalar.copy(dx_second[j][:], bank[:, halves[1]])
+        for j in range(3):
             scatter(j, 1, dx_second[j][:])
             nc.sync.dma_start(out_rows[j], windows[j][:])
         dx_pass(3, banks[2], slice(0, SLOTS))
-        nc.scalar.copy(dx_whole[3], banks[2][:])
-        clear_window(3, "g_scales")
-        for j in (2, 3):
-            nc.vector.tensor_copy(windows[j][:].indirect(offsets[:]), dx_whole[j])
-            nc.sync.dma_start(out_rows[j], windows[j][:])
+        nc.scalar.copy(dx_last, banks[2][:])
+        nc.vector.tensor_copy(windows[3][:].indirect(offsets[:]), dx_last)
+        nc.sync.dma_start(out_rows[3], windows[3][:])
 
         def chunk(c):
             return slice(c * CHUNK, (c + 1) * CHUNK)
@@ -333,7 +328,7 @@ def tile_attend_grouter_x_pl_kernel(tc, xT, W, dg, lb, ce, tx, offs, out_0, out_
                 nc.scalar.copy(pairs[:, u, back, k], windows[j][:, back])
             else:
                 nc.vector.tensor_copy(pairs[:, u, 0:VECTOR_COLUMNS, k], windows[j][:, 0:VECTOR_COLUMNS])
-                ends = range(CHUNK, TOKENS + 1, CHUNK) if j == LANES - 1 else [TOKENS]
+                ends = range(2 * CHUNK, TOKENS + 1, CHUNK) if j == LANES - 1 else [TOKENS]
                 first = VECTOR_COLUMNS
                 for end in ends:
                     nc.scalar.copy(pairs[:, u, first:end, k], windows[j][:, first:end])
@@ -356,7 +351,7 @@ def tile_attend_grouter_x_pl_kernel(tc, xT, W, dg, lb, ce, tx, offs, out_0, out_
                            .rearrange("p u x -> p x u")[:, piece, :])
 
         def quantise_y(c):
-            scales = y_scales[4 * (c // 2):P, chunk(c % 2)]
+            scales = y_scales[SCALE_ROWS * (c // 2):P, chunk(c % 2)]
             for piece in pieces(c):
                 nc.vector.quantize_mx(out=y_codes[:, chunk(c)][:, piece].bitcast(E4M3X4), scales=scales[:, piece],
                                       in_=y_bf[c][:, LANES * piece.start:LANES * piece.stop])
@@ -372,5 +367,7 @@ def tile_attend_grouter_x_pl_kernel(tc, xT, W, dg, lb, ce, tx, offs, out_0, out_
             quantise_y(c)
         for quad in range(QUADRANTS):
             queue = nc.sync if quad % 2 == 0 else nc.scalar
-            queue.dma_start(out_2[0, 4 * quad:4 * quad + 4, :].bitcast(I32).rearrange("f (k x) -> k f x", k=2),
-                            y_scales[32 * quad:32 * quad + 8, :].bitcast(I32))
+            rows = out_2[0, SCALE_ROWS * quad:SCALE_ROWS * (quad + 1), :]
+            first = quad * P // QUADRANTS
+            queue.dma_start(rows.bitcast(I32).rearrange("f (k x) -> k f x", k=2),
+                            y_scales[first:first + 2 * SCALE_ROWS, :].bitcast(I32))

@@ -86,10 +86,9 @@ def tile_attend_grouter_x_pl_kernel(tc, xT, W, dg, lb, ce, tx, offs, out_0, out_
         x_raw = [sb("x_raw%d" % j, [P, TOKENS], F32) for j in range(LANES)]
         for j in X_ORDER:
             nc.sync.dma_start(x_raw[j][:], x_rows[j])
-        dg_raw = [sb("dg_raw%d" % half, [P, 2, E], F32) for half in range(2)]
-        for half in range(2):
-            nc.sync.dma_start(dg_raw[half][:],
-                              dg[half * HALF:(half + 1) * HALF, :].rearrange("(n p) e -> p n e", p=P))
+        dg_raw = [sb("dg_raw%d" % n, [P, E], F32) for n in range(SLOT_TILES)]
+        for n in (0, 2, 3, 1):
+            nc.sync.dma_start(dg_raw[n][:], dg[block(n), :])
 
         w_bf = sb("w_bf", [P, E, LANES], BF16)
         w_dealt = w_bf[:].rearrange("p (t b r) j -> p t b r j", t=LANES, r=RUN)
@@ -125,14 +124,16 @@ def tile_attend_grouter_x_pl_kernel(tc, xT, W, dg, lb, ce, tx, offs, out_0, out_
         for t in range(LANES):
             nc.gpsimd.tensor_scalar(scale_t[:, t, :], neg_tx_rows[:], ce_col[:, t:t + 1], -1.0, ALU.mult, ALU.mult)
 
-        x_bf = sb("x_bf", [P, SLOTS, LANES], BF16)
-        nc.vector.tensor_copy(x_bf[:, :, 2], x_raw[2][:].indirect(offsets[:]))
-        x_pair = sb("x_pair", [P, 2, SLOTS], BF16)
-        nc.vector.tensor_copy(x_pair[:, 0, :], x_raw[0][:].indirect(offsets[:]))
-        for half in range(2):
-            cols = slice(half * HALF, (half + 1) * HALF)
-            nc.vector.tensor_copy(x_pair[:, 1, cols], x_raw[1][:].indirect(half_offsets[half]))
-            nc.scalar.copy(x_bf[:, cols, 0:2], x_pair[:, :, cols].rearrange("p j i -> p i j"))
+        x_bf = [sb("x_bf%d" % half, [P, HALF, LANES], BF16) for half in range(2)]
+        x_lane2 = sb("x_lane2", [P, HALF], BF16)
+        nc.vector.tensor_copy(x_lane2[:], x_raw[2][:].indirect(half_offsets[1]))
+        nc.vector.tensor_copy(x_bf[0][:, :, 2], x_raw[2][:].indirect(half_offsets[0]))
+        nc.scalar.copy(x_bf[1][:, :, 2], x_lane2[:])
+        x_pair = sb("x_pair", [P, 2, HALF], BF16)
+        for j in range(2):
+            nc.vector.tensor_copy(x_pair[:, j, :], x_raw[j][:].indirect(half_offsets[0]))
+            nc.vector.tensor_copy(x_bf[1][:, :, j], x_raw[j][:].indirect(half_offsets[1]))
+        nc.scalar.copy(x_bf[0][:, :, 0:2], x_pair[:].rearrange("p j i -> p i j"))
 
         w_words = w_bf[:].rearrange("p e j -> p (e j)").bitcast(F32)
         wt_bf = sb("wt_bf", [P, D, LANES], BF16)
@@ -150,12 +151,13 @@ def tile_attend_grouter_x_pl_kernel(tc, xT, W, dg, lb, ce, tx, offs, out_0, out_
         x_codes = sb("x_codes", [P, SLOTS], U32)
         x_scales = sb("x_scales", [P, SLOTS], U8)
         scaled_t = [sb("scaled_t%d" % half, [P, LANES, HALF], F32) for half in range(2)]
-        for half in range(2):
-            cols = slice(half * HALF, (half + 1) * HALF)
-            nc.vector.tensor_copy(x_bf[:, cols, LANES - 1], x_raw[LANES - 1][:].indirect(half_offsets[half]))
-            for part in ([block(0), block(1)], [cols])[half]:
-                nc.vector.quantize_mx(out=x_codes[:, part].bitcast(E4M3X4), scales=x_scales[:, part],
-                                      in_=x_bf[:, part, :].rearrange("p i j -> p (i j)"))
+        nc.vector.tensor_copy(x_bf[0][:, :, 3], x_raw[3][:].indirect(half_offsets[0]))
+        nc.scalar.activation(x_bf[1][:, :, 3], x_raw[3][:].indirect(half_offsets[1]), ACT.Copy)
+        for first, width in ((0, P), (P, P), (HALF, HALF)):
+            part = slice(first, first + width)
+            nc.vector.quantize_mx(out=x_codes[:, part].bitcast(E4M3X4), scales=x_scales[:, part],
+                                  in_=x_bf[first // HALF][:, first % HALF:first % HALF + width, :]
+                                  .rearrange("p i j -> p (i j)"))
         expert_halves = [slice(0, E // 2), slice(E // 2, E)]
         direct_sums = [banks[0][:, expert_halves[0]], banks[4][:, expert_halves[1]]]
 
@@ -188,7 +190,7 @@ def tile_attend_grouter_x_pl_kernel(tc, xT, W, dg, lb, ce, tx, offs, out_0, out_
                               in_=wt_bf[:].rearrange("p d t -> p (d t)"))
         clear_window(0, "wt_bf")
 
-        h_late = sb("h_late", [P, 2, E], F32, tag="x_bf")
+        h_late = sb("h_late", [P, 2, E], F32, tag="x_bf1")
         h_tiles = [sb("h0", [P, E], F32)[:], sb("h1", [P, E], F32, tag="ce_rows")[:], h_late[:, 0, :], h_late[:, 1, :]]
         for t in range(LANES):
             nc.tensor.transpose(banks[7][:, block(t)], lb_col[:, t:t + 1].to_broadcast([P, P]), ident[:])
@@ -197,10 +199,10 @@ def tile_attend_grouter_x_pl_kernel(tc, xT, W, dg, lb, ce, tx, offs, out_0, out_
 
         def add_h(n):
             if n < VECTOR_H:
-                nc.vector.tensor_tensor(dealt(h_tiles[n]), natural(dg_raw[n // 2][:, n % 2, :]),
+                nc.vector.tensor_tensor(dealt(h_tiles[n]), natural(dg_raw[n][:]),
                                         dealt(banks[7][:]), ALU.add)
             else:
-                nc.gpsimd.tensor_tensor(dealt(h_tiles[n]), natural(dg_raw[n // 2][:, n % 2, :]),
+                nc.gpsimd.tensor_tensor(dealt(h_tiles[n]), natural(dg_raw[n][:]),
                                         dealt(lb_rows[:]), ALU.add)
 
         def per_tile(name, width):
@@ -266,7 +268,7 @@ def tile_attend_grouter_x_pl_kernel(tc, xT, W, dg, lb, ce, tx, offs, out_0, out_
         terms(1)
         turn(0)
         softmax(3)
-        clear_window(2, "dg_raw1")
+        clear_window(2, "dg_raw3")
         terms(2)
         turn(1)
         quantise_g(0, HALF)
@@ -290,7 +292,7 @@ def tile_attend_grouter_x_pl_kernel(tc, xT, W, dg, lb, ce, tx, offs, out_0, out_
             else:
                 nc.vector.tensor_copy(window, values)
 
-        dx_first = [sb("dx_first%d" % j, [P, HALF], F32, tag=tag) for j, tag in enumerate(("x_bf", "q3", "scale_t"))]
+        dx_first = [sb("dx_first%d" % j, [P, HALF], F32, tag=tag) for j, tag in enumerate(("x_bf1", "q3", "scale_t"))]
         for j in range(2):
             dx_pass(j, banks[6 + j], halves[0])
             nc.scalar.copy(dx_first[j][:], banks[6 + j][:, halves[0]])

@@ -32,6 +32,8 @@ GPSIMD_COLUMNS = 1408
 VECTOR_COLUMNS = 512
 VECTOR_MERGES = 3
 X_ORDER = (2, 0, 1, 3)
+BLOCKS = E // (LANES * RUN)
+VECTOR_BLOCKS = 12
 DIRECT = 1
 VECTOR_H = 2
 QUADRANTS = 4
@@ -93,8 +95,8 @@ def tile_attend_grouter_x_pl_kernel(tc, xT, W, dg, lb, ce, tx, offs, out_0, out_
         w_bf = sb("w_bf", [P, E, LANES], BF16)
         w_dealt = w_bf[:].rearrange("p (t b r) j -> p t b r j", t=LANES, r=RUN)
         w_natural = w_raw[:].rearrange("p j (b t r) -> p t b r j", t=LANES, r=RUN)
-        nc.vector.tensor_copy(w_dealt[:, 0:2], w_natural[:, 0:2])
-        nc.scalar.copy(w_dealt[:, 2:LANES], w_natural[:, 2:LANES])
+        nc.vector.tensor_copy(w_dealt[:, :, 0:VECTOR_BLOCKS], w_natural[:, :, 0:VECTOR_BLOCKS])
+        nc.scalar.copy(w_dealt[:, :, VECTOR_BLOCKS:BLOCKS], w_natural[:, :, VECTOR_BLOCKS:BLOCKS])
 
         expert_dealt = sb("expert_dealt", [P, E], F32)
         nc.vector.tensor_copy(dealt(expert_dealt[:]), natural(expert_rows[:]))
@@ -188,7 +190,6 @@ def tile_attend_grouter_x_pl_kernel(tc, xT, W, dg, lb, ce, tx, offs, out_0, out_
         w_e_scales = sb("w_e_scales", [P, D], U8)
         nc.vector.quantize_mx(out=w_e_codes[:].bitcast(E4M3X4), scales=w_e_scales[:],
                               in_=wt_bf[:].rearrange("p d t -> p (d t)"))
-        clear_window(0, "wt_bf")
 
         h_late = sb("h_late", [P, 2, E], F32, tag="x_bf1")
         h_tiles = [sb("h0", [P, E], F32)[:], sb("h1", [P, E], F32, tag="ce_rows")[:], h_late[:, 0, :], h_late[:, 1, :]]
@@ -268,7 +269,8 @@ def tile_attend_grouter_x_pl_kernel(tc, xT, W, dg, lb, ce, tx, offs, out_0, out_
         terms(1)
         turn(0)
         softmax(3)
-        clear_window(2, "dg_raw3")
+        for j, tag in ((0, "dg_raw3"), (2, "lb_rows")):
+            clear_window(j, tag)
         terms(2)
         turn(1)
         quantise_g(0, HALF)
@@ -279,8 +281,8 @@ def tile_attend_grouter_x_pl_kernel(tc, xT, W, dg, lb, ce, tx, offs, out_0, out_
 
         halves = [slice(0, HALF), slice(HALF, SLOTS)]
 
-        def dx_pass(j, bank, cols):
-            nc.tensor.matmul_mx(out=bank[:, cols], lhsT=w_e_codes[:, block(j)].bitcast(E4M3X4),
+        def dx_pass(j, sums, cols):
+            nc.tensor.matmul_mx(out=sums, lhsT=w_e_codes[:, block(j)].bitcast(E4M3X4),
                                 lhsT_scale=w_e_scales[:, block(j)],
                                 rhs=g_codes[:, cols].bitcast(E5M2X4), rhs_scale=g_scales[:, cols],
                                 start=True, stop=True)
@@ -292,15 +294,18 @@ def tile_attend_grouter_x_pl_kernel(tc, xT, W, dg, lb, ce, tx, offs, out_0, out_
             else:
                 nc.vector.tensor_copy(window, values)
 
-        dx_first = [sb("dx_first%d" % j, [P, HALF], F32, tag=tag) for j, tag in enumerate(("x_bf1", "q3", "scale_t"))]
-        for j in range(2):
-            dx_pass(j, banks[6 + j], halves[0])
-            nc.scalar.copy(dx_first[j][:], banks[6 + j][:, halves[0]])
-            scatter(j, 0, dx_first[j][:])
-        dx_pass(2, banks[5], halves[0])
-        nc.vector.tensor_copy(dx_first[2][:], banks[5][:, halves[0]])
         quantise_g(3 * P, P)
-        scatter(2, 0, dx_first[2][:])
+
+        dx_even = sb("dx_even", [P, 2, HALF], F32, tag="x_bf1")
+        dx_odd = sb("dx_odd", [P, HALF], F32, tag="q3")
+        for k in range(2):
+            dx_pass(2 * k, banks[6][:, halves[k]], halves[0])
+        nc.scalar.copy(dx_even[:].rearrange("p k i -> p (k i)"), banks[6][:])
+        dx_pass(1, banks[7][:, halves[0]], halves[0])
+        nc.scalar.copy(dx_odd[:], banks[7][:, halves[0]])
+        scatter(1, 0, dx_odd[:])
+        for k in range(2):
+            scatter(2 * k, 0, dx_even[:, k, :])
         clear_window(3, "g_bf1")
 
         dx_second = [sb("dx_second%d" % j, [P, HALF], F32) for j in range(3)]
@@ -309,12 +314,12 @@ def tile_attend_grouter_x_pl_kernel(tc, xT, W, dg, lb, ce, tx, offs, out_0, out_
         dx_last = pairs[:].rearrange("p u x k -> p (u x k)").bitcast(F32)[:, TOKENS:TOKENS + SLOTS]
         out_rows = out_0.rearrange("(p j) x -> j p x", j=LANES)
         for j, bank in ((0, banks[4]), (2, banks[0]), (1, banks[1])):
-            dx_pass(j, bank, halves[1])
+            dx_pass(j, bank[:, halves[1]], halves[1])
             nc.scalar.copy(dx_second[j][:], bank[:, halves[1]])
         for j in range(3):
             scatter(j, 1, dx_second[j][:])
             nc.sync.dma_start(out_rows[j], windows[j][:])
-        dx_pass(3, banks[2], slice(0, SLOTS))
+        dx_pass(3, banks[2][:], slice(0, SLOTS))
         nc.scalar.copy(dx_last, banks[2][:])
         nc.vector.tensor_copy(windows[3][:].indirect(offsets[:]), dx_last)
         nc.sync.dma_start(out_rows[3], windows[3][:])
@@ -352,21 +357,25 @@ def tile_attend_grouter_x_pl_kernel(tc, xT, W, dg, lb, ce, tx, offs, out_0, out_
                            pairs[:, :, chunk(c), :].rearrange("p u x k -> p u (x k)").bitcast(F32)
                            .rearrange("p u x -> p x u")[:, piece, :])
 
+        store_from = {2 * CHUNK: 0, TOKENS - CHUNK // 2: 2 * CHUNK, TOKENS: TOKENS - CHUNK // 2}
+
         def quantise_y(c):
             scales = y_scales[SCALE_ROWS * (c // 2):P, chunk(c % 2)]
             for piece in pieces(c):
                 nc.vector.quantize_mx(out=y_codes[:, chunk(c)][:, piece].bitcast(E4M3X4), scales=scales[:, piece],
                                       in_=y_bf[c][:, LANES * piece.start:LANES * piece.stop])
-            if c > 0:
-                cols = slice(0, 2 * CHUNK) if c == 1 else chunk(c)
-                nc.sync.dma_start(words_out[:, cols], y_codes[:, cols].bitcast(I32))
+                end = c * CHUNK + piece.stop
+                if end in store_from:
+                    cols = slice(store_from[end], end)
+                    nc.sync.dma_start(words_out[:, cols], y_codes[:, cols].bitcast(I32))
 
         for j in range(LANES):
             round_plane(j)
-        for c in range(CHUNKS):
+        merge(0)
+        for c in range(1, CHUNKS):
             merge(c)
-        for c in range(CHUNKS):
-            quantise_y(c)
+            quantise_y(c - 1)
+        quantise_y(CHUNKS - 1)
         for quad in range(QUADRANTS):
             queue = nc.sync if quad % 2 == 0 else nc.scalar
             rows = out_2[0, SCALE_ROWS * quad:SCALE_ROWS * (quad + 1), :]

@@ -126,6 +126,20 @@ def tile_attend_grouter_x_pl_kernel(tc, xT, W, dg, lb, ce, tx, offs, out_0, out_
         for t in range(LANES):
             nc.gpsimd.tensor_scalar(scale_t[:, t, :], neg_tx_rows[:], ce_col[:, t:t + 1], -1.0, ALU.mult, ALU.mult)
 
+        w_words = w_bf[:].rearrange("p e j -> p (e j)").bitcast(F32)
+        wt_bf = sb("wt_bf", [P, D, LANES], BF16)
+        for u in range(2):
+            for t in range(LANES):
+                nc.tensor.transpose(banks[5 + u][:, block(t)], w_words[:, 2 * P * t + u:2 * P * (t + 1):2], ident[:])
+            nc.scalar.copy(wt_bf[:, 2 * P * u:2 * P * (u + 1), :].rearrange("p (k v w) t -> p v t w k", k=2, w=2),
+                           banks[5 + u][:].bitcast(BF16).rearrange("p (t v w k) -> p v t w k", t=LANES, w=2, k=2))
+
+        w_e_codes = sb("w_e_codes", [P, D], U32)
+        w_e_scales = sb("w_e_scales", [P, D], U8)
+        nc.vector.quantize_mx(out=w_e_codes[:].bitcast(E4M3X4), scales=w_e_scales[:],
+                              in_=wt_bf[:].rearrange("p d t -> p (d t)"))
+        clear_window(0, "wt_bf")
+
         x_bf = [sb("x_bf%d" % half, [P, HALF, LANES], BF16) for half in range(2)]
         x_lane2 = sb("x_lane2", [P, HALF], BF16)
         nc.vector.tensor_copy(x_lane2[:], x_raw[2][:].indirect(half_offsets[1]))
@@ -136,14 +150,6 @@ def tile_attend_grouter_x_pl_kernel(tc, xT, W, dg, lb, ce, tx, offs, out_0, out_
             nc.vector.tensor_copy(x_pair[:, j, :], x_raw[j][:].indirect(half_offsets[0]))
             nc.vector.tensor_copy(x_bf[1][:, :, j], x_raw[j][:].indirect(half_offsets[1]))
         nc.scalar.copy(x_bf[0][:, :, 0:2], x_pair[:].rearrange("p j i -> p i j"))
-
-        w_words = w_bf[:].rearrange("p e j -> p (e j)").bitcast(F32)
-        wt_bf = sb("wt_bf", [P, D, LANES], BF16)
-        for u in range(2):
-            for t in range(LANES):
-                nc.tensor.transpose(banks[5 + u][:, block(t)], w_words[:, 2 * P * t + u:2 * P * (t + 1):2], ident[:])
-            nc.scalar.copy(wt_bf[:, 2 * P * u:2 * P * (u + 1), :].rearrange("p (k v w) t -> p v t w k", k=2, w=2),
-                           banks[5 + u][:].bitcast(BF16).rearrange("p (t v w k) -> p v t w k", t=LANES, w=2, k=2))
 
         w_d_codes = sb("w_d_codes", [P, E], U32)
         w_d_scales = sb("w_d_scales", [P, E], U8)
@@ -185,11 +191,6 @@ def tile_attend_grouter_x_pl_kernel(tc, xT, W, dg, lb, ce, tx, offs, out_0, out_
                                 rhs_scale=w_d_scales[:, expert_halves[k]], start=True, stop=True)
         for n in range(DIRECT, SLOT_TILES):
             scores(n)
-
-        w_e_codes = sb("w_e_codes", [P, D], U32)
-        w_e_scales = sb("w_e_scales", [P, D], U8)
-        nc.vector.quantize_mx(out=w_e_codes[:].bitcast(E4M3X4), scales=w_e_scales[:],
-                              in_=wt_bf[:].rearrange("p d t -> p (d t)"))
 
         h_late = sb("h_late", [P, 2, E], F32, tag="x_bf1")
         h_tiles = [sb("h0", [P, E], F32)[:], sb("h1", [P, E], F32, tag="ce_rows")[:], h_late[:, 0, :], h_late[:, 1, :]]
@@ -269,8 +270,7 @@ def tile_attend_grouter_x_pl_kernel(tc, xT, W, dg, lb, ce, tx, offs, out_0, out_
         terms(1)
         turn(0)
         softmax(3)
-        for j, tag in ((0, "dg_raw3"), (2, "lb_rows")):
-            clear_window(j, tag)
+        clear_window(2, "dg_raw3")
         terms(2)
         turn(1)
         quantise_g(0, HALF)
@@ -296,16 +296,16 @@ def tile_attend_grouter_x_pl_kernel(tc, xT, W, dg, lb, ce, tx, offs, out_0, out_
 
         quantise_g(3 * P, P)
 
-        dx_even = sb("dx_even", [P, 2, HALF], F32, tag="x_bf1")
-        dx_odd = sb("dx_odd", [P, HALF], F32, tag="q3")
+        dx_lead = sb("dx_lead", [P, HALF], F32, tag="x_bf1")
+        dx_next = sb("dx_next", [P, 2, HALF], F32, tag="q3")
+        dx_pass(0, banks[6][:, halves[0]], halves[0])
+        nc.scalar.copy(dx_lead[:], banks[6][:, halves[0]])
         for k in range(2):
-            dx_pass(2 * k, banks[6][:, halves[k]], halves[0])
-        nc.scalar.copy(dx_even[:].rearrange("p k i -> p (k i)"), banks[6][:])
-        dx_pass(1, banks[7][:, halves[0]], halves[0])
-        nc.scalar.copy(dx_odd[:], banks[7][:, halves[0]])
-        scatter(1, 0, dx_odd[:])
-        for k in range(2):
-            scatter(2 * k, 0, dx_even[:, k, :])
+            dx_pass(1 + k, banks[7][:, halves[k]], halves[0])
+        nc.scalar.copy(dx_next[:].rearrange("p k i -> p (k i)"), banks[7][:])
+        scatter(1, 0, dx_next[:, 0, :])
+        scatter(0, 0, dx_lead[:])
+        scatter(2, 0, dx_next[:, 1, :])
         clear_window(3, "g_bf1")
 
         dx_second = [sb("dx_second%d" % j, [P, HALF], F32) for j in range(3)]

from contextlib import ExitStack

import concourse.mybir as mybir
from concourse.masks import make_identity

F32 = mybir.dt.float32
BF16 = mybir.dt.bfloat16
I32 = mybir.dt.int32
U32 = mybir.dt.uint32
U16 = mybir.dt.uint16
U8 = mybir.dt.uint8
E4M3X4 = mybir.dt.float8_e4m3fn_x4
E5M2X4 = mybir.dt.float8_e5m2_x4
ALU = mybir.AluOpType
ACT = mybir.ActivationFunctionType

P = 128
LANES = 4
RUN = 8
BANK = 512
D = 512
E = 512
SLOTS = 512
TOKENS = 2048
HALF = SLOTS // 2
SLOT_TILES = SLOTS // P
LIST_ROWS = 16
CHUNK = 512
CHUNKS = TOKENS // CHUNK
SCALAR_PLANE = 1
GPSIMD_COLUMNS = 1408
VECTOR_COLUMNS = 512
VECTOR_MERGES = 3
X_ORDER = (2, 0, 1, 3)
BLOCKS = E // (LANES * RUN)
VECTOR_BLOCKS = 12
DIRECT = 1
VECTOR_H = 2
QUADRANTS = 4
SCALE_ROWS = 4

FLOPS = 2 * 2 * D * E * SLOTS
BYTES = (4 * (D * TOKENS + D * E + SLOTS * E + 2 * E + TOKENS) + 2 * P * SLOTS // LIST_ROWS
         + 4 * D * TOKENS + D * TOKENS + 16 * TOKENS)


def tile_attend_grouter_x_pl_kernel(tc, xT, W, dg, lb, ce, tx, offs, out_0, out_1, out_2):
    nc = tc.nc
    with ExitStack() as ctx:
        keep = ctx.enter_context(tc.tile_pool(name="keep", bufs=1))
        psum = ctx.enter_context(tc.psum_pool(name="psum", bufs=1))

        def sb(name, shape, dtype, tag=""):
            return keep.tile(shape, dtype, name=name, tag=tag or name, align_bytes=64)

        def block(number):
            return slice(number * P, (number + 1) * P)

        def dealt(ap):
            return ap.rearrange("p (t b r) -> p t b r", t=LANES, r=RUN)

        def natural(ap):
            return ap.rearrange("p (b t r) -> p t b r", t=LANES, r=RUN)

        banks = [psum.tile([P, BANK], F32, name="bank%d" % b) for b in range(8)]

        offsets = sb("offsets", [P, SLOTS // LIST_ROWS], U16)
        nc.sync.dma_start(offsets[:], offs)
        half_columns = HALF // LIST_ROWS
        half_offsets = [offsets[:, 0:half_columns], offsets[:, half_columns:2 * half_columns]]

        ident = sb("ident", [P, P], F32)
        make_identity(nc, ident[:])
        neg_tx_col = sb("neg_tx_col", [P, SLOT_TILES], F32)
        ones = sb("ones", [P, 1], F32)
        nc.scalar.activation(ones[:], ident[:, 0:1], ACT.Exp, scale=0.0)

        expert_rows = sb("expert_rows", [P, E], F32)
        tx_window = sb("tx_window", [P, TOKENS], F32)
        nc.vector.memset(expert_rows[0:P - 2, :], 0.0)
        nc.vector.memset(tx_window[0:P - 1, :].bitcast(I32), 0)
        nc.sync.dma_start(expert_rows[P - 1:P, :], ce[0:1, :])
        nc.sync.dma_start(expert_rows[P - 2:P - 1, :], lb[0:1, :])
        nc.sync.dma_start(tx_window[P - 1:P, :], tx[0:1, :])
        w_raw = sb("w_raw", [P, LANES, E], F32)
        nc.sync.dma_start(w_raw[:], W.rearrange("(p j) e -> p j e", j=LANES))
        x_rows = xT.rearrange("(p j) x -> j p x", j=LANES)
        x_raw = [sb("x_raw%d" % j, [P, TOKENS], F32) for j in range(LANES)]
        for j in X_ORDER:
            nc.sync.dma_start(x_raw[j][:], x_rows[j])
        dg_raw = [sb("dg_raw%d" % n, [P, E], F32) for n in range(SLOT_TILES)]
        for n in (0, 2, 3, 1):
            nc.sync.dma_start(dg_raw[n][:], dg[block(n), :])

        w_bf = sb("w_bf", [P, E, LANES], BF16)
        w_dealt = w_bf[:].rearrange("p (t b r) j -> p t b r j", t=LANES, r=RUN)
        w_natural = w_raw[:].rearrange("p j (b t r) -> p t b r j", t=LANES, r=RUN)
        nc.vector.tensor_copy(w_dealt[:, :, 0:VECTOR_BLOCKS], w_natural[:, :, 0:VECTOR_BLOCKS])
        nc.scalar.copy(w_dealt[:, :, VECTOR_BLOCKS:BLOCKS], w_natural[:, :, VECTOR_BLOCKS:BLOCKS])

        expert_dealt = sb("expert_dealt", [P, E], F32)
        nc.vector.tensor_copy(dealt(expert_dealt[:]), natural(expert_rows[:]))
        for t in range(LANES):
            nc.tensor.transpose(banks[2][:, block(t)], expert_dealt[:, block(t)], ident[:])
        ce_col = sb("ce_col", [P, LANES], F32)
        nc.scalar.copy(ce_col[:], banks[2][:, P - 1:BANK:P])
        lb_col = sb("lb_col", [P, LANES], F32)
        nc.scalar.copy(lb_col[:], banks[2][:, P - 2:BANK:P])
        tx_listed = sb("tx_listed", [P, SLOTS], F32)
        nc.vector.tensor_copy(tx_listed[:], tx_window[:].indirect(offsets[:]))
        windows = {}

        def clear_window(j, tag):
            windows[j] = sb("window%d" % j, [P, TOKENS], F32, tag=tag)
            nc.gpsimd.memset(windows[j][:].bitcast(I32), 0)

        clear_window(1, "expert_rows")
        for n in range(SLOT_TILES):
            nc.tensor.transpose(banks[3][:, block(n)], tx_listed[:, block(n)], ident[:])
        nc.scalar.activation(neg_tx_col[:], banks[3][:, P - 1:BANK:P], ACT.Copy, scale=-1.0)
        for n in range(SLOT_TILES):
            nc.tensor.transpose(banks[1][:, block(n)], neg_tx_col[:, n:n + 1].to_broadcast([P, P]), ident[:])
        neg_tx_rows = sb("neg_tx_rows", [P, SLOTS], F32)
        nc.scalar.activation(neg_tx_rows[:], banks[1][:], ACT.Copy, scale=ones[:])
        scale_t = sb("scale_t", [P, LANES, SLOTS], F32)
        for t in range(LANES):
            nc.gpsimd.tensor_scalar(scale_t[:, t, :], neg_tx_rows[:], ce_col[:, t:t + 1], -1.0, ALU.mult, ALU.mult)

        w_words = w_bf[:].rearrange("p e j -> p (e j)").bitcast(F32)
        wt_bf = sb("wt_bf", [P, D, LANES], BF16)
        for u in range(2):
            for t in range(LANES):
                nc.tensor.transpose(banks[5 + u][:, block(t)], w_words[:, 2 * P * t + u:2 * P * (t + 1):2], ident[:])
            nc.scalar.copy(wt_bf[:, 2 * P * u:2 * P * (u + 1), :].rearrange("p (k v w) t -> p v t w k", k=2, w=2),
                           banks[5 + u][:].bitcast(BF16).rearrange("p (t v w k) -> p v t w k", t=LANES, w=2, k=2))

        w_e_codes = sb("w_e_codes", [P, D], U32)
        w_e_scales = sb("w_e_scales", [P, D], U8)
        nc.vector.quantize_mx(out=w_e_codes[:].bitcast(E4M3X4), scales=w_e_scales[:],
                              in_=wt_bf[:].rearrange("p d t -> p (d t)"))
        clear_window(0, "wt_bf")

        x_bf = [sb("x_bf%d" % half, [P, HALF, LANES], BF16) for half in range(2)]
        x_lane2 = sb("x_lane2", [P, HALF], BF16)
        nc.vector.tensor_copy(x_lane2[:], x_raw[2][:].indirect(half_offsets[1]))
        nc.vector.tensor_copy(x_bf[0][:, :, 2], x_raw[2][:].indirect(half_offsets[0]))
        nc.scalar.copy(x_bf[1][:, :, 2], x_lane2[:])
        x_pair = sb("x_pair", [P, 2, HALF], BF16)
        for j in range(2):
            nc.vector.tensor_copy(x_pair[:, j, :], x_raw[j][:].indirect(half_offsets[0]))
            nc.vector.tensor_copy(x_bf[1][:, :, j], x_raw[j][:].indirect(half_offsets[1]))
        nc.scalar.copy(x_bf[0][:, :, 0:2], x_pair[:].rearrange("p j i -> p i j"))

        w_d_codes = sb("w_d_codes", [P, E], U32)
        w_d_scales = sb("w_d_scales", [P, E], U8)
        nc.vector.quantize_mx(out=w_d_codes[:].bitcast(E4M3X4), scales=w_d_scales[:],
                              in_=w_bf[:].rearrange("p e j -> p (e j)"))

        x_codes = sb("x_codes", [P, SLOTS], U32)
        x_scales = sb("x_scales", [P, SLOTS], U8)
        scaled_t = [sb("scaled_t%d" % half, [P, LANES, HALF], F32) for half in range(2)]
        nc.vector.tensor_copy(x_bf[0][:, :, 3], x_raw[3][:].indirect(half_offsets[0]))
        nc.scalar.activation(x_bf[1][:, :, 3], x_raw[3][:].indirect(half_offsets[1]), ACT.Copy)
        for first, width in ((0, P), (P, P), (HALF, HALF)):
            part = slice(first, first + width)
            nc.vector.quantize_mx(out=x_codes[:, part].bitcast(E4M3X4), scales=x_scales[:, part],
                                  in_=x_bf[first // HALF][:, first % HALF:first % HALF + width, :]
                                  .rearrange("p i j -> p (i j)"))
        expert_halves = [slice(0, E // 2), slice(E // 2, E)]
        direct_sums = [banks[0][:, expert_halves[0]], banks[4][:, expert_halves[1]]]

        def scores(n):
            sums = [banks[6 if n == DIRECT and t >= 2 else n][:, block(t)] for t in range(LANES)]
            for t in range(LANES):
                nc.tensor.matmul_mx(out=sums[t], lhsT=w_d_codes[:, block(t)].bitcast(E4M3X4),
                                    lhsT_scale=w_d_scales[:, block(t)],
                                    rhs=x_codes[:, block(n)].bitcast(E4M3X4), rhs_scale=x_scales[:, block(n)],
                                    start=True, stop=True)
            for t in range(LANES):
                nc.scalar.activation(scaled_t[n // 2][:, t, block(n % 2)], sums[t],
                                     ACT.Copy, scale=ce_col[:, t:t + 1])

        for t in range(LANES):
            nc.tensor.transpose(banks[0][:, block(t)], ce_col[:, t:t + 1].to_broadcast([P, P]), ident[:])
        ce_rows = sb("ce_rows", [P, E], F32)
        nc.scalar.copy(ce_rows[:], banks[0][:])
        for k in range(2):
            nc.tensor.matmul_mx(out=direct_sums[k], lhsT=x_codes[:, block(0)].bitcast(E4M3X4),
                                lhsT_scale=x_scales[:, block(0)],
                                rhs=w_d_codes[:, expert_halves[k]].bitcast(E4M3X4),
                                rhs_scale=w_d_scales[:, expert_halves[k]], start=True, stop=True)
        for n in range(DIRECT, SLOT_TILES):
            scores(n)

        h_late = sb("h_late", [P, 2, E], F32, tag="x_bf1")
        h_tiles = [sb("h0", [P, E], F32)[:], sb("h1", [P, E], F32, tag="ce_rows")[:], h_late[:, 0, :], h_late[:, 1, :]]
        for t in range(LANES):
            nc.tensor.transpose(banks[7][:, block(t)], lb_col[:, t:t + 1].to_broadcast([P, P]), ident[:])
        lb_rows = sb("lb_rows", [P, E], F32)
        nc.scalar.copy(lb_rows[:], banks[7][:])

        def add_h(n):
            if n < VECTOR_H:
                nc.vector.tensor_tensor(dealt(h_tiles[n]), natural(dg_raw[n][:]),
                                        dealt(banks[7][:]), ALU.add)
            else:
                nc.gpsimd.tensor_tensor(dealt(h_tiles[n]), natural(dg_raw[n][:]),
                                        dealt(lb_rows[:]), ALU.add)

        def per_tile(name, width):
            return [sb("%s%d" % (name, n), [P, width], F32) for n in range(SLOT_TILES)]

        q, term_h, term_s = [per_tile(name, E) for name in ("q", "term_h", "term_s")]
        neg_z = per_tile("neg_z", E)
        neg_m, tot, inv_tot, neg_inv_tot, s_sum, s_factor = [
            per_tile(name, 1) for name in ("neg_m", "tot", "inv_tot", "neg_inv_tot", "s_sum", "s_factor")]
        g_bf = [sb("g_bf%d" % half, [P, HALF, LANES], BF16) for half in range(2)]

        def softmax(n):
            neg_tx = neg_tx_col[:, n:n + 1]
            bank = banks[4 + n]
            if n < DIRECT:
                for k in range(2):
                    nc.vector.scalar_tensor_tensor(neg_z[n][:, expert_halves[k]], direct_sums[k], neg_tx,
                                                   ce_rows[:, expert_halves[k]], ALU.mult, ALU.mult)
                nc.vector.tensor_reduce(neg_m[n][:], neg_z[n][:], mybir.AxisListType.X, ALU.min)
            else:
                add_h(n)
                for t in range(LANES):
                    nc.tensor.transpose(bank[:, block(t)], scaled_t[n // 2][:, t, block(n % 2)], ident[:])
                nc.vector.tensor_scalar(neg_z[n][:], bank[:], neg_tx, None, ALU.mult, ALU.min,
                                        accum_out=neg_m[n][:])
            nc.scalar.activation(q[n][:], neg_z[n][:], ACT.Exp, bias=neg_m[n][:], scale=-1.0, accum_out=tot[n][:])

        def terms(n):
            nc.vector.reciprocal(inv_tot[n][:], tot[n][:])
            nc.vector.scalar_tensor_tensor(term_h[n][:], q[n][:], inv_tot[n][:], h_tiles[n],
                                           ALU.mult, ALU.mult, accum_out=s_sum[n][:])
            nc.vector.tensor_scalar(neg_inv_tot[n][:], inv_tot[n][:], -1.0, None, ALU.mult)
            nc.scalar.activation(s_factor[n][:], s_sum[n][:], ACT.Copy, scale=neg_inv_tot[n][:])
            for cols in expert_halves:
                nc.scalar.activation(term_s[n][:, cols], q[n][:, cols], ACT.Copy, scale=s_factor[n][:])

        def turn(n):
            bank = banks[n]
            for t in range(LANES):
                nc.tensor.matmul(bank[:, block(t)], term_h[n][:, block(t)], ident[:],
                                 start=(t == 0), stop=False, is_transpose=True)
            for t in range(LANES):
                nc.tensor.matmul(bank[:, block(t)], term_s[n][:, block(t)], ident[:],
                                 start=False, stop=(t == LANES - 1), is_transpose=True)
            nc.vector.tensor_tensor(g_bf[n // 2][:, block(n % 2), :].rearrange("p (i w) t -> p i t w", w=2),
                                    bank[:].rearrange("p (t i w) -> p i t w", t=LANES, w=2),
                                    scale_t[:, :, block(n)].rearrange("p t (i w) -> p i t w", w=2), ALU.mult)

        g_codes = sb("g_codes", [P, SLOTS], U32)
        g_scales = sb("g_scales", [P, SLOTS], U8)

        def quantise_g(first, width):
            cols = slice(first, first + width)
            nc.vector.quantize_mx(out=g_codes[:, cols].bitcast(E5M2X4), scales=g_scales[:, cols],
                                  in_=g_bf[first // HALF][:, first % HALF:first % HALF + width, :]
                                  .rearrange("p i t -> p (i t)"))

        add_h(0)
        softmax(0)
        softmax(1)
        terms(0)
        softmax(2)
        terms(1)
        turn(0)
        softmax(3)
        clear_window(2, "dg_raw3")
        terms(2)
        turn(1)
        quantise_g(0, HALF)
        terms(3)
        turn(2)
        turn(3)
        quantise_g(2 * P, P)

        halves = [slice(0, HALF), slice(HALF, SLOTS)]

        def dx_pass(j, sums, cols):
            nc.tensor.matmul_mx(out=sums, lhsT=w_e_codes[:, block(j)].bitcast(E4M3X4),
                                lhsT_scale=w_e_scales[:, block(j)],
                                rhs=g_codes[:, cols].bitcast(E5M2X4), rhs_scale=g_scales[:, cols],
                                start=True, stop=True)

        def scatter(j, half, values):
            window = windows[j][:].indirect(half_offsets[half])
            if j == SCALAR_PLANE:
                nc.scalar.activation(window, values, ACT.Copy)
            else:
                nc.vector.tensor_copy(window, values)

        quantise_g(3 * P, P)

        dx_lead = sb("dx_lead", [P, HALF], F32, tag="x_bf1")
        dx_next = sb("dx_next", [P, 2, HALF], F32, tag="q3")
        dx_pass(0, banks[6][:, halves[0]], halves[0])
        nc.scalar.copy(dx_lead[:], banks[6][:, halves[0]])
        for k in range(2):
            dx_pass(1 + k, banks[7][:, halves[k]], halves[0])
        nc.scalar.copy(dx_next[:].rearrange("p k i -> p (k i)"), banks[7][:])
        scatter(1, 0, dx_next[:, 0, :])
        scatter(0, 0, dx_lead[:])
        scatter(2, 0, dx_next[:, 1, :])
        clear_window(3, "g_bf1")

        dx_second = [sb("dx_second%d" % j, [P, HALF], F32) for j in range(3)]
        spare = SLOTS - VECTOR_COLUMNS
        pairs = sb("pairs", [P, 2, TOKENS + spare, 2], BF16)
        dx_last = pairs[:].rearrange("p u x k -> p (u x k)").bitcast(F32)[:, TOKENS:TOKENS + SLOTS]
        out_rows = out_0.rearrange("(p j) x -> j p x", j=LANES)
        for j, bank in ((0, banks[4]), (2, banks[0]), (1, banks[1])):
            dx_pass(j, bank[:, halves[1]], halves[1])
            nc.scalar.copy(dx_second[j][:], bank[:, halves[1]])
        for j in range(3):
            scatter(j, 1, dx_second[j][:])
            nc.sync.dma_start(out_rows[j], windows[j][:])
        dx_pass(3, banks[2][:], slice(0, SLOTS))
        nc.scalar.copy(dx_last, banks[2][:])
        nc.vector.tensor_copy(windows[3][:].indirect(offsets[:]), dx_last)
        nc.sync.dma_start(out_rows[3], windows[3][:])

        def chunk(c):
            return slice(c * CHUNK, (c + 1) * CHUNK)

        def round_plane(j):
            u, k = divmod(j, 2)
            if u == 0:
                front, back = slice(0, GPSIMD_COLUMNS), slice(GPSIMD_COLUMNS, TOKENS)
                nc.gpsimd.tensor_scalar(pairs[:, u, front, k], windows[j][:, front], 1.0, 0.0, ALU.mult, ALU.add)
                nc.scalar.copy(pairs[:, u, back, k], windows[j][:, back])
            else:
                nc.vector.tensor_copy(pairs[:, u, 0:VECTOR_COLUMNS, k], windows[j][:, 0:VECTOR_COLUMNS])
                ends = range(2 * CHUNK, TOKENS + 1, CHUNK) if j == LANES - 1 else [TOKENS]
                first = VECTOR_COLUMNS
                for end in ends:
                    nc.scalar.copy(pairs[:, u, first:end, k], windows[j][:, first:end])
                    first = end

        y_bf = [sb("y_bf%d" % c, [P, CHUNK * LANES], BF16) for c in range(CHUNKS)]
        y_codes = sb("y_codes", [P, TOKENS], U32)
        y_scales = sb("y_scales", [P, 2 * CHUNK], U8)
        words_out = out_1[0].rearrange("p x j -> p (x j)").bitcast(I32)

        def pieces(c):
            width = CHUNK // 2 if c == CHUNKS - 1 else CHUNK
            return [slice(first, first + width) for first in range(0, CHUNK, width)]

        def merge(c):
            copy_words = nc.scalar.copy if c >= VECTOR_MERGES else nc.vector.tensor_copy
            for piece in pieces(c):
                copy_words(y_bf[c][:].bitcast(F32).rearrange("p (x u) -> p x u", u=2)[:, piece, :],
                           pairs[:, :, chunk(c), :].rearrange("p u x k -> p u (x k)").bitcast(F32)
                           .rearrange("p u x -> p x u")[:, piece, :])

        store_from = {2 * CHUNK: 0, TOKENS - CHUNK // 2: 2 * CHUNK, TOKENS: TOKENS - CHUNK // 2}

        def quantise_y(c):
            scales = y_scales[SCALE_ROWS * (c // 2):P, chunk(c % 2)]
            for piece in pieces(c):
                nc.vector.quantize_mx(out=y_codes[:, chunk(c)][:, piece].bitcast(E4M3X4), scales=scales[:, piece],
                                      in_=y_bf[c][:, LANES * piece.start:LANES * piece.stop])
                end = c * CHUNK + piece.stop
                if end in store_from:
                    cols = slice(store_from[end], end)
                    nc.sync.dma_start(words_out[:, cols], y_codes[:, cols].bitcast(I32))

        for j in range(LANES):
            round_plane(j)
        merge(0)
        for c in range(1, CHUNKS):
            merge(c)
            quantise_y(c - 1)
        quantise_y(CHUNKS - 1)
        for quad in range(QUADRANTS):
            queue = nc.sync if quad % 2 == 0 else nc.scalar
            rows = out_2[0, SCALE_ROWS * quad:SCALE_ROWS * (quad + 1), :]
            first = quad * P // QUADRANTS
            queue.dma_start(rows.bitcast(I32).rearrange("f (k x) -> k f x", k=2),
                            y_scales[first:first + 2 * SCALE_ROWS, :].bitcast(I32))
